import numpy as np
import ml_dtypes


def mxq(x, axis, fmt="e4m3"):
    dtype, down = {"e4m3": (ml_dtypes.float8_e4m3fn, 7), "e5m2": (ml_dtypes.float8_e5m2, 14)}[fmt]
    v = np.moveaxis(np.asarray(x, np.float32).astype(ml_dtypes.bfloat16).astype(np.float64), axis, -1)
    blocks = v.reshape(v.shape[:-1] + (-1, 32))
    amax = np.abs(blocks).max(-1, keepdims=True)
    byte = np.maximum(np.where(amax > 0, np.frexp(amax)[1] - 1 + 127, 0) - down, 1)
    scale = np.exp2(byte - 127.0)
    codes = (blocks / scale).astype(np.float32).astype(dtype).astype(np.float64)
    return np.moveaxis((codes * scale).reshape(v.shape), -1, axis)


WIDE = False


def mx_kscale(k):
    if not WIDE:
        return np.ones(k)
    levels = np.array([10, -10, 5, -5, 0])
    if k % 512:
        return np.exp2(np.random.permutation(np.resize(levels, k // 32))).repeat(32)
    a = np.empty((k // 512, 16))
    for p in range(k // 512):
        a[p, :8] = np.random.permutation(np.resize(levels, 8))
        for g in range(8):
            far = levels[np.abs(levels - a[p, g]) >= 10]
            a[p, g + 8] = far[np.random.randint(len(far))]
    return np.exp2(a.ravel()).repeat(32)


def f64(x):
    return np.asarray(x).astype(np.float64)


def striped(idx):
    return np.tile(np.asarray(idx).reshape(-1, 16).T, (8, 1)).astype(np.uint16)


def unstriped(offs):
    return offs[:16].T.reshape(-1).astype(np.int64)


E2M1 = np.array([0.0, 0.5, 1.0, 1.5, 2.0, 3.0, 4.0, 6.0, -0.0, -0.5, -1.0, -1.5, -2.0, -3.0, -4.0, -6.0])


def pack_weight(w, fmt):
    k, n = w.shape
    w = f64(np.asarray(w, np.float32).astype(ml_dtypes.bfloat16)).reshape(k // 32, 32, n)
    amax = np.abs(w).max(1)
    if fmt == "e4m3":
        byte = np.frexp(amax)[1] - 1 + 127 - 7
    else:
        mant, ex = np.frexp(amax / 6.0)
        byte = np.where(mant > 0.5, ex, ex - 1) + 127
    byte = np.clip(np.where(amax > 0, byte, 1), 1, 254)
    scaled = (w * np.exp2(127.0 - byte)[:, None, :]).reshape(k, n).astype(np.float32)
    by_word = np.ascontiguousarray(scaled.reshape(k // 512, 128, 4, n).transpose(0, 1, 3, 2))
    if fmt == "e4m3":
        words = by_word.astype(ml_dtypes.float8_e4m3fn).view(np.uint8)
    else:
        c = by_word.astype(ml_dtypes.float4_e2m1fn).view(np.uint8) & 0xF
        words = (c[..., 0::2] | (c[..., 1::2] << 4)).reshape(k // 512, 128, 2 * n)
    return np.ascontiguousarray(words), np.ascontiguousarray(byte.astype(np.uint8).reshape(k // 512, 16, n))


def unpack_weight(words, scales, fmt):
    g, _, n = scales.shape
    words = np.ascontiguousarray(words).reshape(g, 128, n, -1)
    if fmt == "e4m3":
        vals = words.view(ml_dtypes.float8_e4m3fn).astype(np.float64)
    else:
        nib = np.empty((g, 128, n, 4), np.uint8)
        nib[..., 0::2] = words & 0xF
        nib[..., 1::2] = words >> 4
        vals = E2M1[nib]
    vals = vals * np.repeat(np.exp2(scales.astype(np.float64) - 127.0), 8, axis=1)[..., None]
    return vals.transpose(0, 1, 3, 2).reshape(g * 512, n)


def sigmoid(v):
    return 1.0 / (1.0 + np.exp(-v))


B, N, T, D, NQ = 1, 512, 2048, 1024, 256


def setup_inputs():
    n = np.random.standard_normal
    idx = np.random.permutation(T)[:B * N]
    s = mx_kscale(D)[:, None]
    kp = pack_weight(n((D, T)) / s, "e2m1")
    return {
        "qT": (n((B, D, NQ)) * s * (1.00 / np.sqrt(D))).astype(np.float32),
        "k_words": np.ascontiguousarray(kp[0].reshape(1, 2, 128, T, 2).transpose(0, 2, 3, 1, 4)).reshape(1, 128, T, 4),
        "k_scales": kp[1],
        "kb": np.tile(n(2048), (128, 1)).astype(np.float32),
        "th": (n((B, NQ, 1))).astype(np.float32),
        "offs": striped(idx),
    }


def reference(qT, k_words, k_scales, kb, th, offs):
    idx = unstriped(offs)
    pick = lambda x, which: x[:, which].reshape(x.shape[0], B, -1).transpose(1, 0, 2)
    k = unpack_weight(k_words.reshape(1, 128, T, 2, 2).transpose(0, 3, 1, 2, 4).reshape(2, 128, 2 * T), k_scales, "e2m1")
    kg = pick(k, idx)
    qq = mxq(f64(qT), 1, "e4m3")
    a = qq.transpose(0, 2, 1) @ kg
    y = sigmoid(a + pick(f64(kb), idx)[:, :1, :] - f64(th))
    out = np.zeros((B, NQ, T))
    for b in range(B):
        out[b][:, idx[b * N:(b + 1) * N]] = y[b]
    return out

@@ -1,0 +1,174 @@
+from contextlib import ExitStack
+
+import concourse.mybir as mybir
+from concourse.masks import make_identity
+
+F32 = mybir.dt.float32
+BF16 = mybir.dt.bfloat16
+I32 = mybir.dt.int32
+U32 = mybir.dt.uint32
+U16 = mybir.dt.uint16
+U8 = mybir.dt.uint8
+FP8X4 = mybir.dt.float8_e4m3fn_x4
+FP4X4 = mybir.dt.float4_e2m1fn_x4
+ACT = mybir.ActivationFunctionType
+
+P = 128
+T, D, NQ, N = 2048, 1024, 256, 512
+PACK = 4
+K_PASS = P * PACK
+PASSES = D // K_PASS
+Q_TILES = NQ // P
+HALVES = 2
+HALF = N // HALVES
+CHUNKS = HALF // P
+KB_ROW = 16
+FLOPS = 2 * NQ * N * D
+
+
+def tile_attend_sigscat_topk_kernel(tc, qT, k_words, k_scales, kb, th, offs, out):
+    nc = tc.nc
+    with ExitStack() as ctx:
+        lists = ctx.enter_context(tc.tile_pool(name="lists", bufs=1))
+        keep = ctx.enter_context(tc.tile_pool(name="keep", bufs=1))
+        psum = ctx.enter_context(tc.psum_pool(name="psum", bufs=1))
+
+        offsets = lists.tile([P, N // 16], U16, name="offsets")
+        nc.sync.dma_start(offsets[:], offs)
+
+        def half_list(h):
+            return offsets[:, h * HALF // 16 : (h + 1) * HALF // 16]
+
+        th_cols = keep.tile([P, Q_TILES], F32, name="th_cols")
+        with nc.allow_non_contiguous_dma(reason="one threshold a partition"):
+            nc.scalar.dma_start(th_cols[:], th[0].rearrange("(t p) o -> p (t o)", p=P))
+
+        kb_pool = keep.tile([P, T], F32, name="kb_pool")
+        nc.vector.memset(kb_pool[:], 0.0)
+        scale_pool = keep.tile([P, PASSES, T // 4], I32, name="scale_pool")
+        nc.vector.memset(scale_pool[:], 0)
+
+        warm_in = keep.tile([P, 1], F32, name="warm_in")
+        warm_out = keep.tile([P, 1], F32, name="warm_out")
+        nc.gpsimd.memset(warm_in[:], 0.0)
+        nc.scalar.activation(warm_out[:], warm_in[:], ACT.Sigmoid)
+        ident = keep.tile([P, P], F32, name="ident")
+        make_identity(nc, ident[:])
+
+        q_raw = {}
+
+        def load_q(t):
+            for g in range(PASSES):
+                q_raw[t, g] = keep.tile([P, PACK, P], F32, name=f"q_raw{t}{g}")
+                rows = qT[0, g * K_PASS : (g + 1) * K_PASS, t * P : (t + 1) * P]
+                nc.sync.dma_start(q_raw[t, g][:], rows.rearrange("(p j) w -> p j w", j=PACK))
+
+        load_q(0)
+        nc.scalar.dma_start(kb_pool[KB_ROW : KB_ROW + 1, :], kb[0:1, :])
+        scale_rows = k_scales.bitcast(I32).rearrange("o (u r) t -> r u o t", r=4)
+        for r in range(4):
+            nc.sync.dma_start(scale_pool[r:P:32, :, :], scale_rows[r])
+        word_pool = keep.tile([P, T], I32, name="word_pool", tag="pool_then_map")
+        nc.sync.dma_start(word_pool[:], k_words[0].rearrange("p t b -> p (t b)").bitcast(I32))
+        load_q(1)
+
+        neg_th = keep.tile([P, Q_TILES], F32, name="neg_th")
+        nc.scalar.activation(neg_th[:], th_cols[:], ACT.Copy, scale=-1.0)
+
+        q_bf, q_codes, q_scales = {}, {}, {}
+
+        def cast_q(t):
+            q_bf[t] = keep.tile([P, PASSES, P, PACK], BF16, name=f"q_bf{t}", align_bytes=64)
+            for g in range(PASSES):
+                nc.scalar.copy(
+                    q_bf[t][:, g].rearrange("p (c i) j -> p c j i", i=4),
+                    q_raw[t, g][:].rearrange("p j (c i) -> p c j i", i=4),
+                )
+
+        def quantize_q(t):
+            q_codes[t] = keep.tile([P, PASSES * P], U32, name=f"q_codes{t}", align_bytes=64)
+            q_scales[t] = keep.tile([P, PASSES * P], U8, name=f"q_scales{t}", align_bytes=64)
+            nc.vector.quantize_mx(
+                out=q_codes[t][:].bitcast(FP8X4),
+                scales=q_scales[t][:],
+                in_=q_bf[t][:].rearrange("p g w j -> p (g w j)"),
+            )
+
+        maps = {0: keep.tile([P, T], F32, name="map0")}
+        nc.vector.memset(maps[0][:], 0.0)
+
+        cast_q(0)
+        kb_listed = keep.tile([P, N], F32, name="kb_listed")
+        nc.vector.tensor_copy(kb_listed[:], kb_pool[:].indirect(offsets[:]))
+        kb_turned = psum.tile([P, N // P, P], F32, name="kb_turned")
+        for c in range(N // P):
+            nc.tensor.transpose(kb_turned[:, c, :], kb_listed[:, c * P : (c + 1) * P], ident[:])
+        kb_cols = keep.tile([P, N // P], F32, name="kb_cols")
+        nc.scalar.copy(kb_cols[:], kb_turned[:, :, KB_ROW])
+        quantize_q(0)
+
+        k_bytes = []
+        for g in range(PASSES):
+            listed = keep.tile([P, N], U8, name=f"k_bytes{g}", align_bytes=64)
+            nc.vector.tensor_copy(listed[:], scale_pool[:, g, :].bitcast(U8).indirect(offsets[:]))
+            k_bytes.append(listed)
+
+        word_pairs, k_codes = [], []
+        for h in range(HALVES):
+            pairs = keep.tile([P, HALF], U32, name=f"word_pairs{h}")
+            nc.vector.tensor_copy(pairs[:], word_pool[:].bitcast(U32).indirect(half_list(h)))
+            word_pairs.append(pairs)
+        for h in range(HALVES):
+            codes = keep.tile([P, PASSES, HALF], U16, name=f"k_codes{h}", align_bytes=64)
+            nc.vector.tensor_copy(codes[:], word_pairs[h][:].bitcast(U16).rearrange("p (n g) -> p g n", g=PASSES))
+            k_codes.append(codes)
+
+        maps[1] = keep.tile([P, T], F32, name="map1", tag="pool_then_map")
+        nc.vector.memset(maps[1][:], 0.0)
+        cast_q(1)
+
+        gates = {}
+
+        def score(t, h):
+            sums = psum.tile([P, CHUNKS, P], F32, name="sums", bufs=3)
+            biased = keep.tile([P, CHUNKS, P], F32, name=f"biased{t}{h}")
+            for c in range(CHUNKS):
+                slots = slice(h * HALF + c * P, h * HALF + (c + 1) * P)
+                for g in range(PASSES):
+                    nc.tensor.matmul_mx(
+                        out=sums[:, c, :],
+                        lhsT=k_codes[h][:, g, c * P : (c + 1) * P].bitcast(FP4X4),
+                        lhsT_scale=k_bytes[g][:, slots],
+                        rhs=q_codes[t][:, g * P : (g + 1) * P].bitcast(FP8X4),
+                        rhs_scale=q_scales[t][:, g * P : (g + 1) * P],
+                        start=(g == 0),
+                        stop=(g == PASSES - 1),
+                    )
+            for c in range(CHUNKS):
+                col = h * CHUNKS + c
+                nc.scalar.activation(biased[:, c, :], sums[:, c, :], ACT.Identity, bias=kb_cols[:, col : col + 1])
+            turned = psum.tile([P, CHUNKS, P], F32, name="turned", bufs=3)
+            for c in range(CHUNKS):
+                nc.tensor.transpose(turned[:, c, :], biased[:, c, :], ident[:])
+            gates[t, h] = keep.tile([P, HALF], F32, name=f"gates{t}{h}")
+            nc.scalar.activation(
+                gates[t, h][:], turned[:].rearrange("p c s -> p (c s)"), ACT.Sigmoid, bias=neg_th[:, t : t + 1]
+            )
+
+        def place(t, h):
+            nc.vector.tensor_copy(maps[t][:].indirect(half_list(h)), gates[t, h][:])
+
+        def store(t):
+            nc.sync.dma_start(out[0, t * P : (t + 1) * P, :], maps[t][:])
+
+        score(0, 0)
+        score(0, 1)
+        place(0, 0)
+        quantize_q(1)
+        score(1, 0)
+        score(1, 1)
+        place(0, 1)
+        store(0)
+        place(1, 0)
+        place(1, 1)
+        store(1)

@@ -22,7 +22,9 @@ Q_TILES = NQ // P
 HALVES = 2
 HALF = N // HALVES
 CHUNKS = HALF // P
+BANK = 512
 KB_ROW = 16
+MAP_ON_VECTOR = 640
 FLOPS = 2 * NQ * N * D
 
 
@@ -39,115 +41,111 @@ def tile_attend_sigscat_topk_kernel(tc, qT, k_words, k_scales, kb, th, offs, out
         def half_list(h):
             return offsets[:, h * HALF // 16 : (h + 1) * HALF // 16]
 
+        def zero_on_vector(tile, columns):
+            nc.vector.memset(tile[:, : columns - 1], 0.0)
+            nc.vector.memset(tile[:, columns - 1 : columns], 0.0)
+
+        word_pool = keep.tile([P, T], I32, name="word_pool")
+        nc.sync.dma_start(word_pool[:], k_words[0].rearrange("p t b -> p (t b)").bitcast(I32))
         th_cols = keep.tile([P, Q_TILES], F32, name="th_cols")
         with nc.allow_non_contiguous_dma(reason="one threshold a partition"):
             nc.scalar.dma_start(th_cols[:], th[0].rearrange("(t p) o -> p (t o)", p=P))
 
-        kb_pool = keep.tile([P, T], F32, name="kb_pool")
-        nc.vector.memset(kb_pool[:], 0.0)
-        scale_pool = keep.tile([P, PASSES, T // 4], I32, name="scale_pool")
-        nc.vector.memset(scale_pool[:], 0)
-
-        warm_in = keep.tile([P, 1], F32, name="warm_in")
-        warm_out = keep.tile([P, 1], F32, name="warm_out")
-        nc.gpsimd.memset(warm_in[:], 0.0)
-        nc.scalar.activation(warm_out[:], warm_in[:], ACT.Sigmoid)
-        ident = keep.tile([P, P], F32, name="ident")
-        make_identity(nc, ident[:])
-
-        q_raw = {}
-
-        def load_q(t):
-            for g in range(PASSES):
-                q_raw[t, g] = keep.tile([P, PACK, P], F32, name=f"q_raw{t}{g}")
-                rows = qT[0, g * K_PASS : (g + 1) * K_PASS, t * P : (t + 1) * P]
-                nc.sync.dma_start(q_raw[t, g][:], rows.rearrange("(p j) w -> p j w", j=PACK))
-
-        load_q(0)
+        kb_pool = keep.tile([P, T], F32, name="kb_pool", tag="kb_then_words")
+        zero_on_vector(kb_pool, T // 2)
+        nc.gpsimd.memset(kb_pool[:, T // 2 :], 0.0)
         nc.scalar.dma_start(kb_pool[KB_ROW : KB_ROW + 1, :], kb[0:1, :])
+        scale_pool = keep.tile([P, PASSES * T // 4 + 1], I32, name="scale_pool")
+        nc.vector.memset(scale_pool[:], 0)
+        scale_passes = scale_pool[:, : PASSES * T // 4].rearrange("p (g w) -> p g w", g=PASSES)
         scale_rows = k_scales.bitcast(I32).rearrange("o (u r) t -> r u o t", r=4)
         for r in range(4):
-            nc.sync.dma_start(scale_pool[r:P:32, :, :], scale_rows[r])
-        word_pool = keep.tile([P, T], I32, name="word_pool", tag="pool_then_map")
-        nc.sync.dma_start(word_pool[:], k_words[0].rearrange("p t b -> p (t b)").bitcast(I32))
-        load_q(1)
+            nc.sync.dma_start(scale_passes[r:P:32, :, :], scale_rows[r])
 
-        neg_th = keep.tile([P, Q_TILES], F32, name="neg_th")
-        nc.scalar.activation(neg_th[:], th_cols[:], ACT.Copy, scale=-1.0)
+        warm_in = keep.tile([P, 1], F32, name="warm_in", tag="q_pass0")
+        warm_out = keep.tile([P, 1], F32, name="warm_out", tag="q_pass1")
+        nc.vector.memset(warm_in[:], 0.0)
+        nc.scalar.activation(warm_out[:], warm_in[:], ACT.Sigmoid)
 
-        q_bf, q_codes, q_scales = {}, {}, {}
+        q_raw = []
+        for g in range(PASSES):
+            raw = keep.tile([P, PACK, NQ], F32, name=f"q_raw{g}", tag=f"q_pass{g}")
+            rows = qT[0, g * K_PASS : (g + 1) * K_PASS, :]
+            nc.sync.dma_start(raw[:], rows.rearrange("(p j) w -> p j w", j=PACK))
+            q_raw.append(raw)
 
-        def cast_q(t):
-            q_bf[t] = keep.tile([P, PASSES, P, PACK], BF16, name=f"q_bf{t}", align_bytes=64)
-            for g in range(PASSES):
+        ident = keep.tile([P, P], F32, name="ident")
+        make_identity(nc, ident[:])
+        maps = [keep.tile([P, T], F32, name=f"map{t}") for t in range(Q_TILES)]
+        zero_on_vector(maps[0], MAP_ON_VECTOR)
+        nc.gpsimd.memset(maps[0][:, MAP_ON_VECTOR:], 0.0)
+        nc.gpsimd.memset(maps[1][:], 0.0)
+
+        q_codes, q_scales, k_bytes, k_codes = {}, {}, {}, {}
+
+        def quantize_q(t, passes, tag):
+            name = f"{t}{passes[0]}"
+            rounded = keep.tile([P, len(passes), P, PACK], BF16, name=f"q_bf{name}", tag=tag, align_bytes=64)
+            codes = keep.tile([P, len(passes), P], U32, name=f"q_codes{name}", align_bytes=64)
+            scales = keep.tile([P, len(passes), P], U8, name=f"q_scales{name}", align_bytes=64)
+            for i, g in enumerate(passes):
                 nc.scalar.copy(
-                    q_bf[t][:, g].rearrange("p (c i) j -> p c j i", i=4),
-                    q_raw[t, g][:].rearrange("p j (c i) -> p c j i", i=4),
+                    rounded[:, i].rearrange("p (c i) j -> p c j i", i=4),
+                    q_raw[g][:, :, t * P : (t + 1) * P].rearrange("p j (c i) -> p c j i", i=4),
                 )
-
-        def quantize_q(t):
-            q_codes[t] = keep.tile([P, PASSES * P], U32, name=f"q_codes{t}", align_bytes=64)
-            q_scales[t] = keep.tile([P, PASSES * P], U8, name=f"q_scales{t}", align_bytes=64)
+                q_codes[t, g], q_scales[t, g] = codes[:, i, :], scales[:, i, :]
             nc.vector.quantize_mx(
-                out=q_codes[t][:].bitcast(FP8X4),
-                scales=q_scales[t][:],
-                in_=q_bf[t][:].rearrange("p g w j -> p (g w j)"),
+                out=codes[:].rearrange("p g w -> p (g w)").bitcast(FP8X4),
+                scales=scales[:].rearrange("p g w -> p (g w)"),
+                in_=rounded[:].rearrange("p g w j -> p (g w j)"),
             )
 
-        maps = {0: keep.tile([P, T], F32, name="map0")}
-        nc.vector.memset(maps[0][:], 0.0)
+        def gather_bytes(h, tag):
+            listed = keep.tile([P, PASSES, HALF], U8, name=f"k_bytes{h}", tag=tag, align_bytes=64)
+            for g in range(PASSES):
+                window = scale_passes[:, g, :].bitcast(U8)
+                nc.vector.tensor_copy(listed[:, g, :], window.indirect(half_list(h)))
+            k_bytes[h] = listed
 
-        cast_q(0)
         kb_listed = keep.tile([P, N], F32, name="kb_listed")
         nc.vector.tensor_copy(kb_listed[:], kb_pool[:].indirect(offsets[:]))
-        kb_turned = psum.tile([P, N // P, P], F32, name="kb_turned")
+        kb_turned = psum.tile([P, N // P, P], F32, name="kb_turned", tag="bank_c")
         for c in range(N // P):
             nc.tensor.transpose(kb_turned[:, c, :], kb_listed[:, c * P : (c + 1) * P], ident[:])
         kb_cols = keep.tile([P, N // P], F32, name="kb_cols")
         nc.scalar.copy(kb_cols[:], kb_turned[:, :, KB_ROW])
-        quantize_q(0)
 
-        k_bytes = []
-        for g in range(PASSES):
-            listed = keep.tile([P, N], U8, name=f"k_bytes{g}", align_bytes=64)
-            nc.vector.tensor_copy(listed[:], scale_pool[:, g, :].bitcast(U8).indirect(offsets[:]))
-            k_bytes.append(listed)
+        word_pairs = keep.tile([P, HALVES, HALF], U32, name="word_pairs", tag="kb_then_words")
 
-        word_pairs, k_codes = [], []
-        for h in range(HALVES):
-            pairs = keep.tile([P, HALF], U32, name=f"word_pairs{h}")
-            nc.vector.tensor_copy(pairs[:], word_pool[:].bitcast(U32).indirect(half_list(h)))
-            word_pairs.append(pairs)
-        for h in range(HALVES):
-            codes = keep.tile([P, PASSES, HALF], U16, name=f"k_codes{h}", align_bytes=64)
-            nc.vector.tensor_copy(codes[:], word_pairs[h][:].bitcast(U16).rearrange("p (n g) -> p g n", g=PASSES))
-            k_codes.append(codes)
+        def gather_words(h):
+            nc.vector.tensor_copy(word_pairs[:, h, :], word_pool[:].bitcast(U32).indirect(half_list(h)))
 
-        maps[1] = keep.tile([P, T], F32, name="map1", tag="pool_then_map")
-        nc.vector.memset(maps[1][:], 0.0)
-        cast_q(1)
+        def part_words(h):
+            k_codes[h] = keep.tile([P, PASSES, HALF], U16, name=f"k_codes{h}", align_bytes=64)
+            nc.vector.tensor_copy(
+                k_codes[h][:], word_pairs[:, h, :].bitcast(U16).rearrange("p (n g) -> p g n", g=PASSES)
+            )
 
         gates = {}
 
-        def score(t, h):
-            sums = psum.tile([P, CHUNKS, P], F32, name="sums", bufs=3)
+        def score(t, h, sums_tag, turned_tag):
+            sums = psum.tile([P, CHUNKS, BANK], F32, name=f"sums{t}{h}", tag=sums_tag)
             biased = keep.tile([P, CHUNKS, P], F32, name=f"biased{t}{h}")
-            for c in range(CHUNKS):
-                slots = slice(h * HALF + c * P, h * HALF + (c + 1) * P)
-                for g in range(PASSES):
+            for g in range(PASSES):
+                for c in range(CHUNKS):
                     nc.tensor.matmul_mx(
-                        out=sums[:, c, :],
+                        out=sums[:, c, :P],
                         lhsT=k_codes[h][:, g, c * P : (c + 1) * P].bitcast(FP4X4),
-                        lhsT_scale=k_bytes[g][:, slots],
-                        rhs=q_codes[t][:, g * P : (g + 1) * P].bitcast(FP8X4),
-                        rhs_scale=q_scales[t][:, g * P : (g + 1) * P],
+                        lhsT_scale=k_bytes[h][:, g, c * P : (c + 1) * P],
+                        rhs=q_codes[t, g].bitcast(FP8X4),
+                        rhs_scale=q_scales[t, g],
                         start=(g == 0),
                         stop=(g == PASSES - 1),
                     )
             for c in range(CHUNKS):
-                col = h * CHUNKS + c
-                nc.scalar.activation(biased[:, c, :], sums[:, c, :], ACT.Identity, bias=kb_cols[:, col : col + 1])
-            turned = psum.tile([P, CHUNKS, P], F32, name="turned", bufs=3)
+                column = h * CHUNKS + c
+                nc.scalar.activation(biased[:, c, :], sums[:, c, :P], ACT.Identity, bias=kb_cols[:, column : column + 1])
+            turned = psum.tile([P, CHUNKS, P], F32, name=f"turned{t}{h}", tag=turned_tag)
             for c in range(CHUNKS):
                 nc.tensor.transpose(turned[:, c, :], biased[:, c, :], ident[:])
             gates[t, h] = keep.tile([P, HALF], F32, name=f"gates{t}{h}")
@@ -158,17 +156,28 @@ def tile_attend_sigscat_topk_kernel(tc, qT, k_words, k_scales, kb, th, offs, out
         def place(t, h):
             nc.vector.tensor_copy(maps[t][:].indirect(half_list(h)), gates[t, h][:])
 
-        def store(t):
-            nc.sync.dma_start(out[0, t * P : (t + 1) * P, :], maps[t][:])
+        def store(t, queue, lo, hi):
+            queue.dma_start(out[0, t * P : (t + 1) * P, lo:hi], maps[t][:, lo:hi])
 
-        score(0, 0)
-        score(0, 1)
+        gather_words(0)
+        gather_words(1)
+        part_words(0)
+        part_words(1)
+        gather_bytes(0, "k_bytes0")
+        quantize_q(0, (0,), "q_bf00")
+        quantize_q(0, (1,), "q_then_bytes")
+        neg_th = keep.tile([P, Q_TILES], F32, name="neg_th")
+        nc.scalar.activation(neg_th[:], th_cols[:], ACT.Copy, scale=-1.0)
+        score(0, 0, "banks_a", "banks_b")
+        gather_bytes(1, "q_then_bytes")
+        quantize_q(1, (0, 1), "q_bf1")
+        score(0, 1, "banks_a", "bank_c")
+        score(1, 0, "banks_b", "bank_d")
+        score(1, 1, "banks_a", "bank_e")
         place(0, 0)
-        quantize_q(1)
-        score(1, 0)
-        score(1, 1)
         place(0, 1)
-        store(0)
+        store(0, nc.sync, 0, T)
         place(1, 0)
         place(1, 1)
-        store(1)
+        store(1, nc.sync, 0, T // 2)
+        store(1, nc.scalar, T // 2, T)

@@ -24,7 +24,6 @@ HALF = N // HALVES
 CHUNKS = HALF // P
 BANK = 512
 KB_ROW = 16
-MAP_ON_VECTOR = 640
 FLOPS = 2 * NQ * N * D
 
 
@@ -41,45 +40,35 @@ def tile_attend_sigscat_topk_kernel(tc, qT, k_words, k_scales, kb, th, offs, out
         def half_list(h):
             return offsets[:, h * HALF // 16 : (h + 1) * HALF // 16]
 
-        def zero_on_vector(tile, columns):
-            nc.vector.memset(tile[:, : columns - 1], 0.0)
-            nc.vector.memset(tile[:, columns - 1 : columns], 0.0)
-
         word_pool = keep.tile([P, T], I32, name="word_pool")
         nc.sync.dma_start(word_pool[:], k_words[0].rearrange("p t b -> p (t b)").bitcast(I32))
-        th_cols = keep.tile([P, Q_TILES], F32, name="th_cols")
-        with nc.allow_non_contiguous_dma(reason="one threshold a partition"):
-            nc.scalar.dma_start(th_cols[:], th[0].rearrange("(t p) o -> p (t o)", p=P))
 
         kb_pool = keep.tile([P, T], F32, name="kb_pool", tag="kb_then_words")
-        zero_on_vector(kb_pool, T // 2)
-        nc.gpsimd.memset(kb_pool[:, T // 2 :], 0.0)
+        nc.vector.memset(kb_pool[:], 0.0)
         nc.scalar.dma_start(kb_pool[KB_ROW : KB_ROW + 1, :], kb[0:1, :])
-        scale_pool = keep.tile([P, PASSES * T // 4 + 1], I32, name="scale_pool")
-        nc.vector.memset(scale_pool[:], 0)
-        scale_passes = scale_pool[:, : PASSES * T // 4].rearrange("p (g w) -> p g w", g=PASSES)
+        scale_passes = keep.tile([P, PASSES, T // 4], I32, name="scale_passes", tag="scales_then_map")
+        nc.vector.memset(scale_passes[:], 0)
         scale_rows = k_scales.bitcast(I32).rearrange("o (u r) t -> r u o t", r=4)
         for r in range(4):
             nc.sync.dma_start(scale_passes[r:P:32, :, :], scale_rows[r])
 
-        warm_in = keep.tile([P, 1], F32, name="warm_in", tag="q_pass0")
-        warm_out = keep.tile([P, 1], F32, name="warm_out", tag="q_pass1")
+        warm_in = keep.tile([P, 1], F32, name="warm_in", tag="warm_then_th")
+        warm_out = keep.tile([P, 1], F32, name="warm_out", tag="warm_then_q")
         nc.vector.memset(warm_in[:], 0.0)
         nc.scalar.activation(warm_out[:], warm_in[:], ACT.Sigmoid)
 
-        q_raw = []
+        q_raw = keep.tile([P, PASSES, PACK, NQ], F32, name="q_raw", tag="warm_then_q")
         for g in range(PASSES):
-            raw = keep.tile([P, PACK, NQ], F32, name=f"q_raw{g}", tag=f"q_pass{g}")
             rows = qT[0, g * K_PASS : (g + 1) * K_PASS, :]
-            nc.sync.dma_start(raw[:], rows.rearrange("(p j) w -> p j w", j=PACK))
-            q_raw.append(raw)
+            nc.sync.dma_start(q_raw[:, g], rows.rearrange("(p j) w -> p j w", j=PACK))
+        th_cols = keep.tile([P, Q_TILES], F32, name="th_cols", tag="warm_then_th")
+        with nc.allow_non_contiguous_dma(reason="one threshold a partition"):
+            nc.sync.dma_start(th_cols[:], th[0].rearrange("(t p) o -> p (t o)", p=P))
 
         ident = keep.tile([P, P], F32, name="ident")
         make_identity(nc, ident[:])
-        maps = [keep.tile([P, T], F32, name=f"map{t}") for t in range(Q_TILES)]
-        zero_on_vector(maps[0], MAP_ON_VECTOR)
-        nc.gpsimd.memset(maps[0][:, MAP_ON_VECTOR:], 0.0)
-        nc.gpsimd.memset(maps[1][:], 0.0)
+        maps = {0: keep.tile([P, T], F32, name="map0")}
+        nc.vector.memset(maps[0][:], 0.0)
 
         q_codes, q_scales, k_bytes, k_codes = {}, {}, {}, {}
 
@@ -91,7 +80,7 @@ def tile_attend_sigscat_topk_kernel(tc, qT, k_words, k_scales, kb, th, offs, out
             for i, g in enumerate(passes):
                 nc.scalar.copy(
                     rounded[:, i].rearrange("p (c i) j -> p c j i", i=4),
-                    q_raw[g][:, :, t * P : (t + 1) * P].rearrange("p j (c i) -> p c j i", i=4),
+                    q_raw[:, g, :, t * P : (t + 1) * P].rearrange("p j (c i) -> p c j i", i=4),
                 )
                 q_codes[t, g], q_scales[t, g] = codes[:, i, :], scales[:, i, :]
             nc.vector.quantize_mx(
@@ -171,6 +160,8 @@ def tile_attend_sigscat_topk_kernel(tc, qT, k_words, k_scales, kb, th, offs, out
         score(0, 0, "banks_a", "banks_b")
         gather_bytes(1, "q_then_bytes")
         quantize_q(1, (0, 1), "q_bf1")
+        maps[1] = keep.tile([P, T], F32, name="map1", tag="scales_then_map")
+        nc.vector.memset(maps[1][:], 0.0)
         score(0, 1, "banks_a", "bank_c")
         score(1, 0, "banks_b", "bank_d")
         score(1, 1, "banks_a", "bank_e")

@@ -24,6 +24,7 @@ HALF = N // HALVES
 CHUNKS = HALF // P
 BANK = 512
 KB_ROW = 16
+SHIFT = 16
 FLOPS = 2 * NQ * N * D
 
 
@@ -40,61 +41,48 @@ def tile_attend_sigscat_topk_kernel(tc, qT, k_words, k_scales, kb, th, offs, out
         def half_list(h):
             return offsets[:, h * HALF // 16 : (h + 1) * HALF // 16]
 
+        q_raw = {}
+
+        def load_q(g):
+            q_raw[g] = keep.tile([P, PACK, NQ], F32, name=f"q_raw{g}")
+            rows = qT[0, g * K_PASS : (g + 1) * K_PASS, :]
+            nc.scalar.dma_start(q_raw[g][:], rows.rearrange("(p j) w -> p j w", j=PACK))
+
+        load_q(0)
         word_pool = keep.tile([P, T], I32, name="word_pool")
-        nc.sync.dma_start(word_pool[:], k_words[0].rearrange("p t b -> p (t b)").bitcast(I32))
+        nc.scalar.dma_start(word_pool[:], k_words[0].rearrange("p t b -> p (t b)").bitcast(I32))
+
+        warm_in = keep.tile([P, 1], F32, name="warm_in")
+        warm_out = keep.tile([P, 1], F32, name="warm_out")
+        nc.gpsimd.memset(warm_in[:], 0.0)
+        nc.scalar.activation(warm_out[:], warm_in[:], ACT.Sigmoid)
+        load_q(1)
+
+        scale_pool = keep.tile([P, T // 4], I32, name="scale_pool", tag="scales_then_th")
+        nc.vector.memset(scale_pool[:], 0)
+        scale_rows = k_scales.bitcast(I32).rearrange("o (u r) t -> r u o t", r=4)
+        for r in range(4):
+            nc.sync.dma_start(scale_pool[r:P:SHIFT, :], scale_rows[r])
 
         kb_pool = keep.tile([P, T], F32, name="kb_pool", tag="kb_then_words")
         nc.vector.memset(kb_pool[:], 0.0)
-        nc.scalar.dma_start(kb_pool[KB_ROW : KB_ROW + 1, :], kb[0:1, :])
-        scale_passes = keep.tile([P, PASSES, T // 4], I32, name="scale_passes", tag="scales_then_map")
-        nc.vector.memset(scale_passes[:], 0)
-        scale_rows = k_scales.bitcast(I32).rearrange("o (u r) t -> r u o t", r=4)
-        for r in range(4):
-            nc.sync.dma_start(scale_passes[r:P:32, :, :], scale_rows[r])
-
-        warm_in = keep.tile([P, 1], F32, name="warm_in", tag="warm_then_th")
-        warm_out = keep.tile([P, 1], F32, name="warm_out", tag="warm_then_q")
-        nc.vector.memset(warm_in[:], 0.0)
-        nc.scalar.activation(warm_out[:], warm_in[:], ACT.Sigmoid)
-
-        q_raw = keep.tile([P, PASSES, PACK, NQ], F32, name="q_raw", tag="warm_then_q")
-        for g in range(PASSES):
-            rows = qT[0, g * K_PASS : (g + 1) * K_PASS, :]
-            nc.sync.dma_start(q_raw[:, g], rows.rearrange("(p j) w -> p j w", j=PACK))
-        th_cols = keep.tile([P, Q_TILES], F32, name="th_cols", tag="warm_then_th")
-        with nc.allow_non_contiguous_dma(reason="one threshold a partition"):
-            nc.sync.dma_start(th_cols[:], th[0].rearrange("(t p) o -> p (t o)", p=P))
+        nc.sync.dma_start(kb_pool[KB_ROW : KB_ROW + 1, :], kb[0:1, :])
 
         ident = keep.tile([P, P], F32, name="ident")
         make_identity(nc, ident[:])
+        shifted_bytes = keep.tile([P, N // 4], I32, name="shifted_bytes", align_bytes=64)
+        nc.vector.memset(shifted_bytes[:], 0)
         maps = {0: keep.tile([P, T], F32, name="map0")}
         nc.vector.memset(maps[0][:], 0.0)
 
-        q_codes, q_scales, k_bytes, k_codes = {}, {}, {}, {}
+        listed_bytes = keep.tile([P, N], U8, name="listed_bytes", align_bytes=64)
+        nc.vector.tensor_copy(listed_bytes[:], scale_pool[:].bitcast(U8).indirect(offsets[:]))
+        nc.sync.dma_start(shifted_bytes[: P - SHIFT, :], listed_bytes[SHIFT:, :].bitcast(I32))
+        k_planes = (listed_bytes[:], shifted_bytes[:].bitcast(U8))
 
-        def quantize_q(t, passes, tag):
-            name = f"{t}{passes[0]}"
-            rounded = keep.tile([P, len(passes), P, PACK], BF16, name=f"q_bf{name}", tag=tag, align_bytes=64)
-            codes = keep.tile([P, len(passes), P], U32, name=f"q_codes{name}", align_bytes=64)
-            scales = keep.tile([P, len(passes), P], U8, name=f"q_scales{name}", align_bytes=64)
-            for i, g in enumerate(passes):
-                nc.scalar.copy(
-                    rounded[:, i].rearrange("p (c i) j -> p c j i", i=4),
-                    q_raw[:, g, :, t * P : (t + 1) * P].rearrange("p j (c i) -> p c j i", i=4),
-                )
-                q_codes[t, g], q_scales[t, g] = codes[:, i, :], scales[:, i, :]
-            nc.vector.quantize_mx(
-                out=codes[:].rearrange("p g w -> p (g w)").bitcast(FP8X4),
-                scales=scales[:].rearrange("p g w -> p (g w)"),
-                in_=rounded[:].rearrange("p g w j -> p (g w j)"),
-            )
-
-        def gather_bytes(h, tag):
-            listed = keep.tile([P, PASSES, HALF], U8, name=f"k_bytes{h}", tag=tag, align_bytes=64)
-            for g in range(PASSES):
-                window = scale_passes[:, g, :].bitcast(U8)
-                nc.vector.tensor_copy(listed[:, g, :], window.indirect(half_list(h)))
-            k_bytes[h] = listed
+        th_cols = keep.tile([P, Q_TILES], F32, name="th_cols", tag="scales_then_th")
+        with nc.allow_non_contiguous_dma(reason="one threshold a partition"):
+            nc.sync.dma_start(th_cols[:], th[0].rearrange("(t p) o -> p (t o)", p=P))
 
         kb_listed = keep.tile([P, N], F32, name="kb_listed")
         nc.vector.tensor_copy(kb_listed[:], kb_pool[:].indirect(offsets[:]))
@@ -103,6 +91,26 @@ def tile_attend_sigscat_topk_kernel(tc, qT, k_words, k_scales, kb, th, offs, out
             nc.tensor.transpose(kb_turned[:, c, :], kb_listed[:, c * P : (c + 1) * P], ident[:])
         kb_cols = keep.tile([P, N // P], F32, name="kb_cols")
         nc.scalar.copy(kb_cols[:], kb_turned[:, :, KB_ROW])
+
+        q_codes, q_scales, k_codes = {}, {}, {}
+
+        def quantize_q(g, tiles, tag):
+            name = f"{g}{tiles[0]}"
+            rounded = keep.tile([P, len(tiles), P, PACK], BF16, name=f"q_bf{name}", tag=tag, align_bytes=64)
+            codes = keep.tile([P, len(tiles), P], U32, name=f"q_codes{name}", align_bytes=64)
+            scales = keep.tile([P, len(tiles), P], U8, name=f"q_scales{name}", align_bytes=64)
+            lo, hi = tiles[0] * P, (tiles[-1] + 1) * P
+            nc.scalar.copy(
+                rounded[:].rearrange("p t (c i) j -> p (t c) j i", i=4),
+                q_raw[g][:, :, lo:hi].rearrange("p j (c i) -> p c j i", i=4),
+            )
+            for i, t in enumerate(tiles):
+                q_codes[t, g], q_scales[t, g] = codes[:, i, :], scales[:, i, :]
+            nc.vector.quantize_mx(
+                out=codes[:].rearrange("p t w -> p (t w)").bitcast(FP8X4),
+                scales=scales[:].rearrange("p t w -> p (t w)"),
+                in_=rounded[:].rearrange("p t w j -> p (t w j)"),
+            )
 
         word_pairs = keep.tile([P, HALVES, HALF], U32, name="word_pairs", tag="kb_then_words")
 
@@ -122,10 +130,11 @@ def tile_attend_sigscat_topk_kernel(tc, qT, k_words, k_scales, kb, th, offs, out
             biased = keep.tile([P, CHUNKS, P], F32, name=f"biased{t}{h}")
             for g in range(PASSES):
                 for c in range(CHUNKS):
+                    slot = h * HALF + c * P
                     nc.tensor.matmul_mx(
                         out=sums[:, c, :P],
                         lhsT=k_codes[h][:, g, c * P : (c + 1) * P].bitcast(FP4X4),
-                        lhsT_scale=k_bytes[h][:, g, c * P : (c + 1) * P],
+                        lhsT_scale=k_planes[g][:, slot : slot + P],
                         rhs=q_codes[t, g].bitcast(FP8X4),
                         rhs_scale=q_scales[t, g],
                         start=(g == 0),
@@ -148,19 +157,17 @@ def tile_attend_sigscat_topk_kernel(tc, qT, k_words, k_scales, kb, th, offs, out
         def store(t, queue, lo, hi):
             queue.dma_start(out[0, t * P : (t + 1) * P, lo:hi], maps[t][:, lo:hi])
 
+        quantize_q(0, (0, 1), "q_bf0")
         gather_words(0)
         gather_words(1)
         part_words(0)
         part_words(1)
-        gather_bytes(0, "k_bytes0")
-        quantize_q(0, (0,), "q_bf00")
-        quantize_q(0, (1,), "q_then_bytes")
+        quantize_q(1, (0,), "q_then_map")
+        quantize_q(1, (1,), "q_bf11")
         neg_th = keep.tile([P, Q_TILES], F32, name="neg_th")
         nc.scalar.activation(neg_th[:], th_cols[:], ACT.Copy, scale=-1.0)
         score(0, 0, "banks_a", "banks_b")
-        gather_bytes(1, "q_then_bytes")
-        quantize_q(1, (0, 1), "q_bf1")
-        maps[1] = keep.tile([P, T], F32, name="map1", tag="scales_then_map")
+        maps[1] = keep.tile([P, T], F32, name="map1", tag="q_then_map", align_bytes=64)
         nc.vector.memset(maps[1][:], 0.0)
         score(0, 1, "banks_a", "bank_c")
         score(1, 0, "banks_b", "bank_d")

@@ -23,6 +23,7 @@ HALVES = 2
 HALF = N // HALVES
 CHUNKS = HALF // P
 BANK = 512
+BANK_BYTES = 4 * BANK
 KB_ROW = 16
 SHIFT = 16
 FLOPS = 2 * NQ * N * D
@@ -41,35 +42,41 @@ def tile_attend_sigscat_topk_kernel(tc, qT, k_words, k_scales, kb, th, offs, out
         def half_list(h):
             return offsets[:, h * HALF // 16 : (h + 1) * HALF // 16]
 
-        q_raw = {}
+        q_raw = [keep.tile([P, PASSES, PACK, P], F32, name="q_raw0")]
 
-        def load_q(g):
-            q_raw[g] = keep.tile([P, PACK, NQ], F32, name=f"q_raw{g}")
-            rows = qT[0, g * K_PASS : (g + 1) * K_PASS, :]
-            nc.scalar.dma_start(q_raw[g][:], rows.rearrange("(p j) w -> p j w", j=PACK))
+        def load_q(t, g):
+            rows = qT[0, g * K_PASS : (g + 1) * K_PASS, t * P : (t + 1) * P]
+            nc.sync.dma_start(q_raw[t][:, g], rows.rearrange("(p j) w -> p j w", j=PACK))
 
-        load_q(0)
-        word_pool = keep.tile([P, T], I32, name="word_pool")
-        nc.scalar.dma_start(word_pool[:], k_words[0].rearrange("p t b -> p (t b)").bitcast(I32))
+        load_q(0, 0)
 
-        warm_in = keep.tile([P, 1], F32, name="warm_in")
-        warm_out = keep.tile([P, 1], F32, name="warm_out")
-        nc.gpsimd.memset(warm_in[:], 0.0)
-        nc.scalar.activation(warm_out[:], warm_in[:], ACT.Sigmoid)
-        load_q(1)
-
-        scale_pool = keep.tile([P, T // 4], I32, name="scale_pool", tag="scales_then_th")
+        scale_pool = keep.tile([P, T // 4], I32, name="scale_pool")
         nc.vector.memset(scale_pool[:], 0)
         scale_rows = k_scales.bitcast(I32).rearrange("o (u r) t -> r u o t", r=4)
         for r in range(4):
             nc.sync.dma_start(scale_pool[r:P:SHIFT, :], scale_rows[r])
+        load_q(0, 1)
 
-        kb_pool = keep.tile([P, T], F32, name="kb_pool", tag="kb_then_words")
+        kb_pool = keep.tile([P, T], F32, name="kb_pool", tag="kb_then_codes", align_bytes=64)
         nc.vector.memset(kb_pool[:], 0.0)
         nc.sync.dma_start(kb_pool[KB_ROW : KB_ROW + 1, :], kb[0:1, :])
 
-        ident = keep.tile([P, P], F32, name="ident")
+        word_pool = keep.tile([P, T], I32, name="word_pool")
+        nc.sync.dma_start(word_pool[:], k_words[0].rearrange("p t b -> p (t b)").bitcast(I32))
+        q_raw.append(keep.tile([P, PASSES, PACK, P], F32, name="q_raw1", tag="q_then_kb"))
+        for g in range(PASSES):
+            load_q(1, g)
+        th_cols = keep.tile([P, Q_TILES], F32, name="th_cols")
+        with nc.allow_non_contiguous_dma(reason="one threshold a partition"):
+            nc.sync.dma_start(th_cols[:], th[0].rearrange("(t p) o -> p (t o)", p=P))
+
+        warm_in = keep.tile([P, 1], F32, name="warm_in", tag="warm_then_ident")
+        warm_out = keep.tile([P, 1], F32, name="warm_out")
+        nc.gpsimd.memset(warm_in[:], 0.0)
+        nc.scalar.activation(warm_out[:], warm_in[:], ACT.Sigmoid)
+        ident = keep.tile([P, P], F32, name="ident", tag="warm_then_ident")
         make_identity(nc, ident[:])
+
         shifted_bytes = keep.tile([P, N // 4], I32, name="shifted_bytes", align_bytes=64)
         nc.vector.memset(shifted_bytes[:], 0)
         maps = {0: keep.tile([P, T], F32, name="map0")}
@@ -77,56 +84,39 @@ def tile_attend_sigscat_topk_kernel(tc, qT, k_words, k_scales, kb, th, offs, out
 
         listed_bytes = keep.tile([P, N], U8, name="listed_bytes", align_bytes=64)
         nc.vector.tensor_copy(listed_bytes[:], scale_pool[:].bitcast(U8).indirect(offsets[:]))
-        nc.sync.dma_start(shifted_bytes[: P - SHIFT, :], listed_bytes[SHIFT:, :].bitcast(I32))
+        for r in range(4):
+            nc.sync.dma_start(shifted_bytes[r:P:32, :], listed_bytes[:].bitcast(I32)[SHIFT + r : P : 32, :])
         k_planes = (listed_bytes[:], shifted_bytes[:].bitcast(U8))
 
-        th_cols = keep.tile([P, Q_TILES], F32, name="th_cols", tag="scales_then_th")
-        with nc.allow_non_contiguous_dma(reason="one threshold a partition"):
-            nc.sync.dma_start(th_cols[:], th[0].rearrange("(t p) o -> p (t o)", p=P))
+        q_codes, q_scales, k_codes, word_pairs = {}, {}, {}, {}
 
-        kb_listed = keep.tile([P, N], F32, name="kb_listed")
-        nc.vector.tensor_copy(kb_listed[:], kb_pool[:].indirect(offsets[:]))
-        kb_turned = psum.tile([P, N // P, P], F32, name="kb_turned", tag="bank_c")
-        for c in range(N // P):
-            nc.tensor.transpose(kb_turned[:, c, :], kb_listed[:, c * P : (c + 1) * P], ident[:])
-        kb_cols = keep.tile([P, N // P], F32, name="kb_cols")
-        nc.scalar.copy(kb_cols[:], kb_turned[:, :, KB_ROW])
-
-        q_codes, q_scales, k_codes = {}, {}, {}
-
-        def quantize_q(g, tiles, tag):
-            name = f"{g}{tiles[0]}"
-            rounded = keep.tile([P, len(tiles), P, PACK], BF16, name=f"q_bf{name}", tag=tag, align_bytes=64)
-            codes = keep.tile([P, len(tiles), P], U32, name=f"q_codes{name}", align_bytes=64)
-            scales = keep.tile([P, len(tiles), P], U8, name=f"q_scales{name}", align_bytes=64)
-            lo, hi = tiles[0] * P, (tiles[-1] + 1) * P
-            nc.scalar.copy(
-                rounded[:].rearrange("p t (c i) j -> p (t c) j i", i=4),
-                q_raw[g][:, :, lo:hi].rearrange("p j (c i) -> p c j i", i=4),
-            )
-            for i, t in enumerate(tiles):
-                q_codes[t, g], q_scales[t, g] = codes[:, i, :], scales[:, i, :]
+        def quantize_q(t, codes_tag):
+            rounded = keep.tile([P, PASSES, P, PACK], BF16, name=f"q_bf{t}", align_bytes=64)
+            q_codes[t] = keep.tile([P, PASSES, P], U32, name=f"q_codes{t}", tag=codes_tag, align_bytes=64)
+            q_scales[t] = keep.tile([P, PASSES, P], U8, name=f"q_scales{t}", align_bytes=64)
+            for g in range(PASSES):
+                nc.scalar.copy(
+                    rounded[:, g].rearrange("p (c i) j -> p c j i", i=4),
+                    q_raw[t][:, g].rearrange("p j (c i) -> p c j i", i=4),
+                )
             nc.vector.quantize_mx(
-                out=codes[:].rearrange("p t w -> p (t w)").bitcast(FP8X4),
-                scales=scales[:].rearrange("p t w -> p (t w)"),
-                in_=rounded[:].rearrange("p t w j -> p (t w j)"),
+                out=q_codes[t][:].rearrange("p g w -> p (g w)").bitcast(FP8X4),
+                scales=q_scales[t][:].rearrange("p g w -> p (g w)"),
+                in_=rounded[:].rearrange("p g w j -> p (g w j)"),
             )
-
-        word_pairs = keep.tile([P, HALVES, HALF], U32, name="word_pairs", tag="kb_then_words")
 
         def gather_words(h):
-            nc.vector.tensor_copy(word_pairs[:, h, :], word_pool[:].bitcast(U32).indirect(half_list(h)))
+            word_pairs[h] = keep.tile([P, HALF], U32, name=f"word_pairs{h}", tag="words_then_map")
+            nc.vector.tensor_copy(word_pairs[h][:], word_pool[:].bitcast(U32).indirect(half_list(h)))
 
         def part_words(h):
             k_codes[h] = keep.tile([P, PASSES, HALF], U16, name=f"k_codes{h}", align_bytes=64)
             nc.vector.tensor_copy(
-                k_codes[h][:], word_pairs[:, h, :].bitcast(U16).rearrange("p (n g) -> p g n", g=PASSES)
+                k_codes[h][:], word_pairs[h][:].bitcast(U16).rearrange("p (n g) -> p g n", g=PASSES)
             )
 
-        gates = {}
-
-        def score(t, h, sums_tag, turned_tag):
-            sums = psum.tile([P, CHUNKS, BANK], F32, name=f"sums{t}{h}", tag=sums_tag)
+        def score(t, h, sums_bank, turned_bank, gates):
+            sums = psum.tile([P, CHUNKS, BANK], F32, name=f"sums{t}{h}", offset=sums_bank * BANK_BYTES)
             biased = keep.tile([P, CHUNKS, P], F32, name=f"biased{t}{h}")
             for g in range(PASSES):
                 for c in range(CHUNKS):
@@ -135,47 +125,51 @@ def tile_attend_sigscat_topk_kernel(tc, qT, k_words, k_scales, kb, th, offs, out
                         out=sums[:, c, :P],
                         lhsT=k_codes[h][:, g, c * P : (c + 1) * P].bitcast(FP4X4),
                         lhsT_scale=k_planes[g][:, slot : slot + P],
-                        rhs=q_codes[t, g].bitcast(FP8X4),
-                        rhs_scale=q_scales[t, g],
+                        rhs=q_codes[t][:, g, :].bitcast(FP8X4),
+                        rhs_scale=q_scales[t][:, g, :],
                         start=(g == 0),
                         stop=(g == PASSES - 1),
                     )
             for c in range(CHUNKS):
                 column = h * CHUNKS + c
                 nc.scalar.activation(biased[:, c, :], sums[:, c, :P], ACT.Identity, bias=kb_cols[:, column : column + 1])
-            turned = psum.tile([P, CHUNKS, P], F32, name=f"turned{t}{h}", tag=turned_tag)
+            turned = psum.tile([P, CHUNKS, P], F32, name=f"turned{t}{h}", offset=turned_bank * BANK_BYTES)
             for c in range(CHUNKS):
                 nc.tensor.transpose(turned[:, c, :], biased[:, c, :], ident[:])
-            gates[t, h] = keep.tile([P, HALF], F32, name=f"gates{t}{h}")
             nc.scalar.activation(
-                gates[t, h][:], turned[:].rearrange("p c s -> p (c s)"), ACT.Sigmoid, bias=neg_th[:, t : t + 1]
+                gates, turned[:].rearrange("p c s -> p (c s)"), ACT.Sigmoid, bias=neg_th[:, t : t + 1]
             )
-
-        def place(t, h):
-            nc.vector.tensor_copy(maps[t][:].indirect(half_list(h)), gates[t, h][:])
 
         def store(t, queue, lo, hi):
             queue.dma_start(out[0, t * P : (t + 1) * P, lo:hi], maps[t][:, lo:hi])
 
-        quantize_q(0, (0, 1), "q_bf0")
+        kb_listed = keep.tile([P, N], F32, name="kb_listed")
+        nc.vector.tensor_copy(kb_listed[:], kb_pool[:].indirect(offsets[:]))
+        kb_turned = psum.tile([P, N // P, P], F32, name="kb_turned", offset=7 * BANK_BYTES)
+        for c in range(N // P):
+            nc.tensor.transpose(kb_turned[:, c, :], kb_listed[:, c * P : (c + 1) * P], ident[:])
+        quantize_q(0, "kb_then_codes")
         gather_words(0)
-        gather_words(1)
         part_words(0)
+        gather_words(1)
         part_words(1)
-        quantize_q(1, (0,), "q_then_map")
-        quantize_q(1, (1,), "q_bf11")
+        quantize_q(1, "q_codes1")
+        kb_cols = keep.tile([P, N // P], F32, name="kb_cols", tag="q_then_kb")
+        nc.scalar.copy(kb_cols[:], kb_turned[:, :, KB_ROW])
         neg_th = keep.tile([P, Q_TILES], F32, name="neg_th")
         nc.scalar.activation(neg_th[:], th_cols[:], ACT.Copy, scale=-1.0)
-        score(0, 0, "banks_a", "banks_b")
-        maps[1] = keep.tile([P, T], F32, name="map1", tag="q_then_map", align_bytes=64)
+        maps[1] = keep.tile([P, T], F32, name="map1", tag="words_then_map")
         nc.vector.memset(maps[1][:], 0.0)
-        score(0, 1, "banks_a", "bank_c")
-        score(1, 0, "banks_b", "bank_d")
-        score(1, 1, "banks_a", "bank_e")
-        place(0, 0)
-        place(0, 1)
+        first_gates = keep.tile([P, HALF], F32, name="first_gates")
+        second_gates = keep.tile([P, HALF], F32, name="second_gates")
+        last_gates = keep.tile([P, N], F32, name="last_gates")
+        score(0, 0, 0, 3, first_gates[:])
+        score(0, 1, 1, 7, second_gates[:])
+        score(1, 0, 3, 5, last_gates[:, :HALF])
+        score(1, 1, 0, 6, last_gates[:, HALF:])
+        nc.vector.tensor_copy(maps[0][:].indirect(half_list(0)), first_gates[:])
+        nc.vector.tensor_copy(maps[0][:].indirect(half_list(1)), second_gates[:])
         store(0, nc.sync, 0, T)
-        place(1, 0)
-        place(1, 1)
+        nc.vector.tensor_copy(maps[1][:].indirect(offsets[:]), last_gates[:])
         store(1, nc.sync, 0, T // 2)
         store(1, nc.scalar, T // 2, T)

@@ -12,6 +12,7 @@ U8 = mybir.dt.uint8
 FP8X4 = mybir.dt.float8_e4m3fn_x4
 FP4X4 = mybir.dt.float4_e2m1fn_x4
 ACT = mybir.ActivationFunctionType
+ADD = mybir.AluOpType.add
 
 P = 128
 T, D, NQ, N = 2048, 1024, 256, 512
@@ -42,20 +43,21 @@ def tile_attend_sigscat_topk_kernel(tc, qT, k_words, k_scales, kb, th, offs, out
         def half_list(h):
             return offsets[:, h * HALF // 16 : (h + 1) * HALF // 16]
 
-        q_raw = [keep.tile([P, PASSES, PACK, P], F32, name="q_raw0")]
+        q_raw = {}
 
-        def load_q(t, g):
+        def load_q(t, g, tag):
+            q_raw[t, g] = keep.tile([P, PACK, P], F32, name=f"q_raw{t}{g}", tag=tag)
             rows = qT[0, g * K_PASS : (g + 1) * K_PASS, t * P : (t + 1) * P]
-            nc.sync.dma_start(q_raw[t][:, g], rows.rearrange("(p j) w -> p j w", j=PACK))
+            nc.sync.dma_start(q_raw[t, g][:], rows.rearrange("(p j) w -> p j w", j=PACK))
 
-        load_q(0, 0)
+        load_q(0, 0, "q_raw00")
 
         scale_pool = keep.tile([P, T // 4], I32, name="scale_pool")
         nc.vector.memset(scale_pool[:], 0)
         scale_rows = k_scales.bitcast(I32).rearrange("o (u r) t -> r u o t", r=4)
         for r in range(4):
             nc.sync.dma_start(scale_pool[r:P:SHIFT, :], scale_rows[r])
-        load_q(0, 1)
+        load_q(0, 1, "q_raw01")
 
         kb_pool = keep.tile([P, T], F32, name="kb_pool", tag="kb_then_codes", align_bytes=64)
         nc.vector.memset(kb_pool[:], 0.0)
@@ -63,9 +65,8 @@ def tile_attend_sigscat_topk_kernel(tc, qT, k_words, k_scales, kb, th, offs, out
 
         word_pool = keep.tile([P, T], I32, name="word_pool")
         nc.sync.dma_start(word_pool[:], k_words[0].rearrange("p t b -> p (t b)").bitcast(I32))
-        q_raw.append(keep.tile([P, PASSES, PACK, P], F32, name="q_raw1", tag="q_then_kb"))
-        for g in range(PASSES):
-            load_q(1, g)
+        load_q(1, 0, "q_raw10")
+        load_q(1, 1, "q_then_kb")
         th_cols = keep.tile([P, Q_TILES], F32, name="th_cols")
         with nc.allow_non_contiguous_dma(reason="one threshold a partition"):
             nc.sync.dma_start(th_cols[:], th[0].rearrange("(t p) o -> p (t o)", p=P))
@@ -82,6 +83,10 @@ def tile_attend_sigscat_topk_kernel(tc, qT, k_words, k_scales, kb, th, offs, out
         maps = {0: keep.tile([P, T], F32, name="map0")}
         nc.vector.memset(maps[0][:], 0.0)
 
+        maps[1] = keep.tile([P, T], F32, name="map1", tag="q_raw00")
+        for lo in range(0, T, N):
+            nc.gpsimd.memset(maps[1][:, lo : lo + N], 0.0)
+
         listed_bytes = keep.tile([P, N], U8, name="listed_bytes", align_bytes=64)
         nc.vector.tensor_copy(listed_bytes[:], scale_pool[:].bitcast(U8).indirect(offsets[:]))
         for r in range(4):
@@ -90,14 +95,14 @@ def tile_attend_sigscat_topk_kernel(tc, qT, k_words, k_scales, kb, th, offs, out
 
         q_codes, q_scales, k_codes, word_pairs = {}, {}, {}, {}
 
-        def quantize_q(t, codes_tag):
-            rounded = keep.tile([P, PASSES, P, PACK], BF16, name=f"q_bf{t}", align_bytes=64)
+        def quantize_q(t, rounded_tag, codes_tag):
+            rounded = keep.tile([P, PASSES, P, PACK], BF16, name=f"q_bf{t}", tag=rounded_tag, align_bytes=64)
             q_codes[t] = keep.tile([P, PASSES, P], U32, name=f"q_codes{t}", tag=codes_tag, align_bytes=64)
             q_scales[t] = keep.tile([P, PASSES, P], U8, name=f"q_scales{t}", align_bytes=64)
             for g in range(PASSES):
                 nc.scalar.copy(
                     rounded[:, g].rearrange("p (c i) j -> p c j i", i=4),
-                    q_raw[t][:, g].rearrange("p j (c i) -> p c j i", i=4),
+                    q_raw[t, g][:].rearrange("p j (c i) -> p c j i", i=4),
                 )
             nc.vector.quantize_mx(
                 out=q_codes[t][:].rearrange("p g w -> p (g w)").bitcast(FP8X4),
@@ -106,36 +111,38 @@ def tile_attend_sigscat_topk_kernel(tc, qT, k_words, k_scales, kb, th, offs, out
             )
 
         def gather_words(h):
-            word_pairs[h] = keep.tile([P, HALF], U32, name=f"word_pairs{h}", tag="words_then_map")
+            word_pairs[h] = keep.tile([P, HALF], U32, name=f"word_pairs{h}", tag="word_pairs")
             nc.vector.tensor_copy(word_pairs[h][:], word_pool[:].bitcast(U32).indirect(half_list(h)))
 
-        def part_words(h):
-            k_codes[h] = keep.tile([P, PASSES, HALF], U16, name=f"k_codes{h}", align_bytes=64)
+        def part_words(h, chunks):
+            lo, hi = chunks[0] * P - h * HALF, (chunks[-1] + 1) * P - h * HALF
+            parted = keep.tile([P, PASSES, hi - lo], U16, name=f"k_codes{chunks[0]}", align_bytes=64)
             nc.vector.tensor_copy(
-                k_codes[h][:], word_pairs[h][:].bitcast(U16).rearrange("p (n g) -> p g n", g=PASSES)
+                parted[:], word_pairs[h][:, lo:hi].bitcast(U16).rearrange("p (n g) -> p g n", g=PASSES)
             )
+            for i, c in enumerate(chunks):
+                k_codes[c] = parted[:, :, i * P : (i + 1) * P]
 
-        def score(t, h, sums_bank, turned_bank, gates):
-            sums = psum.tile([P, CHUNKS, BANK], F32, name=f"sums{t}{h}", offset=sums_bank * BANK_BYTES)
-            biased = keep.tile([P, CHUNKS, P], F32, name=f"biased{t}{h}")
+        def score(t, chunks, sums_bank, turned_bank, gates):
+            name = f"{t}{chunks[0]}"
+            sums = psum.tile([P, len(chunks), BANK], F32, name=f"sums{name}", offset=sums_bank * BANK_BYTES)
+            biased = keep.tile([P, len(chunks), P], F32, name=f"biased{name}")
             for g in range(PASSES):
-                for c in range(CHUNKS):
-                    slot = h * HALF + c * P
+                for i, c in enumerate(chunks):
                     nc.tensor.matmul_mx(
-                        out=sums[:, c, :P],
-                        lhsT=k_codes[h][:, g, c * P : (c + 1) * P].bitcast(FP4X4),
-                        lhsT_scale=k_planes[g][:, slot : slot + P],
+                        out=sums[:, i, :P],
+                        lhsT=k_codes[c][:, g, :].bitcast(FP4X4),
+                        lhsT_scale=k_planes[g][:, c * P : (c + 1) * P],
                         rhs=q_codes[t][:, g, :].bitcast(FP8X4),
                         rhs_scale=q_scales[t][:, g, :],
                         start=(g == 0),
                         stop=(g == PASSES - 1),
                     )
-            for c in range(CHUNKS):
-                column = h * CHUNKS + c
-                nc.scalar.activation(biased[:, c, :], sums[:, c, :P], ACT.Identity, bias=kb_cols[:, column : column + 1])
-            turned = psum.tile([P, CHUNKS, P], F32, name=f"turned{t}{h}", offset=turned_bank * BANK_BYTES)
-            for c in range(CHUNKS):
-                nc.tensor.transpose(turned[:, c, :], biased[:, c, :], ident[:])
+            for i, c in enumerate(chunks):
+                nc.scalar.activation(biased[:, i, :], sums[:, i, :P], ACT.Identity, bias=kb_cols[:, c : c + 1])
+            turned = psum.tile([P, len(chunks), P], F32, name=f"turned{name}", offset=turned_bank * BANK_BYTES)
+            for i in range(len(chunks)):
+                nc.tensor.transpose(turned[:, i, :], biased[:, i, :], ident[:])
             nc.scalar.activation(
                 gates, turned[:].rearrange("p c s -> p (c s)"), ACT.Sigmoid, bias=neg_th[:, t : t + 1]
             )
@@ -148,26 +155,28 @@ def tile_attend_sigscat_topk_kernel(tc, qT, k_words, k_scales, kb, th, offs, out
         kb_turned = psum.tile([P, N // P, P], F32, name="kb_turned", offset=7 * BANK_BYTES)
         for c in range(N // P):
             nc.tensor.transpose(kb_turned[:, c, :], kb_listed[:, c * P : (c + 1) * P], ident[:])
-        quantize_q(0, "kb_then_codes")
+        quantize_q(0, "q_bf0", "kb_then_codes")
         gather_words(0)
-        part_words(0)
+        part_words(0, (0,))
+        part_words(0, (1,))
         gather_words(1)
-        part_words(1)
-        quantize_q(1, "q_codes1")
+        part_words(1, (2, 3))
+        quantize_q(1, "first_gates1", "q_codes1")
         kb_cols = keep.tile([P, N // P], F32, name="kb_cols", tag="q_then_kb")
         nc.scalar.copy(kb_cols[:], kb_turned[:, :, KB_ROW])
         neg_th = keep.tile([P, Q_TILES], F32, name="neg_th")
         nc.scalar.activation(neg_th[:], th_cols[:], ACT.Copy, scale=-1.0)
-        maps[1] = keep.tile([P, T], F32, name="map1", tag="words_then_map")
-        nc.vector.memset(maps[1][:], 0.0)
-        first_gates = keep.tile([P, HALF], F32, name="first_gates")
+        first_gates = [keep.tile([P, P], F32, name=f"first_gates{c}", tag=f"first_gates{c}", align_bytes=64) for c in range(CHUNKS)]
         second_gates = keep.tile([P, HALF], F32, name="second_gates")
         last_gates = keep.tile([P, N], F32, name="last_gates")
-        score(0, 0, 0, 3, first_gates[:])
-        score(0, 1, 1, 7, second_gates[:])
-        score(1, 0, 3, 5, last_gates[:, :HALF])
-        score(1, 1, 0, 6, last_gates[:, HALF:])
-        nc.vector.tensor_copy(maps[0][:].indirect(half_list(0)), first_gates[:])
+        score(0, (0,), 0, 2, first_gates[0][:])
+        score(0, (1,), 1, 3, first_gates[1][:])
+        score(0, (2, 3), 0, 7, second_gates[:])
+        score(1, (0, 1), 3, 5, last_gates[:, :HALF])
+        score(1, (2, 3), 0, 6, last_gates[:, HALF:])
+        for c in range(CHUNKS):
+            chunk_list = offsets[:, c * P // 16 : (c + 1) * P // 16]
+            nc.vector.tensor_tensor(maps[0][:].indirect(chunk_list), first_gates[c][:], maps[1][:, :P], ADD)
         nc.vector.tensor_copy(maps[0][:].indirect(half_list(1)), second_gates[:])
         store(0, nc.sync, 0, T)
         nc.vector.tensor_copy(maps[1][:].indirect(offsets[:]), last_gates[:])

@@ -25,7 +25,7 @@ HALF = N // HALVES
 CHUNKS = HALF // P
 BANK = 512
 BANK_BYTES = 4 * BANK
-KB_ROW = 16
+KB_ROW = P - 1
 SHIFT = 16
 FLOPS = 2 * NQ * N * D
 
@@ -37,55 +37,72 @@ def tile_attend_sigscat_topk_kernel(tc, qT, k_words, k_scales, kb, th, offs, out
         keep = ctx.enter_context(tc.tile_pool(name="keep", bufs=1))
         psum = ctx.enter_context(tc.psum_pool(name="psum", bufs=1))
 
+        def bank(name, shape, b):
+            return psum.tile(shape, F32, name=name, offset=b * BANK_BYTES)
+
         offsets = lists.tile([P, N // 16], U16, name="offsets")
         nc.sync.dma_start(offsets[:], offs)
 
-        def half_list(h):
-            return offsets[:, h * HALF // 16 : (h + 1) * HALF // 16]
+        def part_list(lo, hi):
+            return offsets[:, lo // 16 : hi // 16]
 
-        q_raw = {}
-
-        def load_q(t, g, tag):
-            q_raw[t, g] = keep.tile([P, PACK, P], F32, name=f"q_raw{t}{g}", tag=tag)
-            rows = qT[0, g * K_PASS : (g + 1) * K_PASS, t * P : (t + 1) * P]
-            nc.sync.dma_start(q_raw[t, g][:], rows.rearrange("(p j) w -> p j w", j=PACK))
-
-        load_q(0, 0, "q_raw00")
+        kb_pool = keep.tile([P, T], F32, name="kb_pool")
+        nc.sync.dma_start(kb_pool[KB_ROW : KB_ROW + 1, :], kb[0:1, :])
+        th_rows = keep.tile([P, P], F32, name="th_rows")
+        nc.sync.dma_start(th_rows[P - Q_TILES :, :], th[0].rearrange("(t p) o -> t (p o)", p=P))
 
         scale_pool = keep.tile([P, T // 4], I32, name="scale_pool")
         nc.vector.memset(scale_pool[:], 0)
         scale_rows = k_scales.bitcast(I32).rearrange("o (u r) t -> r u o t", r=4)
         for r in range(4):
             nc.sync.dma_start(scale_pool[r:P:SHIFT, :], scale_rows[r])
-        load_q(0, 1, "q_raw01")
-
-        kb_pool = keep.tile([P, T], F32, name="kb_pool", tag="kb_then_codes", align_bytes=64)
-        nc.vector.memset(kb_pool[:], 0.0)
-        nc.sync.dma_start(kb_pool[KB_ROW : KB_ROW + 1, :], kb[0:1, :])
 
         word_pool = keep.tile([P, T], I32, name="word_pool")
         nc.sync.dma_start(word_pool[:], k_words[0].rearrange("p t b -> p (t b)").bitcast(I32))
-        load_q(1, 0, "q_raw10")
-        load_q(1, 1, "q_then_kb")
-        th_cols = keep.tile([P, Q_TILES], F32, name="th_cols")
-        with nc.allow_non_contiguous_dma(reason="one threshold a partition"):
-            nc.sync.dma_start(th_cols[:], th[0].rearrange("(t p) o -> p (t o)", p=P))
-
-        warm_in = keep.tile([P, 1], F32, name="warm_in", tag="warm_then_ident")
-        warm_out = keep.tile([P, 1], F32, name="warm_out")
-        nc.gpsimd.memset(warm_in[:], 0.0)
-        nc.scalar.activation(warm_out[:], warm_in[:], ACT.Sigmoid)
-        ident = keep.tile([P, P], F32, name="ident", tag="warm_then_ident")
-        make_identity(nc, ident[:])
+        q_raw = [keep.tile([P, PACK, NQ], F32, name=f"q_raw{g}") for g in range(PASSES)]
+        for g in range(PASSES):
+            nc.sync.dma_start(q_raw[g][:], qT[0, g * K_PASS : (g + 1) * K_PASS, :].rearrange("(p j) w -> p j w", j=PACK))
 
         shifted_bytes = keep.tile([P, N // 4], I32, name="shifted_bytes", align_bytes=64)
         nc.vector.memset(shifted_bytes[:], 0)
-        maps = {0: keep.tile([P, T], F32, name="map0")}
-        nc.vector.memset(maps[0][:], 0.0)
+        nc.vector.memset(th_rows[: P - Q_TILES, :], 0.0)
+        nc.vector.memset(kb_pool[:KB_ROW, :], 0.0)
 
-        maps[1] = keep.tile([P, T], F32, name="map1", tag="q_raw00")
+        warm_in = keep.tile([P, 1], F32, name="warm_in")
+        warm_out = keep.tile([P, 1], F32, name="warm_out", tag="warm_then_map")
+        nc.gpsimd.memset(warm_in[:], 0.0)
+        nc.scalar.activation(warm_out[:], warm_in[:], ACT.Sigmoid)
+        ident = keep.tile([P, P], F32, name="ident")
+        make_identity(nc, ident[:])
+
+        maps = {
+            0: keep.tile([P, T], F32, name="map0"),
+            1: keep.tile([P, T], F32, name="map1", tag="warm_then_map"),
+        }
+        nc.vector.memset(maps[0][:], 0.0)
         for lo in range(0, T, N):
             nc.gpsimd.memset(maps[1][:, lo : lo + N], 0.0)
+
+        kb_cols, kb_rows = {}, {}
+
+        def bias_half(h, listed):
+            nc.vector.tensor_copy(listed[:], kb_pool[:].indirect(part_list(h * HALF, (h + 1) * HALF)))
+            turned = bank(f"kb_turned{h}", [P, CHUNKS, P], 4 + 2 * h)
+            for i in range(CHUNKS):
+                nc.tensor.transpose(turned[:, i, :], listed[:, i * P : (i + 1) * P], ident[:])
+            cols = keep.tile([P, CHUNKS], F32, name=f"kb_cols{h}")
+            nc.scalar.copy(cols[:], turned[:, :, KB_ROW])
+            spread = bank(f"kb_spread{h}", [P, CHUNKS, P], 5 + 2 * h)
+            for i in range(CHUNKS):
+                nc.tensor.transpose(spread[:, i, :], cols[:, i : i + 1].to_broadcast([P, P]), ident[:])
+            rows = keep.tile([P, CHUNKS, P], F32, name=f"kb_rows{h}")
+            nc.scalar.copy(rows[:], spread[:])
+            for i in range(CHUNKS):
+                kb_cols[h * CHUNKS + i] = cols[:, i : i + 1]
+                kb_rows[h * CHUNKS + i] = rows[:, i, :]
+
+        for h in range(HALVES):
+            bias_half(h, keep.tile([P, HALF], F32, name=f"kb_listed{h}"))
 
         listed_bytes = keep.tile([P, N], U8, name="listed_bytes", align_bytes=64)
         nc.vector.tensor_copy(listed_bytes[:], scale_pool[:].bitcast(U8).indirect(offsets[:]))
@@ -95,52 +112,67 @@ def tile_attend_sigscat_topk_kernel(tc, qT, k_words, k_scales, kb, th, offs, out
 
         q_codes, q_scales, k_codes, word_pairs = {}, {}, {}, {}
 
-        def quantize_q(t, rounded_tag, codes_tag):
-            rounded = keep.tile([P, PASSES, P, PACK], BF16, name=f"q_bf{t}", tag=rounded_tag, align_bytes=64)
-            q_codes[t] = keep.tile([P, PASSES, P], U32, name=f"q_codes{t}", tag=codes_tag, align_bytes=64)
-            q_scales[t] = keep.tile([P, PASSES, P], U8, name=f"q_scales{t}", align_bytes=64)
-            for g in range(PASSES):
-                nc.scalar.copy(
-                    rounded[:, g].rearrange("p (c i) j -> p c j i", i=4),
-                    q_raw[t, g][:].rearrange("p j (c i) -> p c j i", i=4),
+        def quantize_q(t, g, on_scalar, rounded_tag, codes_tag):
+            rounded = keep.tile([P, P, PACK], BF16, name=f"q_bf{t}{g}", tag=rounded_tag, align_bytes=64)
+            codes = keep.tile([P, P], U32, name=f"q_codes{t}{g}", tag=codes_tag, align_bytes=64)
+            scales = keep.tile([P, P], U8, name=f"q_scales{t}{g}", align_bytes=64)
+            raw = q_raw[g][:, :, t * P : (t + 1) * P]
+            nc.scalar.copy(
+                rounded[:, :on_scalar].rearrange("p (c i) j -> p c j i", i=4),
+                raw[:, :, :on_scalar].rearrange("p j (c i) -> p c j i", i=4),
+            )
+            if on_scalar < P:
+                nc.vector.tensor_copy(
+                    rounded[:, on_scalar:].rearrange("p (c i) j -> p c j i", i=4),
+                    raw[:, :, on_scalar:].rearrange("p j (c i) -> p c j i", i=4),
                 )
             nc.vector.quantize_mx(
-                out=q_codes[t][:].rearrange("p g w -> p (g w)").bitcast(FP8X4),
-                scales=q_scales[t][:].rearrange("p g w -> p (g w)"),
-                in_=rounded[:].rearrange("p g w j -> p (g w j)"),
+                out=codes[:].bitcast(FP8X4), scales=scales[:], in_=rounded[:].rearrange("p w j -> p (w j)")
             )
+            q_codes[t, g], q_scales[t, g] = codes[:].bitcast(FP8X4), scales[:]
 
         def gather_words(h):
-            word_pairs[h] = keep.tile([P, HALF], U32, name=f"word_pairs{h}", tag="word_pairs")
-            nc.vector.tensor_copy(word_pairs[h][:], word_pool[:].bitcast(U32).indirect(half_list(h)))
+            word_pairs[h] = keep.tile([P, HALF], U32, name=f"word_pairs{h}", tag=f"words_then_q0{h}", align_bytes=64)
+            nc.vector.tensor_copy(word_pairs[h][:], word_pool[:].bitcast(U32).indirect(part_list(h * HALF, (h + 1) * HALF)))
 
-        def part_words(h, chunks):
-            lo, hi = chunks[0] * P - h * HALF, (chunks[-1] + 1) * P - h * HALF
-            parted = keep.tile([P, PASSES, hi - lo], U16, name=f"k_codes{chunks[0]}", align_bytes=64)
-            nc.vector.tensor_copy(
-                parted[:], word_pairs[h][:, lo:hi].bitcast(U16).rearrange("p (n g) -> p g n", g=PASSES)
-            )
-            for i, c in enumerate(chunks):
-                k_codes[c] = parted[:, :, i * P : (i + 1) * P]
+        def part_words(h):
+            parted = keep.tile([P, PASSES, HALF], U16, name=f"k_codes{h}", align_bytes=64)
+            nc.vector.tensor_copy(parted[:], word_pairs[h][:].bitcast(U16).rearrange("p (n g) -> p g n", g=PASSES))
+            for i in range(CHUNKS):
+                for g in range(PASSES):
+                    k_codes[h * CHUNKS + i, g] = parted[:, g, i * P : (i + 1) * P].bitcast(FP4X4)
 
-        def score(t, chunks, sums_bank, turned_bank, gates):
-            name = f"{t}{chunks[0]}"
-            sums = psum.tile([P, len(chunks), BANK], F32, name=f"sums{name}", offset=sums_bank * BANK_BYTES)
-            biased = keep.tile([P, len(chunks), P], F32, name=f"biased{name}")
+        def score_by_rows(t, c, b, biased):
+            sums = bank(f"row_sums{c}", [P, P], b)
             for g in range(PASSES):
-                for i, c in enumerate(chunks):
+                nc.tensor.matmul_mx(
+                    out=sums[:],
+                    lhsT=q_codes[t, g],
+                    lhsT_scale=q_scales[t, g],
+                    rhs=k_codes[c, g],
+                    rhs_scale=k_planes[g][:, c * P : (c + 1) * P],
+                    start=(g == 0),
+                    stop=(g == PASSES - 1),
+                )
+            nc.vector.tensor_tensor(biased, sums[:], kb_rows[c], ADD)
+
+        def score(t, chunks, sums_banks, turned_bank, gates):
+            name = f"{t}{chunks[0]}"
+            biased = keep.tile([P, len(chunks), P], F32, name=f"biased{name}")
+            for i, c in enumerate(chunks):
+                sums = bank(f"sums{t}{c}", [P, P], sums_banks[i])
+                for g in range(PASSES):
                     nc.tensor.matmul_mx(
-                        out=sums[:, i, :P],
-                        lhsT=k_codes[c][:, g, :].bitcast(FP4X4),
+                        out=sums[:],
+                        lhsT=k_codes[c, g],
                         lhsT_scale=k_planes[g][:, c * P : (c + 1) * P],
-                        rhs=q_codes[t][:, g, :].bitcast(FP8X4),
-                        rhs_scale=q_scales[t][:, g, :],
+                        rhs=q_codes[t, g],
+                        rhs_scale=q_scales[t, g],
                         start=(g == 0),
                         stop=(g == PASSES - 1),
                     )
-            for i, c in enumerate(chunks):
-                nc.scalar.activation(biased[:, i, :], sums[:, i, :P], ACT.Identity, bias=kb_cols[:, c : c + 1])
-            turned = psum.tile([P, len(chunks), P], F32, name=f"turned{name}", offset=turned_bank * BANK_BYTES)
+                nc.scalar.activation(biased[:, i, :], sums[:], ACT.Identity, bias=kb_cols[c])
+            turned = bank(f"turned{name}", [P, len(chunks), P], turned_bank)
             for i in range(len(chunks)):
                 nc.tensor.transpose(turned[:, i, :], biased[:, i, :], ident[:])
             nc.scalar.activation(
@@ -150,35 +182,34 @@ def tile_attend_sigscat_topk_kernel(tc, qT, k_words, k_scales, kb, th, offs, out
         def store(t, queue, lo, hi):
             queue.dma_start(out[0, t * P : (t + 1) * P, lo:hi], maps[t][:, lo:hi])
 
-        kb_listed = keep.tile([P, N], F32, name="kb_listed")
-        nc.vector.tensor_copy(kb_listed[:], kb_pool[:].indirect(offsets[:]))
-        kb_turned = psum.tile([P, N // P, P], F32, name="kb_turned", offset=7 * BANK_BYTES)
-        for c in range(N // P):
-            nc.tensor.transpose(kb_turned[:, c, :], kb_listed[:, c * P : (c + 1) * P], ident[:])
-        quantize_q(0, "q_bf0", "kb_then_codes")
         gather_words(0)
-        part_words(0, (0,))
-        part_words(0, (1,))
         gather_words(1)
-        part_words(1, (2, 3))
-        quantize_q(1, "first_gates1", "q_codes1")
-        kb_cols = keep.tile([P, N // P], F32, name="kb_cols", tag="q_then_kb")
-        nc.scalar.copy(kb_cols[:], kb_turned[:, :, KB_ROW])
+        part_words(0)
+        quantize_q(0, 0, P, "q_bf00", "words_then_q00")
+        part_words(1)
+        quantize_q(0, 1, 48, "words_then_q01", "q_codes01")
+        th_turned = bank("th_turned", [P, P], 4)
+        nc.tensor.transpose(th_turned[:], th_rows[:], ident[:])
         neg_th = keep.tile([P, Q_TILES], F32, name="neg_th")
-        nc.scalar.activation(neg_th[:], th_cols[:], ACT.Copy, scale=-1.0)
-        first_gates = [keep.tile([P, P], F32, name=f"first_gates{c}", tag=f"first_gates{c}", align_bytes=64) for c in range(CHUNKS)]
-        second_gates = keep.tile([P, HALF], F32, name="second_gates")
-        last_gates = keep.tile([P, N], F32, name="last_gates")
-        score(0, (0,), 0, 2, first_gates[0][:])
-        score(0, (1,), 1, 3, first_gates[1][:])
-        score(0, (2, 3), 0, 7, second_gates[:])
-        score(1, (0, 1), 3, 5, last_gates[:, :HALF])
-        score(1, (2, 3), 0, 6, last_gates[:, HALF:])
-        for c in range(CHUNKS):
-            chunk_list = offsets[:, c * P // 16 : (c + 1) * P // 16]
-            nc.vector.tensor_tensor(maps[0][:].indirect(chunk_list), first_gates[c][:], maps[1][:, :P], ADD)
-        nc.vector.tensor_copy(maps[0][:].indirect(half_list(1)), second_gates[:])
+        nc.scalar.activation(neg_th[:], th_turned[:, P - Q_TILES :], ACT.Copy, scale=-1.0)
+
+        first_biased = keep.tile([P, P], F32, name="first_biased")
+        rest_biased = keep.tile([P, N - P], F32, name="rest_biased")
+        first_gates = keep.tile([P, P], F32, name="first_gates")
+        rest_gates = keep.tile([P, N - P], F32, name="rest_gates")
+        score_by_rows(0, 0, 0, first_biased[:])
+        for c in range(1, N // P):
+            score_by_rows(0, c, c, rest_biased[:, (c - 1) * P : c * P])
+        quantize_q(1, 0, P, "q_bf10", "words_then_q01")
+        quantize_q(1, 1, P, "q_bf11", "q_codes11")
+        nc.scalar.activation(first_gates[:], first_biased[:], ACT.Sigmoid, bias=neg_th[:, 0:1])
+        nc.scalar.activation(rest_gates[:], rest_biased[:], ACT.Sigmoid, bias=neg_th[:, 0:1])
+        nc.vector.tensor_tensor(maps[0][:].indirect(part_list(0, P)), first_gates[:], maps[1][:, :P], ADD)
+        nc.vector.tensor_copy(maps[0][:].indirect(part_list(P, N)), rest_gates[:])
         store(0, nc.sync, 0, T)
+        last_gates = keep.tile([P, N], F32, name="last_gates")
+        score(1, (0, 1), (0, 1), 4, last_gates[:, :HALF])
+        score(1, (2, 3), (2, 3), 5, last_gates[:, HALF:])
         nc.vector.tensor_copy(maps[1][:].indirect(offsets[:]), last_gates[:])
         store(1, nc.sync, 0, T // 2)
         store(1, nc.scalar, T // 2, T)

@@ -26,7 +26,7 @@ CHUNKS = HALF // P
 BANK = 512
 BANK_BYTES = 4 * BANK
 KB_ROW = P - 1
-SHIFT = 16
+SCALE_ROW = P - 32
 FLOPS = 2 * NQ * N * D
 
 
@@ -46,25 +46,28 @@ def tile_attend_sigscat_topk_kernel(tc, qT, k_words, k_scales, kb, th, offs, out
         def part_list(lo, hi):
             return offsets[:, lo // 16 : hi // 16]
 
+        scale_pool = keep.tile([P, T // 4], I32, name="scale_pool", tag="scales_then_q")
+        nc.sync.dma_start(scale_pool[SCALE_ROW:, :], k_scales.bitcast(I32).rearrange("o f t -> (o f) t"))
+        nc.vector.memset(scale_pool[:SCALE_ROW, :], 0)
+
         kb_pool = keep.tile([P, T], F32, name="kb_pool")
         nc.sync.dma_start(kb_pool[KB_ROW : KB_ROW + 1, :], kb[0:1, :])
         th_rows = keep.tile([P, P], F32, name="th_rows")
         nc.sync.dma_start(th_rows[P - Q_TILES :, :], th[0].rearrange("(t p) o -> t (p o)", p=P))
 
-        scale_pool = keep.tile([P, T // 4], I32, name="scale_pool")
-        nc.vector.memset(scale_pool[:], 0)
-        scale_rows = k_scales.bitcast(I32).rearrange("o (u r) t -> r u o t", r=4)
-        for r in range(4):
-            nc.sync.dma_start(scale_pool[r:P:SHIFT, :], scale_rows[r])
-
         word_pool = keep.tile([P, T], I32, name="word_pool")
         nc.sync.dma_start(word_pool[:], k_words[0].rearrange("p t b -> p (t b)").bitcast(I32))
-        q_raw = [keep.tile([P, PACK, NQ], F32, name=f"q_raw{g}") for g in range(PASSES)]
-        for g in range(PASSES):
+        q_raw = {}
+
+        def load_q(g, tag):
+            q_raw[g] = keep.tile([P, PACK, NQ], F32, name=f"q_raw{g}", tag=tag)
             nc.sync.dma_start(q_raw[g][:], qT[0, g * K_PASS : (g + 1) * K_PASS, :].rearrange("(p j) w -> p j w", j=PACK))
 
-        shifted_bytes = keep.tile([P, N // 4], I32, name="shifted_bytes", align_bytes=64)
-        nc.vector.memset(shifted_bytes[:], 0)
+        load_q(0, "q_raw0")
+
+        planes = [keep.tile([P, N // 4], I32, name=f"plane{g}", align_bytes=64) for g in range(PASSES)]
+        for g in range(PASSES):
+            nc.vector.memset(planes[g][:], 0)
         nc.vector.memset(th_rows[: P - Q_TILES, :], 0.0)
         nc.vector.memset(kb_pool[:KB_ROW, :], 0.0)
 
@@ -79,9 +82,23 @@ def tile_attend_sigscat_topk_kernel(tc, qT, k_words, k_scales, kb, th, offs, out
             0: keep.tile([P, T], F32, name="map0"),
             1: keep.tile([P, T], F32, name="map1", tag="warm_then_map"),
         }
-        nc.vector.memset(maps[0][:], 0.0)
+        nc.vector.memset(maps[0][:, : T // 2 + 8], 0.0)
         for lo in range(0, T, N):
             nc.gpsimd.memset(maps[1][:, lo : lo + N], 0.0)
+        nc.gpsimd.memset(maps[0][:, T // 2 :], 0.0)
+
+        listed_bytes = keep.tile([P, N], U8, name="listed_bytes")
+        nc.vector.tensor_copy(listed_bytes[:], scale_pool[:].bitcast(U8).indirect(offsets[:]))
+
+        def move_plane(g):
+            first = SCALE_ROW + 16 * g
+            for r in range(4):
+                nc.sync.dma_start(planes[g][r:P:32, :], listed_bytes[:].bitcast(I32)[first + r : first + 16 : 4, :])
+
+        move_plane(0)
+        load_q(1, "scales_then_q")
+        move_plane(1)
+        k_planes = [plane[:].bitcast(U8) for plane in planes]
 
         kb_cols, kb_rows = {}, {}
 
@@ -102,13 +119,7 @@ def tile_attend_sigscat_topk_kernel(tc, qT, k_words, k_scales, kb, th, offs, out
                 kb_rows[h * CHUNKS + i] = rows[:, i, :]
 
         for h in range(HALVES):
-            bias_half(h, keep.tile([P, HALF], F32, name=f"kb_listed{h}"))
-
-        listed_bytes = keep.tile([P, N], U8, name="listed_bytes", align_bytes=64)
-        nc.vector.tensor_copy(listed_bytes[:], scale_pool[:].bitcast(U8).indirect(offsets[:]))
-        for r in range(4):
-            nc.sync.dma_start(shifted_bytes[r:P:32, :], listed_bytes[:].bitcast(I32)[SHIFT + r : P : 32, :])
-        k_planes = (listed_bytes[:], shifted_bytes[:].bitcast(U8))
+            bias_half(h, keep.tile([P, HALF], F32, name=f"kb_listed{h}", tag=f"kb_then_q{h}", align_bytes=64))
 
         q_codes, q_scales, k_codes, word_pairs = {}, {}, {}, {}
 
@@ -117,10 +128,11 @@ def tile_attend_sigscat_topk_kernel(tc, qT, k_words, k_scales, kb, th, offs, out
             codes = keep.tile([P, P], U32, name=f"q_codes{t}{g}", tag=codes_tag, align_bytes=64)
             scales = keep.tile([P, P], U8, name=f"q_scales{t}{g}", align_bytes=64)
             raw = q_raw[g][:, :, t * P : (t + 1) * P]
-            nc.scalar.copy(
-                rounded[:, :on_scalar].rearrange("p (c i) j -> p c j i", i=4),
-                raw[:, :, :on_scalar].rearrange("p j (c i) -> p c j i", i=4),
-            )
+            if on_scalar > 0:
+                nc.scalar.copy(
+                    rounded[:, :on_scalar].rearrange("p (c i) j -> p c j i", i=4),
+                    raw[:, :, :on_scalar].rearrange("p j (c i) -> p c j i", i=4),
+                )
             if on_scalar < P:
                 nc.vector.tensor_copy(
                     rounded[:, on_scalar:].rearrange("p (c i) j -> p c j i", i=4),
@@ -185,9 +197,9 @@ def tile_attend_sigscat_topk_kernel(tc, qT, k_words, k_scales, kb, th, offs, out
         gather_words(0)
         gather_words(1)
         part_words(0)
-        quantize_q(0, 0, P, "q_bf00", "words_then_q00")
+        quantize_q(0, 0, P, "kb_then_q1", "words_then_q00")
         part_words(1)
-        quantize_q(0, 1, 48, "words_then_q01", "q_codes01")
+        quantize_q(0, 1, 0, "words_then_q01", "q_codes01")
         th_turned = bank("th_turned", [P, P], 4)
         nc.tensor.transpose(th_turned[:], th_rows[:], ident[:])
         neg_th = keep.tile([P, Q_TILES], F32, name="neg_th")

@@ -35,10 +35,14 @@ def tile_attend_sigscat_topk_kernel(tc, qT, k_words, k_scales, kb, th, offs, out
     with ExitStack() as ctx:
         lists = ctx.enter_context(tc.tile_pool(name="lists", bufs=1))
         keep = ctx.enter_context(tc.tile_pool(name="keep", bufs=1))
+        placed = ctx.enter_context(tc.tile_pool(name="placed", bufs=1))
         psum = ctx.enter_context(tc.psum_pool(name="psum", bufs=1))
 
         def bank(name, shape, b):
             return psum.tile(shape, F32, name=name, offset=b * BANK_BYTES)
+
+        def place(name, shape, dtype, at):
+            return placed.tile(shape, dtype, name=name, offset=at, align_bytes=64)
 
         offsets = lists.tile([P, N // 16], U16, name="offsets")
         nc.sync.dma_start(offsets[:], offs)
@@ -57,13 +61,9 @@ def tile_attend_sigscat_topk_kernel(tc, qT, k_words, k_scales, kb, th, offs, out
 
         word_pool = keep.tile([P, T], I32, name="word_pool")
         nc.sync.dma_start(word_pool[:], k_words[0].rearrange("p t b -> p (t b)").bitcast(I32))
-        q_raw = {}
-
-        def load_q(g, tag):
-            q_raw[g] = keep.tile([P, PACK, NQ], F32, name=f"q_raw{g}", tag=tag)
-            nc.sync.dma_start(q_raw[g][:], qT[0, g * K_PASS : (g + 1) * K_PASS, :].rearrange("(p j) w -> p j w", j=PACK))
-
-        load_q(0, "q_raw0")
+        q_rows = qT[0].rearrange("(g p j) w -> g p j w", g=PASSES, j=PACK)
+        first_pass = keep.tile([P, PACK, NQ], F32, name="first_pass")
+        nc.sync.dma_start(first_pass[:], q_rows[0])
 
         planes = [keep.tile([P, N // 4], I32, name=f"plane{g}", align_bytes=64) for g in range(PASSES)]
         for g in range(PASSES):
@@ -71,7 +71,7 @@ def tile_attend_sigscat_topk_kernel(tc, qT, k_words, k_scales, kb, th, offs, out
         nc.vector.memset(th_rows[: P - Q_TILES, :], 0.0)
         nc.vector.memset(kb_pool[:KB_ROW, :], 0.0)
 
-        warm_in = keep.tile([P, 1], F32, name="warm_in")
+        warm_in = keep.tile([P, 1], F32, name="warm_in", tag="warm_then_map0")
         warm_out = keep.tile([P, 1], F32, name="warm_out", tag="warm_then_map")
         nc.gpsimd.memset(warm_in[:], 0.0)
         nc.scalar.activation(warm_out[:], warm_in[:], ACT.Sigmoid)
@@ -79,13 +79,12 @@ def tile_attend_sigscat_topk_kernel(tc, qT, k_words, k_scales, kb, th, offs, out
         make_identity(nc, ident[:])
 
         maps = {
-            0: keep.tile([P, T], F32, name="map0"),
+            0: keep.tile([P, T], F32, name="map0", tag="warm_then_map0"),
             1: keep.tile([P, T], F32, name="map1", tag="warm_then_map"),
         }
-        nc.vector.memset(maps[0][:, : T // 2 + 8], 0.0)
-        for lo in range(0, T, N):
-            nc.gpsimd.memset(maps[1][:, lo : lo + N], 0.0)
-        nc.gpsimd.memset(maps[0][:, T // 2 :], 0.0)
+        for t in range(Q_TILES):
+            for lo in range(0, T, N):
+                nc.gpsimd.memset(maps[t][:, lo : lo + N], 0.0)
 
         listed_bytes = keep.tile([P, N], U8, name="listed_bytes")
         nc.vector.tensor_copy(listed_bytes[:], scale_pool[:].bitcast(U8).indirect(offsets[:]))
@@ -96,8 +95,13 @@ def tile_attend_sigscat_topk_kernel(tc, qT, k_words, k_scales, kb, th, offs, out
                 nc.sync.dma_start(planes[g][r:P:32, :], listed_bytes[:].bitcast(I32)[first + r : first + 16 : 4, :])
 
         move_plane(0)
-        load_q(1, "scales_then_q")
+        second_pass = keep.tile([P, Q_TILES, PACK, P], F32, name="second_pass", tag="scales_then_q")
+        nc.sync.dma_start(second_pass[:, 0], q_rows[1][:, :, :P])
+        nc.sync.dma_start(second_pass[:, 1], q_rows[1][:, :, P:])
         move_plane(1)
+        q_raw = {(t, 0): first_pass[:, :, t * P : (t + 1) * P] for t in range(Q_TILES)}
+        for t in range(Q_TILES):
+            q_raw[t, 1] = second_pass[:, t]
         k_planes = [plane[:].bitcast(U8) for plane in planes]
 
         kb_cols, kb_rows = {}, {}
@@ -123,11 +127,9 @@ def tile_attend_sigscat_topk_kernel(tc, qT, k_words, k_scales, kb, th, offs, out
 
         q_codes, q_scales, k_codes, word_pairs = {}, {}, {}, {}
 
-        def quantize_q(t, g, on_scalar, rounded_tag, codes_tag):
-            rounded = keep.tile([P, P, PACK], BF16, name=f"q_bf{t}{g}", tag=rounded_tag, align_bytes=64)
-            codes = keep.tile([P, P], U32, name=f"q_codes{t}{g}", tag=codes_tag, align_bytes=64)
+        def quantize_q(t, g, on_scalar, rounded, codes):
             scales = keep.tile([P, P], U8, name=f"q_scales{t}{g}", align_bytes=64)
-            raw = q_raw[g][:, :, t * P : (t + 1) * P]
+            raw = q_raw[t, g]
             if on_scalar > 0:
                 nc.scalar.copy(
                     rounded[:, :on_scalar].rearrange("p (c i) j -> p c j i", i=4),
@@ -143,8 +145,8 @@ def tile_attend_sigscat_topk_kernel(tc, qT, k_words, k_scales, kb, th, offs, out
             )
             q_codes[t, g], q_scales[t, g] = codes[:].bitcast(FP8X4), scales[:]
 
-        def gather_words(h):
-            word_pairs[h] = keep.tile([P, HALF], U32, name=f"word_pairs{h}", tag=f"words_then_q0{h}", align_bytes=64)
+        def gather_words(h, pairs):
+            word_pairs[h] = pairs
             nc.vector.tensor_copy(word_pairs[h][:], word_pool[:].bitcast(U32).indirect(part_list(h * HALF, (h + 1) * HALF)))
 
         def part_words(h):
@@ -194,12 +196,12 @@ def tile_attend_sigscat_topk_kernel(tc, qT, k_words, k_scales, kb, th, offs, out
         def store(t, queue, lo, hi):
             queue.dma_start(out[0, t * P : (t + 1) * P, lo:hi], maps[t][:, lo:hi])
 
-        gather_words(0)
-        gather_words(1)
+        gather_words(0, keep.tile([P, HALF], U32, name="word_pairs0", tag="words_then_q", align_bytes=64))
+        gather_words(1, place("word_pairs1", [P, HALF], U32, 0))
         part_words(0)
-        quantize_q(0, 0, P, "kb_then_q1", "words_then_q00")
+        quantize_q(0, 0, P, keep.tile([P, P, PACK], BF16, name="q_bf00", tag="kb_then_q0", align_bytes=64), keep.tile([P, P], U32, name="q_codes00", tag="words_then_q", align_bytes=64))
         part_words(1)
-        quantize_q(0, 1, 0, "words_then_q01", "q_codes01")
+        quantize_q(0, 1, 0, place("q_bf01", [P, P, PACK], BF16, 0), keep.tile([P, P], U32, name="q_codes01", align_bytes=64))
         th_turned = bank("th_turned", [P, P], 4)
         nc.tensor.transpose(th_turned[:], th_rows[:], ident[:])
         neg_th = keep.tile([P, Q_TILES], F32, name="neg_th")
@@ -212,8 +214,8 @@ def tile_attend_sigscat_topk_kernel(tc, qT, k_words, k_scales, kb, th, offs, out
         score_by_rows(0, 0, 0, first_biased[:])
         for c in range(1, N // P):
             score_by_rows(0, c, c, rest_biased[:, (c - 1) * P : c * P])
-        quantize_q(1, 0, P, "q_bf10", "words_then_q01")
-        quantize_q(1, 1, P, "q_bf11", "q_codes11")
+        quantize_q(1, 0, P, keep.tile([P, P, PACK], BF16, name="q_bf10", tag="kb_then_q1", align_bytes=64), place("q_codes10", [P, P], U32, 0))
+        quantize_q(1, 1, P, keep.tile([P, P, PACK], BF16, name="q_bf11", align_bytes=64), place("q_codes11", [P, P], U32, 512))
         nc.scalar.activation(first_gates[:], first_biased[:], ACT.Sigmoid, bias=neg_th[:, 0:1])
         nc.scalar.activation(rest_gates[:], rest_biased[:], ACT.Sigmoid, bias=neg_th[:, 0:1])
         nc.vector.tensor_tensor(maps[0][:].indirect(part_list(0, P)), first_gates[:], maps[1][:, :P], ADD)

@@ -22,11 +22,10 @@ PASSES = D // K_PASS
 Q_TILES = NQ // P
 HALVES = 2
 HALF = N // HALVES
-CHUNKS = HALF // P
-BANK = 512
-BANK_BYTES = 4 * BANK
+CHUNKS = N // P
+BANK_BYTES = 2048
 KB_ROW = P - 1
-SCALE_ROW = P - 32
+SCALE_ROW = P - 16
 FLOPS = 2 * NQ * N * D
 
 
@@ -50,180 +49,176 @@ def tile_attend_sigscat_topk_kernel(tc, qT, k_words, k_scales, kb, th, offs, out
         def part_list(lo, hi):
             return offsets[:, lo // 16 : hi // 16]
 
-        scale_pool = keep.tile([P, T // 4], I32, name="scale_pool", tag="scales_then_q")
-        nc.sync.dma_start(scale_pool[SCALE_ROW:, :], k_scales.bitcast(I32).rearrange("o f t -> (o f) t"))
-        nc.vector.memset(scale_pool[:SCALE_ROW, :], 0)
-
+        scale_pool = keep.tile([P, PASSES * T // 4], I32, name="scale_pool")
+        nc.sync.dma_start(
+            scale_pool[SCALE_ROW:, :].rearrange("f (o t) -> f o t", o=PASSES),
+            k_scales.bitcast(I32).rearrange("o f t -> f o t"),
+        )
         kb_pool = keep.tile([P, T], F32, name="kb_pool")
         nc.sync.dma_start(kb_pool[KB_ROW : KB_ROW + 1, :], kb[0:1, :])
         th_rows = keep.tile([P, P], F32, name="th_rows")
         nc.sync.dma_start(th_rows[P - Q_TILES :, :], th[0].rearrange("(t p) o -> t (p o)", p=P))
-
         word_pool = keep.tile([P, T], I32, name="word_pool")
         nc.sync.dma_start(word_pool[:], k_words[0].rearrange("p t b -> p (t b)").bitcast(I32))
         q_rows = qT[0].rearrange("(g p j) w -> g p j w", g=PASSES, j=PACK)
         first_pass = keep.tile([P, PACK, NQ], F32, name="first_pass")
         nc.sync.dma_start(first_pass[:], q_rows[0])
+        second_pass = keep.tile([P, Q_TILES, PACK, P], F32, name="second_pass")
+        for t in range(Q_TILES):
+            nc.sync.dma_start(second_pass[:, t], q_rows[1][:, :, t * P : (t + 1) * P])
 
-        planes = [keep.tile([P, N // 4], I32, name=f"plane{g}", align_bytes=64) for g in range(PASSES)]
-        for g in range(PASSES):
-            nc.vector.memset(planes[g][:], 0)
-        nc.vector.memset(th_rows[: P - Q_TILES, :], 0.0)
-        nc.vector.memset(kb_pool[:KB_ROW, :], 0.0)
+        def zero_on_vector(tile, rows, lo, hi):
+            nc.vector.memset(tile[:rows, lo : hi - 1], 0)
+            nc.vector.memset(tile[:rows, hi - 1 : hi], 0)
 
-        warm_in = keep.tile([P, 1], F32, name="warm_in", tag="warm_then_map0")
-        warm_out = keep.tile([P, 1], F32, name="warm_out", tag="warm_then_map")
+        warm_in = keep.tile([P, 1], F32, name="warm_in")
+        warm_out = keep.tile([P, 1], F32, name="warm_out")
         nc.gpsimd.memset(warm_in[:], 0.0)
         nc.scalar.activation(warm_out[:], warm_in[:], ACT.Sigmoid)
+
+        maps = {0: keep.tile([P, T], F32, name="map0")}
+        plane_pair = keep.tile([P, PASSES * N // 4], I32, name="planes", align_bytes=64)
+        planes = [plane_pair[:, g * N // 4 : (g + 1) * N // 4] for g in range(PASSES)]
+        zero_on_vector(kb_pool, KB_ROW, 0, T // 2)
+        zero_on_vector(scale_pool, SCALE_ROW, 0, 3 * T // 8)
+        nc.gpsimd.memset(kb_pool[:KB_ROW, T // 2 :], 0.0)
+        nc.gpsimd.memset(scale_pool[:SCALE_ROW, 3 * T // 8 :], 0)
         ident = keep.tile([P, P], F32, name="ident")
         make_identity(nc, ident[:])
+        zeros = keep.tile([P, P], F32, name="zeros")
+        nc.gpsimd.memset(zeros[:], 0.0)
+        nc.gpsimd.memset(th_rows[: P - Q_TILES, :], 0.0)
+        nc.gpsimd.memset(plane_pair[:], 0)
+        nc.gpsimd.memset(maps[0][:], 0.0)
 
-        maps = {
-            0: keep.tile([P, T], F32, name="map0", tag="warm_then_map0"),
-            1: keep.tile([P, T], F32, name="map1", tag="warm_then_map"),
-        }
-        for t in range(Q_TILES):
-            for lo in range(0, T, N):
-                nc.gpsimd.memset(maps[t][:, lo : lo + N], 0.0)
+        listed_bytes = keep.tile([P, PASSES * N], U8, name="listed_bytes")
+        for g in range(PASSES):
+            window = scale_pool[:].bitcast(U8)[:, g * T : (g + 1) * T]
+            nc.vector.tensor_copy(listed_bytes[:, g * N : (g + 1) * N], window.indirect(offsets[:]))
+        for r in range(4):
+            nc.sync.dma_start(plane_pair[r:P:32, :], listed_bytes[:].bitcast(I32)[SCALE_ROW + r : P : 4, :])
 
-        listed_bytes = keep.tile([P, N], U8, name="listed_bytes")
-        nc.vector.tensor_copy(listed_bytes[:], scale_pool[:].bitcast(U8).indirect(offsets[:]))
-
-        def move_plane(g):
-            first = SCALE_ROW + 16 * g
-            for r in range(4):
-                nc.sync.dma_start(planes[g][r:P:32, :], listed_bytes[:].bitcast(I32)[first + r : first + 16 : 4, :])
-
-        move_plane(0)
-        second_pass = keep.tile([P, Q_TILES, PACK, P], F32, name="second_pass", tag="scales_then_q")
-        nc.sync.dma_start(second_pass[:, 0], q_rows[1][:, :, :P])
-        nc.sync.dma_start(second_pass[:, 1], q_rows[1][:, :, P:])
-        move_plane(1)
         q_raw = {(t, 0): first_pass[:, :, t * P : (t + 1) * P] for t in range(Q_TILES)}
         for t in range(Q_TILES):
             q_raw[t, 1] = second_pass[:, t]
-        k_planes = [plane[:].bitcast(U8) for plane in planes]
+        k_planes = [plane.bitcast(U8) for plane in planes]
 
-        kb_cols, kb_rows = {}, {}
-
-        def bias_half(h, listed):
-            nc.vector.tensor_copy(listed[:], kb_pool[:].indirect(part_list(h * HALF, (h + 1) * HALF)))
-            turned = bank(f"kb_turned{h}", [P, CHUNKS, P], 4 + 2 * h)
-            for i in range(CHUNKS):
-                nc.tensor.transpose(turned[:, i, :], listed[:, i * P : (i + 1) * P], ident[:])
-            cols = keep.tile([P, CHUNKS], F32, name=f"kb_cols{h}")
-            nc.scalar.copy(cols[:], turned[:, :, KB_ROW])
-            spread = bank(f"kb_spread{h}", [P, CHUNKS, P], 5 + 2 * h)
-            for i in range(CHUNKS):
-                nc.tensor.transpose(spread[:, i, :], cols[:, i : i + 1].to_broadcast([P, P]), ident[:])
-            rows = keep.tile([P, CHUNKS, P], F32, name=f"kb_rows{h}")
-            nc.scalar.copy(rows[:], spread[:])
-            for i in range(CHUNKS):
-                kb_cols[h * CHUNKS + i] = cols[:, i : i + 1]
-                kb_rows[h * CHUNKS + i] = rows[:, i, :]
-
+        kb_listed = place("kb_listed", [P, N], F32, 512)
+        kb_cols = keep.tile([P, CHUNKS], F32, name="kb_cols")
+        kb_rows = keep.tile([P, N], F32, name="kb_rows")
         for h in range(HALVES):
-            bias_half(h, keep.tile([P, HALF], F32, name=f"kb_listed{h}", tag=f"kb_then_q{h}", align_bytes=64))
+            cols = slice(h * HALF, (h + 1) * HALF)
+            nc.scalar.activation(kb_listed[:, cols], kb_pool[:].indirect(part_list(cols.start, cols.stop)), ACT.Copy)
+        for h in range(HALVES):
+            turned = bank(f"kb_turned{h}", [P, 2, P], 4 + h)
+            for i in range(2):
+                c = 2 * h + i
+                nc.tensor.transpose(turned[:, i, :], kb_listed[:, c * P : (c + 1) * P], ident[:])
+            nc.scalar.copy(kb_cols[:, 2 * h : 2 * h + 2], turned[:, :, KB_ROW])
+        for h in range(HALVES):
+            spread = bank(f"kb_spread{h}", [P, 2, P], 6 + h)
+            for i in range(2):
+                c = 2 * h + i
+                nc.tensor.transpose(spread[:, i, :], kb_cols[:, c : c + 1].to_broadcast([P, P]), ident[:])
+            nc.scalar.copy(kb_rows[:, h * HALF : (h + 1) * HALF], spread[:].rearrange("p c s -> p (c s)"))
 
-        q_codes, q_scales, k_codes, word_pairs = {}, {}, {}, {}
+        q_codes, q_scales, k_parted, word_pairs = {}, {}, {}, {}
 
-        def quantize_q(t, g, on_scalar, rounded, codes):
+        def round_q(engine_copy, t, g, rounded):
+            engine_copy(
+                rounded[:].rearrange("p (c i) j -> p c j i", i=4),
+                q_raw[t, g].rearrange("p j (c i) -> p c j i", i=4),
+            )
+
+        def quantize_q(t, g, rounded):
+            codes = keep.tile([P, P], U32, name=f"q_codes{t}{g}", align_bytes=64)
             scales = keep.tile([P, P], U8, name=f"q_scales{t}{g}", align_bytes=64)
-            raw = q_raw[t, g]
-            if on_scalar > 0:
-                nc.scalar.copy(
-                    rounded[:, :on_scalar].rearrange("p (c i) j -> p c j i", i=4),
-                    raw[:, :, :on_scalar].rearrange("p j (c i) -> p c j i", i=4),
-                )
-            if on_scalar < P:
-                nc.vector.tensor_copy(
-                    rounded[:, on_scalar:].rearrange("p (c i) j -> p c j i", i=4),
-                    raw[:, :, on_scalar:].rearrange("p j (c i) -> p c j i", i=4),
-                )
             nc.vector.quantize_mx(
                 out=codes[:].bitcast(FP8X4), scales=scales[:], in_=rounded[:].rearrange("p w j -> p (w j)")
             )
             q_codes[t, g], q_scales[t, g] = codes[:].bitcast(FP8X4), scales[:]
 
-        def gather_words(h, pairs):
-            word_pairs[h] = pairs
+        for h in range(HALVES):
+            word_pairs[h] = place(f"word_pairs{h}", [P, HALF], U32, 3072 + 1024 * h)
             nc.vector.tensor_copy(word_pairs[h][:], word_pool[:].bitcast(U32).indirect(part_list(h * HALF, (h + 1) * HALF)))
+        for h in range(HALVES):
+            k_parted[h] = keep.tile([P, PASSES, HALF], U16, name=f"k_codes{h}", align_bytes=64)
+            nc.vector.tensor_copy(k_parted[h][:], word_pairs[h][:].bitcast(U16).rearrange("p (n g) -> p g n", g=PASSES))
 
-        def part_words(h):
-            parted = keep.tile([P, PASSES, HALF], U16, name=f"k_codes{h}", align_bytes=64)
-            nc.vector.tensor_copy(parted[:], word_pairs[h][:].bitcast(U16).rearrange("p (n g) -> p g n", g=PASSES))
-            for i in range(CHUNKS):
-                for g in range(PASSES):
-                    k_codes[h * CHUNKS + i, g] = parted[:, g, i * P : (i + 1) * P].bitcast(FP4X4)
+        def k_codes(lo, hi, g):
+            h = lo // HALF
+            return k_parted[h][:, g, lo - h * HALF : hi - h * HALF].bitcast(FP4X4)
 
-        def score_by_rows(t, c, b, biased):
-            sums = bank(f"row_sums{c}", [P, P], b)
-            for g in range(PASSES):
-                nc.tensor.matmul_mx(
-                    out=sums[:],
-                    lhsT=q_codes[t, g],
-                    lhsT_scale=q_scales[t, g],
-                    rhs=k_codes[c, g],
-                    rhs_scale=k_planes[g][:, c * P : (c + 1) * P],
-                    start=(g == 0),
-                    stop=(g == PASSES - 1),
-                )
-            nc.vector.tensor_tensor(biased, sums[:], kb_rows[c], ADD)
-
-        def score(t, chunks, sums_banks, turned_bank, gates):
-            name = f"{t}{chunks[0]}"
-            biased = keep.tile([P, len(chunks), P], F32, name=f"biased{name}")
-            for i, c in enumerate(chunks):
-                sums = bank(f"sums{t}{c}", [P, P], sums_banks[i])
-                for g in range(PASSES):
-                    nc.tensor.matmul_mx(
-                        out=sums[:],
-                        lhsT=k_codes[c, g],
-                        lhsT_scale=k_planes[g][:, c * P : (c + 1) * P],
-                        rhs=q_codes[t, g],
-                        rhs_scale=q_scales[t, g],
-                        start=(g == 0),
-                        stop=(g == PASSES - 1),
-                    )
-                nc.scalar.activation(biased[:, i, :], sums[:], ACT.Identity, bias=kb_cols[c])
-            turned = bank(f"turned{name}", [P, len(chunks), P], turned_bank)
-            for i in range(len(chunks)):
-                nc.tensor.transpose(turned[:, i, :], biased[:, i, :], ident[:])
-            nc.scalar.activation(
-                gates, turned[:].rearrange("p c s -> p (c s)"), ACT.Sigmoid, bias=neg_th[:, t : t + 1]
-            )
-
-        def store(t, queue, lo, hi):
-            queue.dma_start(out[0, t * P : (t + 1) * P, lo:hi], maps[t][:, lo:hi])
-
-        gather_words(0, keep.tile([P, HALF], U32, name="word_pairs0", tag="words_then_q", align_bytes=64))
-        gather_words(1, place("word_pairs1", [P, HALF], U32, 0))
-        part_words(0)
-        quantize_q(0, 0, P, keep.tile([P, P, PACK], BF16, name="q_bf00", tag="kb_then_q0", align_bytes=64), keep.tile([P, P], U32, name="q_codes00", tag="words_then_q", align_bytes=64))
-        part_words(1)
-        quantize_q(0, 1, 0, place("q_bf01", [P, P, PACK], BF16, 0), keep.tile([P, P], U32, name="q_codes01", align_bytes=64))
+        rounded = {
+            (0, 0): place("q_bf00", [P, P, PACK], BF16, 0),
+            (1, 0): place("q_bf10", [P, P, PACK], BF16, 1024),
+            (0, 1): place("q_bf01", [P, P, PACK], BF16, 4096),
+            (1, 1): place("q_bf11", [P, P, PACK], BF16, 2048),
+        }
+        round_q(nc.scalar.copy, 0, 0, rounded[0, 0])
+        round_q(nc.scalar.copy, 1, 0, rounded[1, 0])
         th_turned = bank("th_turned", [P, P], 4)
         nc.tensor.transpose(th_turned[:], th_rows[:], ident[:])
         neg_th = keep.tile([P, Q_TILES], F32, name="neg_th")
         nc.scalar.activation(neg_th[:], th_turned[:, P - Q_TILES :], ACT.Copy, scale=-1.0)
+        round_q(nc.scalar.copy, 1, 1, rounded[1, 1])
+        quantize_q(0, 0, rounded[0, 0])
+        round_q(nc.vector.tensor_copy, 0, 1, rounded[0, 1])
+        quantize_q(0, 1, rounded[0, 1])
+        quantize_q(1, 0, rounded[1, 0])
+        quantize_q(1, 1, rounded[1, 1])
+        maps[1] = place("map1", [P, T], F32, 0)
+        for lo in range(0, T, N):
+            nc.gpsimd.memset(maps[1][:, lo : lo + N], 0.0)
 
-        first_biased = keep.tile([P, P], F32, name="first_biased")
-        rest_biased = keep.tile([P, N - P], F32, name="rest_biased")
-        first_gates = keep.tile([P, P], F32, name="first_gates")
-        rest_gates = keep.tile([P, N - P], F32, name="rest_gates")
-        score_by_rows(0, 0, 0, first_biased[:])
-        for c in range(1, N // P):
-            score_by_rows(0, c, c, rest_biased[:, (c - 1) * P : c * P])
-        quantize_q(1, 0, P, keep.tile([P, P, PACK], BF16, name="q_bf10", tag="kb_then_q1", align_bytes=64), place("q_codes10", [P, P], U32, 0))
-        quantize_q(1, 1, P, keep.tile([P, P, PACK], BF16, name="q_bf11", align_bytes=64), place("q_codes11", [P, P], U32, 512))
-        nc.scalar.activation(first_gates[:], first_biased[:], ACT.Sigmoid, bias=neg_th[:, 0:1])
-        nc.scalar.activation(rest_gates[:], rest_biased[:], ACT.Sigmoid, bias=neg_th[:, 0:1])
-        nc.vector.tensor_tensor(maps[0][:].indirect(part_list(0, P)), first_gates[:], maps[1][:, :P], ADD)
+        def score_by_rows(name, pieces, b):
+            lo, hi = pieces[0][0], pieces[-1][1]
+            sums = bank(f"row_sums_{name}", [P, hi - lo], b)
+            for g in range(PASSES):
+                for i, (a, z) in enumerate(pieces):
+                    nc.tensor.matmul_mx(
+                        out=sums[:, a - lo : z - lo],
+                        lhsT=q_codes[0, g],
+                        lhsT_scale=q_scales[0, g],
+                        rhs=k_codes(a, z, g),
+                        rhs_scale=k_planes[g][:, a:z],
+                        start=(g == 0 and i == 0),
+                        stop=(g == PASSES - 1 and i == len(pieces) - 1),
+                    )
+            biased = keep.tile([P, hi - lo], F32, name=f"biased_{name}")
+            nc.vector.tensor_tensor(biased[:], sums[:], kb_rows[:, lo:hi], ADD)
+            gates = keep.tile([P, hi - lo], F32, name=f"gates_{name}")
+            nc.scalar.activation(gates[:], biased[:], ACT.Sigmoid, bias=neg_th[:, 0:1])
+            return gates
+
+        first_gates = score_by_rows("first", [(0, P)], 0)
+        rest_gates = score_by_rows("rest", [(P, HALF), (HALF, N)], 1)
+        nc.vector.tensor_tensor(maps[0][:].indirect(part_list(0, P)), first_gates[:], zeros[:], ADD)
         nc.vector.tensor_copy(maps[0][:].indirect(part_list(P, N)), rest_gates[:])
-        store(0, nc.sync, 0, T)
-        last_gates = keep.tile([P, N], F32, name="last_gates")
-        score(1, (0, 1), (0, 1), 4, last_gates[:, :HALF])
-        score(1, (2, 3), (2, 3), 5, last_gates[:, HALF:])
-        nc.vector.tensor_copy(maps[1][:].indirect(offsets[:]), last_gates[:])
-        store(1, nc.sync, 0, T // 2)
-        store(1, nc.scalar, T // 2, T)
+        nc.sync.dma_start(out[0, :P, :], maps[0][:])
+
+        for h in range(HALVES):
+            biased = keep.tile([P, 2, P], F32, name=f"biased{h}")
+            sums = bank(f"sums{h}", [P, 2, P], h)
+            for i in range(2):
+                c = 2 * h + i
+                for g in range(PASSES):
+                    nc.tensor.matmul_mx(
+                        out=sums[:, i, :],
+                        lhsT=k_codes(c * P, (c + 1) * P, g),
+                        lhsT_scale=k_planes[g][:, c * P : (c + 1) * P],
+                        rhs=q_codes[1, g],
+                        rhs_scale=q_scales[1, g],
+                        start=(g == 0),
+                        stop=(g == PASSES - 1),
+                    )
+            for i in range(2):
+                c = 2 * h + i
+                nc.scalar.activation(biased[:, i, :], sums[:, i, :], ACT.Identity, bias=kb_cols[:, c : c + 1])
+            turned = bank(f"turned{h}", [P, 2, P], 6 + h)
+            for i in range(2):
+                nc.tensor.transpose(turned[:, i, :], biased[:, i, :], ident[:])
+            gates = keep.tile([P, HALF], F32, name=f"gates{h}")
+            nc.scalar.activation(gates[:], turned[:].rearrange("p c s -> p (c s)"), ACT.Sigmoid, bias=neg_th[:, 1:2])
+            nc.scalar.activation(maps[1][:].indirect(part_list(h * HALF, (h + 1) * HALF)), gates[:], ACT.Copy)
+        nc.sync.dma_start(out[0, P:, :], maps[1][:])

@@ -63,9 +63,8 @@ def tile_attend_sigscat_topk_kernel(tc, qT, k_words, k_scales, kb, th, offs, out
         q_rows = qT[0].rearrange("(g p j) w -> g p j w", g=PASSES, j=PACK)
         first_pass = keep.tile([P, PACK, NQ], F32, name="first_pass")
         nc.sync.dma_start(first_pass[:], q_rows[0])
-        second_pass = keep.tile([P, Q_TILES, PACK, P], F32, name="second_pass")
-        for t in range(Q_TILES):
-            nc.sync.dma_start(second_pass[:, t], q_rows[1][:, :, t * P : (t + 1) * P])
+        second_pass = keep.tile([P, PACK, NQ], F32, name="second_pass")
+        nc.sync.dma_start(second_pass[:], q_rows[1])
 
         def zero_on_vector(tile, rows, lo, hi):
             nc.vector.memset(tile[:rows, lo : hi - 1], 0)
@@ -100,7 +99,7 @@ def tile_attend_sigscat_topk_kernel(tc, qT, k_words, k_scales, kb, th, offs, out
 
         q_raw = {(t, 0): first_pass[:, :, t * P : (t + 1) * P] for t in range(Q_TILES)}
         for t in range(Q_TILES):
-            q_raw[t, 1] = second_pass[:, t]
+            q_raw[t, 1] = second_pass[:, :, t * P : (t + 1) * P]
         k_planes = [plane.bitcast(U8) for plane in planes]
 
         kb_listed = place("kb_listed", [P, N], F32, 512)
@@ -171,35 +170,38 @@ def tile_attend_sigscat_topk_kernel(tc, qT, k_words, k_scales, kb, th, offs, out
         for lo in range(0, T, N):
             nc.gpsimd.memset(maps[1][:, lo : lo + N], 0.0)
 
-        def score_by_rows(name, pieces, b):
-            lo, hi = pieces[0][0], pieces[-1][1]
-            sums = bank(f"row_sums_{name}", [P, hi - lo], b)
-            for g in range(PASSES):
-                for i, (a, z) in enumerate(pieces):
+        pieces = {"first": [(0, P)], "rest": [(P, HALF), (HALF, N)]}
+        row_sums = {"first": bank("row_sums_first", [P, P], 0), "rest": bank("row_sums_rest", [P, N - P], 1)}
+        for g in range(PASSES):
+            for name, spans in (("first", pieces["first"]), ("rest", pieces["rest"])):
+                for i, (a, z) in enumerate(spans):
                     nc.tensor.matmul_mx(
-                        out=sums[:, a - lo : z - lo],
+                        out=row_sums[name][:, a - spans[0][0] : z - spans[0][0]],
                         lhsT=q_codes[0, g],
                         lhsT_scale=q_scales[0, g],
                         rhs=k_codes(a, z, g),
                         rhs_scale=k_planes[g][:, a:z],
                         start=(g == 0 and i == 0),
-                        stop=(g == PASSES - 1 and i == len(pieces) - 1),
+                        stop=(g == PASSES - 1 and i == len(spans) - 1),
                     )
+
+        def gate_rows(name):
+            lo, hi = pieces[name][0][0], pieces[name][-1][1]
             biased = keep.tile([P, hi - lo], F32, name=f"biased_{name}")
-            nc.vector.tensor_tensor(biased[:], sums[:], kb_rows[:, lo:hi], ADD)
+            nc.vector.tensor_tensor(biased[:], row_sums[name][:], kb_rows[:, lo:hi], ADD)
             gates = keep.tile([P, hi - lo], F32, name=f"gates_{name}")
             nc.scalar.activation(gates[:], biased[:], ACT.Sigmoid, bias=neg_th[:, 0:1])
             return gates
 
-        first_gates = score_by_rows("first", [(0, P)], 0)
-        rest_gates = score_by_rows("rest", [(P, HALF), (HALF, N)], 1)
+        first_gates = gate_rows("first")
+        rest_gates = gate_rows("rest")
         nc.vector.tensor_tensor(maps[0][:].indirect(part_list(0, P)), first_gates[:], zeros[:], ADD)
         nc.vector.tensor_copy(maps[0][:].indirect(part_list(P, N)), rest_gates[:])
         nc.sync.dma_start(out[0, :P, :], maps[0][:])
 
         for h in range(HALVES):
             biased = keep.tile([P, 2, P], F32, name=f"biased{h}")
-            sums = bank(f"sums{h}", [P, 2, P], h)
+            sums = bank(f"sums{h}", [P, 2, P], 2 + h)
             for i in range(2):
                 c = 2 * h + i
                 for g in range(PASSES):

@@ -56,10 +56,10 @@ def tile_attend_sigscat_topk_kernel(tc, qT, k_words, k_scales, kb, th, offs, out
         )
         kb_pool = keep.tile([P, T], F32, name="kb_pool")
         nc.sync.dma_start(kb_pool[KB_ROW : KB_ROW + 1, :], kb[0:1, :])
-        th_rows = keep.tile([P, P], F32, name="th_rows")
-        nc.sync.dma_start(th_rows[P - Q_TILES :, :], th[0].rearrange("(t p) o -> t (p o)", p=P))
         word_pool = keep.tile([P, T], I32, name="word_pool")
         nc.sync.dma_start(word_pool[:], k_words[0].rearrange("p t b -> p (t b)").bitcast(I32))
+        th_rows = keep.tile([P, P], F32, name="th_rows")
+        nc.sync.dma_start(th_rows[P - Q_TILES :, :], th[0].rearrange("(t p) o -> t (p o)", p=P))
         q_rows = qT[0].rearrange("(g p j) w -> g p j w", g=PASSES, j=PACK)
         first_pass = keep.tile([P, PACK, NQ], F32, name="first_pass")
         nc.sync.dma_start(first_pass[:], q_rows[0])
@@ -123,18 +123,24 @@ def tile_attend_sigscat_topk_kernel(tc, qT, k_words, k_scales, kb, th, offs, out
 
         q_codes, q_scales, k_parted, word_pairs = {}, {}, {}, {}
 
-        def round_q(engine_copy, t, g, rounded):
-            engine_copy(
-                rounded[:].rearrange("p (c i) j -> p c j i", i=4),
-                q_raw[t, g].rearrange("p j (c i) -> p c j i", i=4),
-            )
+        def round_q(engine_copy, t, g, rounded, parts=1):
+            width = P // parts
+            for lo in range(0, P, width):
+                engine_copy(
+                    rounded[:, lo : lo + width].rearrange("p (c i) j -> p c j i", i=4),
+                    q_raw[t, g][:, :, lo : lo + width].rearrange("p j (c i) -> p c j i", i=4),
+                )
 
-        def quantize_q(t, g, rounded):
+        def quantize_q(t, g, rounded, parts=1):
             codes = keep.tile([P, P], U32, name=f"q_codes{t}{g}", align_bytes=64)
             scales = keep.tile([P, P], U8, name=f"q_scales{t}{g}", align_bytes=64)
-            nc.vector.quantize_mx(
-                out=codes[:].bitcast(FP8X4), scales=scales[:], in_=rounded[:].rearrange("p w j -> p (w j)")
-            )
+            width = P // parts
+            for lo in range(0, P, width):
+                nc.vector.quantize_mx(
+                    out=codes[:, lo : lo + width].bitcast(FP8X4),
+                    scales=scales[:, lo : lo + width],
+                    in_=rounded[:, lo : lo + width].rearrange("p w j -> p (w j)"),
+                )
             q_codes[t, g], q_scales[t, g] = codes[:].bitcast(FP8X4), scales[:]
 
         for h in range(HALVES):
@@ -156,45 +162,42 @@ def tile_attend_sigscat_topk_kernel(tc, qT, k_words, k_scales, kb, th, offs, out
         }
         round_q(nc.scalar.copy, 0, 0, rounded[0, 0])
         round_q(nc.scalar.copy, 1, 0, rounded[1, 0])
-        th_turned = bank("th_turned", [P, P], 4)
+        th_turned = bank("th_turned", [P, P], 6)
         nc.tensor.transpose(th_turned[:], th_rows[:], ident[:])
         neg_th = keep.tile([P, Q_TILES], F32, name="neg_th")
         nc.scalar.activation(neg_th[:], th_turned[:, P - Q_TILES :], ACT.Copy, scale=-1.0)
         round_q(nc.scalar.copy, 1, 1, rounded[1, 1])
         quantize_q(0, 0, rounded[0, 0])
-        round_q(nc.vector.tensor_copy, 0, 1, rounded[0, 1])
-        quantize_q(0, 1, rounded[0, 1])
+        round_q(nc.vector.tensor_copy, 0, 1, rounded[0, 1], parts=2)
+        quantize_q(0, 1, rounded[0, 1], parts=2)
         quantize_q(1, 0, rounded[1, 0])
         quantize_q(1, 1, rounded[1, 1])
         maps[1] = place("map1", [P, T], F32, 0)
         for lo in range(0, T, N):
             nc.gpsimd.memset(maps[1][:, lo : lo + N], 0.0)
 
-        pieces = {"first": [(0, P)], "rest": [(P, HALF), (HALF, N)]}
-        row_sums = {"first": bank("row_sums_first", [P, P], 0), "rest": bank("row_sums_rest", [P, N - P], 1)}
+        spans = [(0, P), (HALF, N), (P, HALF)]
+        row_sums = [bank(f"row_sums{lo}", [P, hi - lo], b) for (lo, hi), b in zip(spans, (0, 1, 4))]
         for g in range(PASSES):
-            for name, spans in (("first", pieces["first"]), ("rest", pieces["rest"])):
-                for i, (a, z) in enumerate(spans):
-                    nc.tensor.matmul_mx(
-                        out=row_sums[name][:, a - spans[0][0] : z - spans[0][0]],
-                        lhsT=q_codes[0, g],
-                        lhsT_scale=q_scales[0, g],
-                        rhs=k_codes(a, z, g),
-                        rhs_scale=k_planes[g][:, a:z],
-                        start=(g == 0 and i == 0),
-                        stop=(g == PASSES - 1 and i == len(spans) - 1),
-                    )
-
-        def gate_rows(name):
-            lo, hi = pieces[name][0][0], pieces[name][-1][1]
-            biased = keep.tile([P, hi - lo], F32, name=f"biased_{name}")
-            nc.vector.tensor_tensor(biased[:], row_sums[name][:], kb_rows[:, lo:hi], ADD)
-            gates = keep.tile([P, hi - lo], F32, name=f"gates_{name}")
-            nc.scalar.activation(gates[:], biased[:], ACT.Sigmoid, bias=neg_th[:, 0:1])
-            return gates
-
-        first_gates = gate_rows("first")
-        rest_gates = gate_rows("rest")
+            for (lo, hi), sums in zip(spans, row_sums):
+                nc.tensor.matmul_mx(
+                    out=sums[:],
+                    lhsT=q_codes[0, g],
+                    lhsT_scale=q_scales[0, g],
+                    rhs=k_codes(lo, hi, g),
+                    rhs_scale=k_planes[g][:, lo:hi],
+                    start=(g == 0),
+                    stop=(g == PASSES - 1),
+                )
+        first_biased = keep.tile([P, P], F32, name="first_biased")
+        rest_biased = keep.tile([P, N - P], F32, name="rest_biased")
+        first_gates = keep.tile([P, P], F32, name="first_gates")
+        rest_gates = keep.tile([P, N - P], F32, name="rest_gates")
+        for (lo, hi), sums in zip(spans, row_sums):
+            biased = first_biased[:] if lo == 0 else rest_biased[:, lo - P : hi - P]
+            nc.vector.tensor_tensor(biased, sums[:], kb_rows[:, lo:hi], ADD)
+        nc.scalar.activation(first_gates[:], first_biased[:], ACT.Sigmoid, bias=neg_th[:, 0:1])
+        nc.scalar.activation(rest_gates[:], rest_biased[:], ACT.Sigmoid, bias=neg_th[:, 0:1])
         nc.vector.tensor_tensor(maps[0][:].indirect(part_list(0, P)), first_gates[:], zeros[:], ADD)
         nc.vector.tensor_copy(maps[0][:].indirect(part_list(P, N)), rest_gates[:])
         nc.sync.dma_start(out[0, :P, :], maps[0][:])
@@ -204,20 +207,20 @@ def tile_attend_sigscat_topk_kernel(tc, qT, k_words, k_scales, kb, th, offs, out
             sums = bank(f"sums{h}", [P, 2, P], 2 + h)
             for i in range(2):
                 c = 2 * h + i
-                for g in range(PASSES):
+                for g in reversed(range(PASSES)):
                     nc.tensor.matmul_mx(
                         out=sums[:, i, :],
                         lhsT=k_codes(c * P, (c + 1) * P, g),
                         lhsT_scale=k_planes[g][:, c * P : (c + 1) * P],
                         rhs=q_codes[1, g],
                         rhs_scale=q_scales[1, g],
-                        start=(g == 0),
-                        stop=(g == PASSES - 1),
+                        start=(g == PASSES - 1),
+                        stop=(g == 0),
                     )
             for i in range(2):
                 c = 2 * h + i
                 nc.scalar.activation(biased[:, i, :], sums[:, i, :], ACT.Identity, bias=kb_cols[:, c : c + 1])
-            turned = bank(f"turned{h}", [P, 2, P], 6 + h)
+            turned = bank(f"turned{h}", [P, 2, P], 7)
             for i in range(2):
                 nc.tensor.transpose(turned[:, i, :], biased[:, i, :], ident[:])
             gates = keep.tile([P, HALF], F32, name=f"gates{h}")

@@ -43,17 +43,19 @@ def tile_attend_sigscat_topk_kernel(tc, qT, k_words, k_scales, kb, th, offs, out
         def place(name, shape, dtype, at):
             return placed.tile(shape, dtype, name=name, offset=at, align_bytes=64)
 
+        scale_pool = keep.tile([P, PASSES * T // 4], I32, name="scale_pool")
+
+        def load_scales(g):
+            nc.sync.dma_start(scale_pool[SCALE_ROW:, g * T // 4 : (g + 1) * T // 4], k_scales.bitcast(I32)[g])
+
+        load_scales(0)
         offsets = lists.tile([P, N // 16], U16, name="offsets")
         nc.sync.dma_start(offsets[:], offs)
+        load_scales(1)
 
         def part_list(lo, hi):
             return offsets[:, lo // 16 : hi // 16]
 
-        scale_pool = keep.tile([P, PASSES * T // 4], I32, name="scale_pool")
-        nc.sync.dma_start(
-            scale_pool[SCALE_ROW:, :].rearrange("f (o t) -> f o t", o=PASSES),
-            k_scales.bitcast(I32).rearrange("o f t -> f o t"),
-        )
         kb_pool = keep.tile([P, T], F32, name="kb_pool")
         nc.sync.dma_start(kb_pool[KB_ROW : KB_ROW + 1, :], kb[0:1, :])
         word_pool = keep.tile([P, T], I32, name="word_pool")

@@ -20,12 +20,13 @@ PACK = 4
 K_PASS = P * PACK
 PASSES = D // K_PASS
 Q_TILES = NQ // P
-HALVES = 2
-HALF = N // HALVES
-CHUNKS = N // P
+HALF = N // 2
 BANK_BYTES = 2048
 KB_ROW = P - 1
-SCALE_ROW = P - 16
+SCALE_ROW = 32
+ROWS = 16
+KB_SPLIT = 1024
+MAP_SPLIT = 640
 FLOPS = 2 * NQ * N * D
 
 
@@ -43,21 +44,18 @@ def tile_attend_sigscat_topk_kernel(tc, qT, k_words, k_scales, kb, th, offs, out
         def place(name, shape, dtype, at):
             return placed.tile(shape, dtype, name=name, offset=at, align_bytes=64)
 
-        scale_pool = keep.tile([P, PASSES * T // 4], I32, name="scale_pool")
-
-        def load_scales(g):
-            nc.sync.dma_start(scale_pool[SCALE_ROW:, g * T // 4 : (g + 1) * T // 4], k_scales.bitcast(I32)[g])
-
-        load_scales(0)
+        scale_pool = place("scale_pool", [P, T // 4], I32, 15360)
+        nc.sync.dma_start(
+            scale_pool[SCALE_ROW : SCALE_ROW + PASSES * ROWS, :], k_scales.bitcast(I32).rearrange("o f t -> (o f) t")
+        )
         offsets = lists.tile([P, N // 16], U16, name="offsets")
         nc.sync.dma_start(offsets[:], offs)
-        load_scales(1)
 
         def part_list(lo, hi):
             return offsets[:, lo // 16 : hi // 16]
 
         kb_pool = keep.tile([P, T], F32, name="kb_pool")
-        nc.sync.dma_start(kb_pool[KB_ROW : KB_ROW + 1, :], kb[0:1, :])
+        nc.scalar.dma_start(kb_pool[KB_ROW : KB_ROW + 1, :], kb[0:1, :])
         word_pool = keep.tile([P, T], I32, name="word_pool")
         nc.sync.dma_start(word_pool[:], k_words[0].rearrange("p t b -> p (t b)").bitcast(I32))
         th_rows = keep.tile([P, P], F32, name="th_rows")
@@ -65,76 +63,83 @@ def tile_attend_sigscat_topk_kernel(tc, qT, k_words, k_scales, kb, th, offs, out
         q_rows = qT[0].rearrange("(g p j) w -> g p j w", g=PASSES, j=PACK)
         first_pass = keep.tile([P, PACK, NQ], F32, name="first_pass")
         nc.sync.dma_start(first_pass[:], q_rows[0])
-        second_pass = keep.tile([P, PACK, NQ], F32, name="second_pass")
-        nc.sync.dma_start(second_pass[:], q_rows[1])
 
         def zero_on_vector(tile, rows, lo, hi):
-            nc.vector.memset(tile[:rows, lo : hi - 1], 0)
-            nc.vector.memset(tile[:rows, hi - 1 : hi], 0)
+            nc.vector.memset(tile[rows, lo : hi - 1], 0)
+            nc.vector.memset(tile[rows, hi - 1 : hi], 0)
 
         warm_in = keep.tile([P, 1], F32, name="warm_in")
         warm_out = keep.tile([P, 1], F32, name="warm_out")
         nc.gpsimd.memset(warm_in[:], 0.0)
         nc.scalar.activation(warm_out[:], warm_in[:], ACT.Sigmoid)
 
-        maps = {0: keep.tile([P, T], F32, name="map0")}
-        plane_pair = keep.tile([P, PASSES * N // 4], I32, name="planes", align_bytes=64)
-        planes = [plane_pair[:, g * N // 4 : (g + 1) * N // 4] for g in range(PASSES)]
-        zero_on_vector(kb_pool, KB_ROW, 0, T // 2)
-        zero_on_vector(scale_pool, SCALE_ROW, 0, 3 * T // 8)
-        nc.gpsimd.memset(kb_pool[:KB_ROW, T // 2 :], 0.0)
-        nc.gpsimd.memset(scale_pool[:SCALE_ROW, 3 * T // 8 :], 0)
+        planes = keep.tile([P, PASSES * N // 4], I32, name="planes", align_bytes=64)
+        zero_on_vector(scale_pool, slice(0, SCALE_ROW), 0, T // 4)
+        zero_on_vector(kb_pool, slice(0, KB_ROW), 0, KB_SPLIT)
+        nc.gpsimd.memset(scale_pool[SCALE_ROW + PASSES * ROWS :, :], 0)
+        nc.gpsimd.memset(kb_pool[:KB_ROW, KB_SPLIT:], 0.0)
+        nc.gpsimd.memset(planes[:], 0)
         ident = keep.tile([P, P], F32, name="ident")
         make_identity(nc, ident[:])
+        nc.gpsimd.memset(th_rows[: P - Q_TILES, :], 0.0)
         zeros = keep.tile([P, P], F32, name="zeros")
         nc.gpsimd.memset(zeros[:], 0.0)
-        nc.gpsimd.memset(th_rows[: P - Q_TILES, :], 0.0)
-        nc.gpsimd.memset(plane_pair[:], 0)
-        nc.gpsimd.memset(maps[0][:], 0.0)
 
-        listed_bytes = keep.tile([P, PASSES * N], U8, name="listed_bytes")
-        for g in range(PASSES):
-            window = scale_pool[:].bitcast(U8)[:, g * T : (g + 1) * T]
-            nc.vector.tensor_copy(listed_bytes[:, g * N : (g + 1) * N], window.indirect(offsets[:]))
-        for r in range(4):
-            nc.sync.dma_start(plane_pair[r:P:32, :], listed_bytes[:].bitcast(I32)[SCALE_ROW + r : P : 4, :])
+        listed_bytes = keep.tile([P, N], U8, name="listed_bytes")
+        nc.vector.tensor_copy(listed_bytes[:], scale_pool[:].bitcast(U8).indirect(offsets[:]))
 
-        q_raw = {(t, 0): first_pass[:, :, t * P : (t + 1) * P] for t in range(Q_TILES)}
-        for t in range(Q_TILES):
-            q_raw[t, 1] = second_pass[:, :, t * P : (t + 1) * P]
-        k_planes = [plane.bitcast(U8) for plane in planes]
+        def move_rows(g, r):
+            first = SCALE_ROW + g * ROWS
+            nc.sync.dma_start(
+                planes[r:P:32, g * N // 4 : (g + 1) * N // 4], listed_bytes[:].bitcast(I32)[first + r : first + ROWS : 4, :]
+            )
 
-        kb_listed = place("kb_listed", [P, N], F32, 512)
-        kb_cols = keep.tile([P, CHUNKS], F32, name="kb_cols")
-        kb_rows = keep.tile([P, N], F32, name="kb_rows")
-        for h in range(HALVES):
-            cols = slice(h * HALF, (h + 1) * HALF)
-            nc.scalar.activation(kb_listed[:, cols], kb_pool[:].indirect(part_list(cols.start, cols.stop)), ACT.Copy)
-        for h in range(HALVES):
-            turned = bank(f"kb_turned{h}", [P, 2, P], 4 + h)
+        moves = [(g, r) for g in range(PASSES) for r in range(4)]
+        move_rows(*moves[0])
+        second_pass = place("second_pass", [P, PACK, NQ], F32, 12288)
+        nc.sync.dma_start(second_pass[:], q_rows[1])
+        for g, r in moves[1:]:
+            move_rows(g, r)
+        k_planes = [planes[:].bitcast(U8)[:, g * N : (g + 1) * N] for g in range(PASSES)]
+
+        maps = {0: place("map0", [P, T], F32, 16384)}
+        zero_on_vector(maps[0], slice(0, P), 0, MAP_SPLIT)
+        nc.gpsimd.memset(maps[0][:, MAP_SPLIT:], 0.0)
+
+        q_raw = {(t, g): (first_pass, second_pass)[g][:, :, t * P : (t + 1) * P] for t in range(Q_TILES) for g in range(PASSES)}
+
+        kb_listed = place("kb_listed", [P, N], F32, 7680)
+        for lo in range(0, N, HALF):
+            nc.scalar.activation(kb_listed[:, lo : lo + HALF], kb_pool[:].indirect(part_list(lo, lo + HALF)), ACT.Copy)
+        low_cols = keep.tile([P, 2], F32, name="low_cols")
+        high_cols = keep.tile([P, 2], F32, name="high_cols")
+        first_rows = place("first_rows", [P, P], F32, 26624)
+
+        def turn_bias(h, cols, b):
+            turned = bank(f"kb_turned{h}", [P, 2, P], b)
             for i in range(2):
                 c = 2 * h + i
                 nc.tensor.transpose(turned[:, i, :], kb_listed[:, c * P : (c + 1) * P], ident[:])
-            nc.scalar.copy(kb_cols[:, 2 * h : 2 * h + 2], turned[:, :, KB_ROW])
-        for h in range(HALVES):
-            spread = bank(f"kb_spread{h}", [P, 2, P], 6 + h)
-            for i in range(2):
-                c = 2 * h + i
-                nc.tensor.transpose(spread[:, i, :], kb_cols[:, c : c + 1].to_broadcast([P, P]), ident[:])
-            nc.scalar.copy(kb_rows[:, h * HALF : (h + 1) * HALF], spread[:].rearrange("p c s -> p (c s)"))
+            nc.scalar.copy(cols, turned[:, :, KB_ROW])
+
+        turn_bias(0, low_cols[:], 4)
+        spread = bank("first_spread", [P, P], 5)
+        nc.tensor.transpose(spread[:], low_cols[:, 0:1].to_broadcast([P, P]), ident[:])
+        nc.scalar.copy(first_rows[:], spread[:])
+        turn_bias(1, high_cols[:], 6)
+        spread = bank("high_spread", [P, 2, P], 7)
+        for i in range(2):
+            nc.tensor.transpose(spread[:, i, :], high_cols[:, i : i + 1].to_broadcast([P, P]), ident[:])
 
         q_codes, q_scales, k_parted, word_pairs = {}, {}, {}, {}
 
-        def round_q(engine_copy, t, g, rounded, parts=1):
-            width = P // parts
-            for lo in range(0, P, width):
-                engine_copy(
-                    rounded[:, lo : lo + width].rearrange("p (c i) j -> p c j i", i=4),
-                    q_raw[t, g][:, :, lo : lo + width].rearrange("p j (c i) -> p c j i", i=4),
-                )
+        def round_q(engine_copy, t, g, rounded, lo=0, hi=P):
+            engine_copy(
+                rounded[:, lo:hi].rearrange("p (c i) j -> p c j i", i=4),
+                q_raw[t, g][:, :, lo:hi].rearrange("p j (c i) -> p c j i", i=4),
+            )
 
-        def quantize_q(t, g, rounded, parts=1):
-            codes = keep.tile([P, P], U32, name=f"q_codes{t}{g}", align_bytes=64)
+        def quantize_q(t, g, rounded, codes, parts=1):
             scales = keep.tile([P, P], U8, name=f"q_scales{t}{g}", align_bytes=64)
             width = P // parts
             for lo in range(0, P, width):
@@ -145,10 +150,10 @@ def tile_attend_sigscat_topk_kernel(tc, qT, k_words, k_scales, kb, th, offs, out
                 )
             q_codes[t, g], q_scales[t, g] = codes[:].bitcast(FP8X4), scales[:]
 
-        for h in range(HALVES):
-            word_pairs[h] = place(f"word_pairs{h}", [P, HALF], U32, 3072 + 1024 * h)
+        for h in range(2):
+            word_pairs[h] = place(f"word_pairs{h}", [P, HALF], U32, 24576 + 1024 * h)
             nc.vector.tensor_copy(word_pairs[h][:], word_pool[:].bitcast(U32).indirect(part_list(h * HALF, (h + 1) * HALF)))
-        for h in range(HALVES):
+        for h in range(2):
             k_parted[h] = keep.tile([P, PASSES, HALF], U16, name=f"k_codes{h}", align_bytes=64)
             nc.vector.tensor_copy(k_parted[h][:], word_pairs[h][:].bitcast(U16).rearrange("p (n g) -> p g n", g=PASSES))
 
@@ -157,75 +162,98 @@ def tile_attend_sigscat_topk_kernel(tc, qT, k_words, k_scales, kb, th, offs, out
             return k_parted[h][:, g, lo - h * HALF : hi - h * HALF].bitcast(FP4X4)
 
         rounded = {
-            (0, 0): place("q_bf00", [P, P, PACK], BF16, 0),
-            (1, 0): place("q_bf10", [P, P, PACK], BF16, 1024),
-            (0, 1): place("q_bf01", [P, P, PACK], BF16, 4096),
-            (1, 1): place("q_bf11", [P, P, PACK], BF16, 2048),
+            (0, 0): place("q_bf00", [P, P, PACK], BF16, 8192),
+            (1, 0): place("q_bf10", [P, P, PACK], BF16, 9216),
+            (0, 1): place("q_bf01", [P, P, PACK], BF16, 8192),
+            (1, 1): place("q_bf11", [P, P, PACK], BF16, 7168),
         }
-        round_q(nc.scalar.copy, 0, 0, rounded[0, 0])
-        round_q(nc.scalar.copy, 1, 0, rounded[1, 0])
-        th_turned = bank("th_turned", [P, P], 6)
+        th_turned = bank("th_turned", [P, P], 4)
         nc.tensor.transpose(th_turned[:], th_rows[:], ident[:])
         neg_th = keep.tile([P, Q_TILES], F32, name="neg_th")
         nc.scalar.activation(neg_th[:], th_turned[:, P - Q_TILES :], ACT.Copy, scale=-1.0)
+        round_q(nc.scalar.copy, 0, 0, rounded[0, 0])
+        round_q(nc.scalar.copy, 1, 0, rounded[1, 0])
+        quantize_q(0, 0, rounded[0, 0], place("q_codes00", [P, P], U32, 25600))
+        for lo in range(0, P, P // 2):
+            round_q(nc.vector.tensor_copy, 0, 1, rounded[0, 1], lo, lo + P // 2)
         round_q(nc.scalar.copy, 1, 1, rounded[1, 1])
-        quantize_q(0, 0, rounded[0, 0])
-        round_q(nc.vector.tensor_copy, 0, 1, rounded[0, 1], parts=2)
-        quantize_q(0, 1, rounded[0, 1], parts=2)
-        quantize_q(1, 0, rounded[1, 0])
-        quantize_q(1, 1, rounded[1, 1])
+        high_rows = place("high_rows", [P, HALF], F32, 14336)
+        nc.scalar.copy(high_rows[:], spread[:].rearrange("p c s -> p (c s)"))
+        quantize_q(0, 1, rounded[0, 1], keep.tile([P, P], U32, name="q_codes01", align_bytes=64), parts=2)
+        quantize_q(1, 0, rounded[1, 0], place("q_codes10", [P, P], U32, 8704))
+        quantize_q(1, 1, rounded[1, 1], keep.tile([P, P], U32, name="q_codes11", align_bytes=64))
         maps[1] = place("map1", [P, T], F32, 0)
         for lo in range(0, T, N):
             nc.gpsimd.memset(maps[1][:, lo : lo + N], 0.0)
 
-        spans = [(0, P), (HALF, N), (P, HALF)]
-        row_sums = [bank(f"row_sums{lo}", [P, hi - lo], b) for (lo, hi), b in zip(spans, (0, 1, 4))]
+        def by_query(sums, t, lo, hi, g, first=0):
+            nc.tensor.matmul_mx(
+                out=sums,
+                lhsT=q_codes[t, g],
+                lhsT_scale=q_scales[t, g],
+                rhs=k_codes(lo, hi, g),
+                rhs_scale=k_planes[g][:, lo:hi],
+                start=(g == first),
+                stop=(g != first),
+            )
+
+        def by_slot(sums, t, lo, g, first=0):
+            nc.tensor.matmul_mx(
+                out=sums,
+                lhsT=k_codes(lo, lo + P, g),
+                lhsT_scale=k_planes[g][:, lo : lo + P],
+                rhs=q_codes[t, g],
+                rhs_scale=q_scales[t, g],
+                start=(g == first),
+                stop=(g != first),
+            )
+
+        first_sums = bank("first_sums", [P, P], 0)
+        high_sums = bank("high_sums", [P, HALF], 1)
+        second_sums = bank("second_sums", [P, P], 2)
         for g in range(PASSES):
-            for (lo, hi), sums in zip(spans, row_sums):
-                nc.tensor.matmul_mx(
-                    out=sums[:],
-                    lhsT=q_codes[0, g],
-                    lhsT_scale=q_scales[0, g],
-                    rhs=k_codes(lo, hi, g),
-                    rhs_scale=k_planes[g][:, lo:hi],
-                    start=(g == 0),
-                    stop=(g == PASSES - 1),
-                )
-        first_biased = keep.tile([P, P], F32, name="first_biased")
-        rest_biased = keep.tile([P, N - P], F32, name="rest_biased")
+            by_query(first_sums[:], 0, 0, P, g)
+            by_query(high_sums[:], 0, HALF, N, g)
+            by_slot(second_sums[:], 0, P, g)
+        first_biased = place("first_biased", [P, P], F32, 12288)
+        high_biased = place("high_biased", [P, HALF], F32, 13312)
         first_gates = keep.tile([P, P], F32, name="first_gates")
         rest_gates = keep.tile([P, N - P], F32, name="rest_gates")
-        for (lo, hi), sums in zip(spans, row_sums):
-            biased = first_biased[:] if lo == 0 else rest_biased[:, lo - P : hi - P]
-            nc.vector.tensor_tensor(biased, sums[:], kb_rows[:, lo:hi], ADD)
+        nc.vector.tensor_tensor(first_biased[:], first_sums[:], first_rows[:], ADD)
+        nc.vector.tensor_tensor(high_biased[:], high_sums[:], high_rows[:], ADD)
         nc.scalar.activation(first_gates[:], first_biased[:], ACT.Sigmoid, bias=neg_th[:, 0:1])
-        nc.scalar.activation(rest_gates[:], rest_biased[:], ACT.Sigmoid, bias=neg_th[:, 0:1])
+        second_biased = place("second_biased", [P, P], F32, 26368)
+        nc.scalar.activation(second_biased[:], second_sums[:], ACT.Identity, bias=low_cols[:, 1:2])
+        nc.scalar.activation(rest_gates[:, P:], high_biased[:], ACT.Sigmoid, bias=neg_th[:, 0:1])
+        other_low = [bank("other_low0", [P, P], 4)]
+        other_high = bank("other_high", [P, HALF], 3)
+        for g in reversed(range(PASSES)):
+            by_slot(other_low[0][:], 1, 0, g, first=PASSES - 1)
+        for g in reversed(range(PASSES)):
+            by_query(other_high[:], 1, HALF, N, g, first=PASSES - 1)
+        second_turned = bank("second_turned", [P, P], 5)
+        nc.tensor.transpose(second_turned[:], second_biased[:], ident[:])
+        nc.scalar.activation(rest_gates[:, :P], second_turned[:], ACT.Sigmoid, bias=neg_th[:, 0:1])
         nc.vector.tensor_tensor(maps[0][:].indirect(part_list(0, P)), first_gates[:], zeros[:], ADD)
+
+        other_low.append(bank("other_low1", [P, P], 2))
+        for g in range(PASSES):
+            by_slot(other_low[1][:], 1, P, g)
+        other_high_biased = place("other_high_biased", [P, HALF], F32, 12288)
+        nc.vector.tensor_tensor(other_high_biased[:], other_high[:], high_rows[:], ADD)
         nc.vector.tensor_copy(maps[0][:].indirect(part_list(P, N)), rest_gates[:])
         nc.sync.dma_start(out[0, :P, :], maps[0][:])
 
-        for h in range(HALVES):
-            biased = keep.tile([P, 2, P], F32, name=f"biased{h}")
-            sums = bank(f"sums{h}", [P, 2, P], 2 + h)
-            for i in range(2):
-                c = 2 * h + i
-                for g in reversed(range(PASSES)):
-                    nc.tensor.matmul_mx(
-                        out=sums[:, i, :],
-                        lhsT=k_codes(c * P, (c + 1) * P, g),
-                        lhsT_scale=k_planes[g][:, c * P : (c + 1) * P],
-                        rhs=q_codes[1, g],
-                        rhs_scale=q_scales[1, g],
-                        start=(g == PASSES - 1),
-                        stop=(g == 0),
-                    )
-            for i in range(2):
-                c = 2 * h + i
-                nc.scalar.activation(biased[:, i, :], sums[:, i, :], ACT.Identity, bias=kb_cols[:, c : c + 1])
-            turned = bank(f"turned{h}", [P, 2, P], 7)
-            for i in range(2):
-                nc.tensor.transpose(turned[:, i, :], biased[:, i, :], ident[:])
-            gates = keep.tile([P, HALF], F32, name=f"gates{h}")
-            nc.scalar.activation(gates[:], turned[:].rearrange("p c s -> p (c s)"), ACT.Sigmoid, bias=neg_th[:, 1:2])
-            nc.scalar.activation(maps[1][:].indirect(part_list(h * HALF, (h + 1) * HALF)), gates[:], ACT.Copy)
+        other_low_biased = [place("other_low_biased0", [P, P], F32, 26880), keep.tile([P, P], F32, name="other_low_biased1")]
+        for i in range(2):
+            nc.scalar.activation(other_low_biased[i][:], other_low[i][:], ACT.Identity, bias=low_cols[:, i : i + 1])
+        other_high_gates = place("other_high_gates", [P, HALF], F32, 8192)
+        nc.scalar.activation(other_high_gates[:], other_high_biased[:], ACT.Sigmoid, bias=neg_th[:, 1:2])
+        nc.scalar.activation(maps[1][:].indirect(part_list(HALF, N)), other_high_gates[:], ACT.Copy)
+        other_turned = bank("other_turned", [P, 2, P], 6)
+        for i in range(2):
+            nc.tensor.transpose(other_turned[:, i, :], other_low_biased[i][:], ident[:])
+        other_low_gates = place("other_low_gates", [P, HALF], F32, 12288)
+        nc.scalar.activation(other_low_gates[:], other_turned[:].rearrange("p c s -> p (c s)"), ACT.Sigmoid, bias=neg_th[:, 1:2])
+        nc.scalar.activation(maps[1][:].indirect(part_list(0, HALF)), other_low_gates[:], ACT.Copy)
         nc.sync.dma_start(out[0, P:, :], maps[1][:])

@@ -23,10 +23,7 @@ Q_TILES = NQ // P
 HALF = N // 2
 BANK_BYTES = 2048
 KB_ROW = P - 1
-SCALE_ROW = 32
-ROWS = 16
-KB_SPLIT = 1024
-MAP_SPLIT = 640
+SCALE_ROW = P - 16
 FLOPS = 2 * NQ * N * D
 
 
@@ -44,18 +41,21 @@ def tile_attend_sigscat_topk_kernel(tc, qT, k_words, k_scales, kb, th, offs, out
         def place(name, shape, dtype, at):
             return placed.tile(shape, dtype, name=name, offset=at, align_bytes=64)
 
-        scale_pool = place("scale_pool", [P, T // 4], I32, 15360)
-        nc.sync.dma_start(
-            scale_pool[SCALE_ROW : SCALE_ROW + PASSES * ROWS, :], k_scales.bitcast(I32).rearrange("o f t -> (o f) t")
-        )
+        scale_pool = keep.tile([P, PASSES * T // 4], I32, name="scale_pool")
+
+        def load_scales(g):
+            nc.sync.dma_start(scale_pool[SCALE_ROW:, g * T // 4 : (g + 1) * T // 4], k_scales.bitcast(I32)[g])
+
+        load_scales(0)
         offsets = lists.tile([P, N // 16], U16, name="offsets")
         nc.sync.dma_start(offsets[:], offs)
+        load_scales(1)
 
         def part_list(lo, hi):
             return offsets[:, lo // 16 : hi // 16]
 
         kb_pool = keep.tile([P, T], F32, name="kb_pool")
-        nc.scalar.dma_start(kb_pool[KB_ROW : KB_ROW + 1, :], kb[0:1, :])
+        nc.sync.dma_start(kb_pool[KB_ROW : KB_ROW + 1, :], kb[0:1, :])
         word_pool = keep.tile([P, T], I32, name="word_pool")
         nc.sync.dma_start(word_pool[:], k_words[0].rearrange("p t b -> p (t b)").bitcast(I32))
         th_rows = keep.tile([P, P], F32, name="th_rows")
@@ -63,6 +63,8 @@ def tile_attend_sigscat_topk_kernel(tc, qT, k_words, k_scales, kb, th, offs, out
         q_rows = qT[0].rearrange("(g p j) w -> g p j w", g=PASSES, j=PACK)
         first_pass = keep.tile([P, PACK, NQ], F32, name="first_pass")
         nc.sync.dma_start(first_pass[:], q_rows[0])
+        second_pass = place("second_pass", [P, PACK, NQ], F32, 12288)
+        nc.sync.dma_start(second_pass[:], q_rows[1])
 
         def zero_on_vector(tile, rows, lo, hi):
             nc.vector.memset(tile[rows, lo : hi - 1], 0)
@@ -74,37 +76,26 @@ def tile_attend_sigscat_topk_kernel(tc, qT, k_words, k_scales, kb, th, offs, out
         nc.scalar.activation(warm_out[:], warm_in[:], ACT.Sigmoid)
 
         planes = keep.tile([P, PASSES * N // 4], I32, name="planes", align_bytes=64)
-        zero_on_vector(scale_pool, slice(0, SCALE_ROW), 0, T // 4)
-        zero_on_vector(kb_pool, slice(0, KB_ROW), 0, KB_SPLIT)
-        nc.gpsimd.memset(scale_pool[SCALE_ROW + PASSES * ROWS :, :], 0)
-        nc.gpsimd.memset(kb_pool[:KB_ROW, KB_SPLIT:], 0.0)
-        nc.gpsimd.memset(planes[:], 0)
+        zero_on_vector(kb_pool, slice(0, KB_ROW), 0, T // 2)
+        zero_on_vector(scale_pool, slice(0, SCALE_ROW), 0, 3 * T // 8)
+        nc.gpsimd.memset(kb_pool[:KB_ROW, T // 2 :], 0.0)
+        nc.gpsimd.memset(scale_pool[:SCALE_ROW, 3 * T // 8 :], 0)
         ident = keep.tile([P, P], F32, name="ident")
         make_identity(nc, ident[:])
-        nc.gpsimd.memset(th_rows[: P - Q_TILES, :], 0.0)
         zeros = keep.tile([P, P], F32, name="zeros")
         nc.gpsimd.memset(zeros[:], 0.0)
+        nc.gpsimd.memset(th_rows[: P - Q_TILES, :], 0.0)
+        nc.gpsimd.memset(planes[:], 0)
+        maps = {0: keep.tile([P, T], F32, name="map0")}
+        nc.gpsimd.memset(maps[0][:], 0.0)
 
-        listed_bytes = keep.tile([P, N], U8, name="listed_bytes")
-        nc.vector.tensor_copy(listed_bytes[:], scale_pool[:].bitcast(U8).indirect(offsets[:]))
-
-        def move_rows(g, r):
-            first = SCALE_ROW + g * ROWS
-            nc.sync.dma_start(
-                planes[r:P:32, g * N // 4 : (g + 1) * N // 4], listed_bytes[:].bitcast(I32)[first + r : first + ROWS : 4, :]
-            )
-
-        moves = [(g, r) for g in range(PASSES) for r in range(4)]
-        move_rows(*moves[0])
-        second_pass = place("second_pass", [P, PACK, NQ], F32, 12288)
-        nc.sync.dma_start(second_pass[:], q_rows[1])
-        for g, r in moves[1:]:
-            move_rows(g, r)
+        listed_bytes = keep.tile([P, PASSES * N], U8, name="listed_bytes")
+        for g in range(PASSES):
+            window = scale_pool[:].bitcast(U8)[:, g * T : (g + 1) * T]
+            nc.vector.tensor_copy(listed_bytes[:, g * N : (g + 1) * N], window.indirect(offsets[:]))
+        for r in range(4):
+            nc.sync.dma_start(planes[r:P:32, :], listed_bytes[:].bitcast(I32)[SCALE_ROW + r : P : 4, :])
         k_planes = [planes[:].bitcast(U8)[:, g * N : (g + 1) * N] for g in range(PASSES)]
-
-        maps = {0: place("map0", [P, T], F32, 16384)}
-        zero_on_vector(maps[0], slice(0, P), 0, MAP_SPLIT)
-        nc.gpsimd.memset(maps[0][:, MAP_SPLIT:], 0.0)
 
         q_raw = {(t, g): (first_pass, second_pass)[g][:, :, t * P : (t + 1) * P] for t in range(Q_TILES) for g in range(PASSES)}
 
@@ -214,7 +205,8 @@ def tile_attend_sigscat_topk_kernel(tc, qT, k_words, k_scales, kb, th, offs, out
         for g in range(PASSES):
             by_query(first_sums[:], 0, 0, P, g)
             by_query(high_sums[:], 0, HALF, N, g)
-            by_slot(second_sums[:], 0, P, g)
+        for g in reversed(range(PASSES)):
+            by_slot(second_sums[:], 0, P, g, first=PASSES - 1)
         first_biased = place("first_biased", [P, P], F32, 12288)
         high_biased = place("high_biased", [P, HALF], F32, 13312)
         first_gates = keep.tile([P, P], F32, name="first_gates")
@@ -245,15 +237,15 @@ def tile_attend_sigscat_topk_kernel(tc, qT, k_words, k_scales, kb, th, offs, out
         nc.sync.dma_start(out[0, :P, :], maps[0][:])
 
         other_low_biased = [place("other_low_biased0", [P, P], F32, 26880), keep.tile([P, P], F32, name="other_low_biased1")]
-        for i in range(2):
-            nc.scalar.activation(other_low_biased[i][:], other_low[i][:], ACT.Identity, bias=low_cols[:, i : i + 1])
-        other_high_gates = place("other_high_gates", [P, HALF], F32, 8192)
+        nc.scalar.activation(other_low_biased[0][:], other_low[0][:], ACT.Identity, bias=low_cols[:, 0:1])
+        other_high_gates = place("other_high_gates", [P, HALF], F32, 25856)
         nc.scalar.activation(other_high_gates[:], other_high_biased[:], ACT.Sigmoid, bias=neg_th[:, 1:2])
-        nc.scalar.activation(maps[1][:].indirect(part_list(HALF, N)), other_high_gates[:], ACT.Copy)
+        nc.scalar.activation(other_low_biased[1][:], other_low[1][:], ACT.Identity, bias=low_cols[:, 1:2])
         other_turned = bank("other_turned", [P, 2, P], 6)
         for i in range(2):
             nc.tensor.transpose(other_turned[:, i, :], other_low_biased[i][:], ident[:])
-        other_low_gates = place("other_low_gates", [P, HALF], F32, 12288)
+        other_low_gates = keep.tile([P, HALF], F32, name="other_low_gates")
         nc.scalar.activation(other_low_gates[:], other_turned[:].rearrange("p c s -> p (c s)"), ACT.Sigmoid, bias=neg_th[:, 1:2])
-        nc.scalar.activation(maps[1][:].indirect(part_list(0, HALF)), other_low_gates[:], ACT.Copy)
+        nc.scalar.activation(maps[1][:].indirect(part_list(HALF, N)), other_high_gates[:], ACT.Copy)
+        nc.vector.tensor_copy(maps[1][:].indirect(part_list(0, HALF)), other_low_gates[:])
         nc.sync.dma_start(out[0, P:, :], maps[1][:])

@@ -155,7 +155,7 @@ def tile_attend_sigscat_topk_kernel(tc, qT, k_words, k_scales, kb, th, offs, out
         rounded = {
             (0, 0): place("q_bf00", [P, P, PACK], BF16, 8192),
             (1, 0): place("q_bf10", [P, P, PACK], BF16, 9216),
-            (0, 1): place("q_bf01", [P, P, PACK], BF16, 8192),
+            (0, 1): place("q_bf01", [P, P, PACK], BF16, 23808),
             (1, 1): place("q_bf11", [P, P, PACK], BF16, 7168),
         }
         th_turned = bank("th_turned", [P, P], 4)
@@ -164,14 +164,14 @@ def tile_attend_sigscat_topk_kernel(tc, qT, k_words, k_scales, kb, th, offs, out
         nc.scalar.activation(neg_th[:], th_turned[:, P - Q_TILES :], ACT.Copy, scale=-1.0)
         round_q(nc.scalar.copy, 0, 0, rounded[0, 0])
         round_q(nc.scalar.copy, 1, 0, rounded[1, 0])
-        quantize_q(0, 0, rounded[0, 0], place("q_codes00", [P, P], U32, 25600))
+        quantize_q(0, 0, rounded[0, 0], place("q_codes00", [P, P], U32, 24832))
         for lo in range(0, P, P // 2):
             round_q(nc.vector.tensor_copy, 0, 1, rounded[0, 1], lo, lo + P // 2)
         round_q(nc.scalar.copy, 1, 1, rounded[1, 1])
         high_rows = place("high_rows", [P, HALF], F32, 14336)
         nc.scalar.copy(high_rows[:], spread[:].rearrange("p c s -> p (c s)"))
         quantize_q(0, 1, rounded[0, 1], keep.tile([P, P], U32, name="q_codes01", align_bytes=64), parts=2)
-        quantize_q(1, 0, rounded[1, 0], place("q_codes10", [P, P], U32, 8704))
+        quantize_q(1, 0, rounded[1, 0], place("q_codes10", [P, P], U32, 23808))
         quantize_q(1, 1, rounded[1, 1], keep.tile([P, P], U32, name="q_codes11", align_bytes=64))
         maps[1] = place("map1", [P, T], F32, 0)
         for lo in range(0, T, N):

@@ -177,6 +177,10 @@ def tile_attend_sigscat_topk_kernel(tc, qT, k_words, k_scales, kb, th, offs, out
         for lo in range(0, T, N):
             nc.gpsimd.memset(maps[1][:, lo : lo + N], 0.0)
 
+        def store(t):
+            for lo in range(0, T, T // 2):
+                nc.sync.dma_start(out[0, t * P : (t + 1) * P, lo : lo + T // 2], maps[t][:, lo : lo + T // 2])
+
         def by_query(sums, t, lo, hi, g, first=0):
             nc.tensor.matmul_mx(
                 out=sums,
@@ -234,7 +238,7 @@ def tile_attend_sigscat_topk_kernel(tc, qT, k_words, k_scales, kb, th, offs, out
         other_high_biased = place("other_high_biased", [P, HALF], F32, 12288)
         nc.vector.tensor_tensor(other_high_biased[:], other_high[:], high_rows[:], ADD)
         nc.vector.tensor_copy(maps[0][:].indirect(part_list(P, N)), rest_gates[:])
-        nc.sync.dma_start(out[0, :P, :], maps[0][:])
+        store(0)
 
         other_low_biased = [place("other_low_biased0", [P, P], F32, 26880), keep.tile([P, P], F32, name="other_low_biased1")]
         nc.scalar.activation(other_low_biased[0][:], other_low[0][:], ACT.Identity, bias=low_cols[:, 0:1])
@@ -248,4 +252,4 @@ def tile_attend_sigscat_topk_kernel(tc, qT, k_words, k_scales, kb, th, offs, out
         nc.scalar.activation(other_low_gates[:], other_turned[:].rearrange("p c s -> p (c s)"), ACT.Sigmoid, bias=neg_th[:, 1:2])
         nc.scalar.activation(maps[1][:].indirect(part_list(HALF, N)), other_high_gates[:], ACT.Copy)
         nc.vector.tensor_copy(maps[1][:].indirect(part_list(0, HALF)), other_low_gates[:])
-        nc.sync.dma_start(out[0, P:, :], maps[1][:])
+        store(1)

@@ -21,9 +21,12 @@ K_PASS = P * PACK
 PASSES = D // K_PASS
 Q_TILES = NQ // P
 HALF = N // 2
+QUAD = 32
+SCALE_ROWS = 16
 BANK_BYTES = 2048
 KB_ROW = P - 1
-SCALE_ROW = P - 16
+KB_ON_VECTOR = 768
+MAP_ON_VECTOR = 384
 FLOPS = 2 * NQ * N * D
 
 
@@ -41,10 +44,11 @@ def tile_attend_sigscat_topk_kernel(tc, qT, k_words, k_scales, kb, th, offs, out
         def place(name, shape, dtype, at):
             return placed.tile(shape, dtype, name=name, offset=at, align_bytes=64)
 
-        scale_pool = keep.tile([P, PASSES * T // 4], I32, name="scale_pool")
+        scale_pool = keep.tile([P, T // 4], I32, name="scale_pool")
 
         def load_scales(g):
-            nc.sync.dma_start(scale_pool[SCALE_ROW:, g * T // 4 : (g + 1) * T // 4], k_scales.bitcast(I32)[g])
+            end = (g + 1) * P // PASSES
+            nc.sync.dma_start(scale_pool[end - SCALE_ROWS : end, :], k_scales.bitcast(I32)[g])
 
         load_scales(0)
         offsets = lists.tile([P, N // 16], U16, name="offsets")
@@ -61,10 +65,16 @@ def tile_attend_sigscat_topk_kernel(tc, qT, k_words, k_scales, kb, th, offs, out
         th_rows = keep.tile([P, P], F32, name="th_rows")
         nc.sync.dma_start(th_rows[P - Q_TILES :, :], th[0].rearrange("(t p) o -> t (p o)", p=P))
         q_rows = qT[0].rearrange("(g p j) w -> g p j w", g=PASSES, j=PACK)
-        first_pass = keep.tile([P, PACK, NQ], F32, name="first_pass")
+        first_pass = place("first_pass", [P, PACK, NQ], F32, 0)
         nc.sync.dma_start(first_pass[:], q_rows[0])
-        second_pass = place("second_pass", [P, PACK, NQ], F32, 12288)
-        nc.sync.dma_start(second_pass[:], q_rows[1])
+        q_raw = {(t, 0): first_pass[:, :, t * P : (t + 1) * P] for t in range(Q_TILES)}
+
+        def load_closing(t, at):
+            tile = place(f"q_raw{t}1", [P, PACK, P], F32, at)
+            nc.sync.dma_start(tile[:], q_rows[1][:, :, t * P : (t + 1) * P])
+            q_raw[t, 1] = tile[:]
+
+        load_closing(0, 6144)
 
         def zero_on_vector(tile, rows, lo, hi):
             nc.vector.memset(tile[rows, lo : hi - 1], 0)
@@ -75,42 +85,43 @@ def tile_attend_sigscat_topk_kernel(tc, qT, k_words, k_scales, kb, th, offs, out
         nc.gpsimd.memset(warm_in[:], 0.0)
         nc.scalar.activation(warm_out[:], warm_in[:], ACT.Sigmoid)
 
-        planes = keep.tile([P, PASSES * N // 4], I32, name="planes", align_bytes=64)
-        zero_on_vector(kb_pool, slice(0, KB_ROW), 0, T // 2)
-        zero_on_vector(scale_pool, slice(0, SCALE_ROW), 0, 3 * T // 8)
-        nc.gpsimd.memset(kb_pool[:KB_ROW, T // 2 :], 0.0)
-        nc.gpsimd.memset(scale_pool[:SCALE_ROW, 3 * T // 8 :], 0)
+        for g in range(PASSES):
+            zero_on_vector(scale_pool, slice(g * P // PASSES, (g + 1) * P // PASSES - SCALE_ROWS), 0, T // 4)
+        zero_on_vector(kb_pool, slice(0, KB_ROW), 0, KB_ON_VECTOR)
+        nc.gpsimd.memset(kb_pool[:KB_ROW, KB_ON_VECTOR:], 0.0)
         ident = keep.tile([P, P], F32, name="ident")
         make_identity(nc, ident[:])
+        planes = keep.tile([P, PASSES * N // 4], I32, name="planes", align_bytes=64)
+        nc.gpsimd.memset(planes[:], 0)
+        nc.gpsimd.memset(th_rows[: P - Q_TILES, :], 0.0)
         zeros = keep.tile([P, P], F32, name="zeros")
         nc.gpsimd.memset(zeros[:], 0.0)
-        nc.gpsimd.memset(th_rows[: P - Q_TILES, :], 0.0)
-        nc.gpsimd.memset(planes[:], 0)
-        maps = {0: keep.tile([P, T], F32, name="map0")}
-        nc.gpsimd.memset(maps[0][:], 0.0)
 
-        listed_bytes = keep.tile([P, PASSES * N], U8, name="listed_bytes")
+        listed_bytes = place("listed_bytes", [P, N], U8, 8192)
+        nc.vector.tensor_copy(listed_bytes[:], scale_pool[:].bitcast(U8).indirect(offsets[:]))
+        paired = keep.tile([P, PASSES * N // 4], I32, name="paired")
         for g in range(PASSES):
-            window = scale_pool[:].bitcast(U8)[:, g * T : (g + 1) * T]
-            nc.vector.tensor_copy(listed_bytes[:, g * N : (g + 1) * N], window.indirect(offsets[:]))
+            end = (g + 1) * P // PASSES
+            nc.vector.tensor_copy(paired[P - QUAD :, g * N // 4 : (g + 1) * N // 4], listed_bytes[:].bitcast(I32)[end - QUAD : end, :])
         for r in range(4):
-            nc.sync.dma_start(planes[r:P:32, :], listed_bytes[:].bitcast(I32)[SCALE_ROW + r : P : 4, :])
+            nc.sync.dma_start(planes[r:P:QUAD, :], paired[P - SCALE_ROWS + r : P : 4, :])
+        load_closing(1, 4096)
+        maps = {0: place("map0", [P, T], F32, 8192)}
+        zero_on_vector(maps[0], slice(0, P), 0, MAP_ON_VECTOR)
+        nc.gpsimd.memset(maps[0][:, MAP_ON_VECTOR:], 0.0)
         k_planes = [planes[:].bitcast(U8)[:, g * N : (g + 1) * N] for g in range(PASSES)]
 
-        q_raw = {(t, g): (first_pass, second_pass)[g][:, :, t * P : (t + 1) * P] for t in range(Q_TILES) for g in range(PASSES)}
-
-        kb_listed = place("kb_listed", [P, N], F32, 7680)
+        kb_listed = place("kb_listed", [P, N], F32, 16896)
         for lo in range(0, N, HALF):
             nc.scalar.activation(kb_listed[:, lo : lo + HALF], kb_pool[:].indirect(part_list(lo, lo + HALF)), ACT.Copy)
         low_cols = keep.tile([P, 2], F32, name="low_cols")
         high_cols = keep.tile([P, 2], F32, name="high_cols")
-        first_rows = place("first_rows", [P, P], F32, 26624)
+        first_rows = keep.tile([P, P], F32, name="first_rows")
 
         def turn_bias(h, cols, b):
             turned = bank(f"kb_turned{h}", [P, 2, P], b)
             for i in range(2):
-                c = 2 * h + i
-                nc.tensor.transpose(turned[:, i, :], kb_listed[:, c * P : (c + 1) * P], ident[:])
+                nc.tensor.transpose(turned[:, i, :], kb_listed[:, (2 * h + i) * P : (2 * h + i + 1) * P], ident[:])
             nc.scalar.copy(cols, turned[:, :, KB_ROW])
 
         turn_bias(0, low_cols[:], 4)
@@ -122,27 +133,21 @@ def tile_attend_sigscat_topk_kernel(tc, qT, k_words, k_scales, kb, th, offs, out
         for i in range(2):
             nc.tensor.transpose(spread[:, i, :], high_cols[:, i : i + 1].to_broadcast([P, P]), ident[:])
 
-        q_codes, q_scales, k_parted, word_pairs = {}, {}, {}, {}
+        q_codes, q_scales, k_parted, word_pairs, rounded = {}, {}, {}, {}, {}
 
-        def round_q(engine_copy, t, g, rounded, lo=0, hi=P):
+        def round_q(engine_copy, t, g, lo=0, hi=P):
             engine_copy(
-                rounded[:, lo:hi].rearrange("p (c i) j -> p c j i", i=4),
+                rounded[t, g][:, lo:hi].rearrange("p (c i) j -> p c j i", i=4),
                 q_raw[t, g][:, :, lo:hi].rearrange("p j (c i) -> p c j i", i=4),
             )
 
-        def quantize_q(t, g, rounded, codes, parts=1):
+        def quantize_q(t, g, codes):
             scales = keep.tile([P, P], U8, name=f"q_scales{t}{g}", align_bytes=64)
-            width = P // parts
-            for lo in range(0, P, width):
-                nc.vector.quantize_mx(
-                    out=codes[:, lo : lo + width].bitcast(FP8X4),
-                    scales=scales[:, lo : lo + width],
-                    in_=rounded[:, lo : lo + width].rearrange("p w j -> p (w j)"),
-                )
+            nc.vector.quantize_mx(out=codes[:].bitcast(FP8X4), scales=scales[:], in_=rounded[t, g][:].rearrange("p w j -> p (w j)"))
             q_codes[t, g], q_scales[t, g] = codes[:].bitcast(FP8X4), scales[:]
 
         for h in range(2):
-            word_pairs[h] = place(f"word_pairs{h}", [P, HALF], U32, 24576 + 1024 * h)
+            word_pairs[h] = keep.tile([P, HALF], U32, name=f"word_pairs{h}")
             nc.vector.tensor_copy(word_pairs[h][:], word_pool[:].bitcast(U32).indirect(part_list(h * HALF, (h + 1) * HALF)))
         for h in range(2):
             k_parted[h] = keep.tile([P, PASSES, HALF], U16, name=f"k_codes{h}", align_bytes=64)
@@ -152,30 +157,23 @@ def tile_attend_sigscat_topk_kernel(tc, qT, k_words, k_scales, kb, th, offs, out
             h = lo // HALF
             return k_parted[h][:, g, lo - h * HALF : hi - h * HALF].bitcast(FP4X4)
 
-        rounded = {
-            (0, 0): place("q_bf00", [P, P, PACK], BF16, 8192),
-            (1, 0): place("q_bf10", [P, P, PACK], BF16, 9216),
-            (0, 1): place("q_bf01", [P, P, PACK], BF16, 23808),
-            (1, 1): place("q_bf11", [P, P, PACK], BF16, 7168),
-        }
         th_turned = bank("th_turned", [P, P], 4)
         nc.tensor.transpose(th_turned[:], th_rows[:], ident[:])
         neg_th = keep.tile([P, Q_TILES], F32, name="neg_th")
         nc.scalar.activation(neg_th[:], th_turned[:, P - Q_TILES :], ACT.Copy, scale=-1.0)
-        round_q(nc.scalar.copy, 0, 0, rounded[0, 0])
-        round_q(nc.scalar.copy, 1, 0, rounded[1, 0])
-        quantize_q(0, 0, rounded[0, 0], place("q_codes00", [P, P], U32, 24832))
-        for lo in range(0, P, P // 2):
-            round_q(nc.vector.tensor_copy, 0, 1, rounded[0, 1], lo, lo + P // 2)
-        round_q(nc.scalar.copy, 1, 1, rounded[1, 1])
-        high_rows = place("high_rows", [P, HALF], F32, 14336)
-        nc.scalar.copy(high_rows[:], spread[:].rearrange("p c s -> p (c s)"))
-        quantize_q(0, 1, rounded[0, 1], keep.tile([P, P], U32, name="q_codes01", align_bytes=64), parts=2)
-        quantize_q(1, 0, rounded[1, 0], place("q_codes10", [P, P], U32, 23808))
-        quantize_q(1, 1, rounded[1, 1], keep.tile([P, P], U32, name="q_codes11", align_bytes=64))
-        maps[1] = place("map1", [P, T], F32, 0)
-        for lo in range(0, T, N):
-            nc.gpsimd.memset(maps[1][:, lo : lo + N], 0.0)
+        rounded[0, 0] = place("q_bf00", [P, P, PACK], BF16, 16384)
+        round_q(nc.scalar.copy, 0, 0)
+        rounded[1, 0] = place("q_bf10", [P, P, PACK], BF16, 17408)
+        round_q(nc.scalar.copy, 1, 0)
+        rounded[0, 1] = place("q_bf01", [P, P, PACK], BF16, 28672)
+        round_q(nc.vector.tensor_copy, 0, 1)
+        for g in range(PASSES):
+            quantize_q(0, g, keep.tile([P, P], U32, name=f"q_codes0{g}", align_bytes=64))
+        quantize_q(1, 0, place("q_codes10", [P, P], U32, 28672))
+        high_rows = place("high_rows", [P, HALF], F32, 29184)
+        nc.vector.tensor_copy(high_rows[:], spread[:].rearrange("p c s -> p (c s)"))
+        rounded[1, 1] = place("q_bf11", [P, P, PACK], BF16, 18432)
+        round_q(nc.scalar.copy, 1, 1)
 
         def store(t):
             for lo in range(0, T, T // 2):
@@ -211,20 +209,21 @@ def tile_attend_sigscat_topk_kernel(tc, qT, k_words, k_scales, kb, th, offs, out
             by_query(high_sums[:], 0, HALF, N, g)
         for g in reversed(range(PASSES)):
             by_slot(second_sums[:], 0, P, g, first=PASSES - 1)
-        first_biased = place("first_biased", [P, P], F32, 12288)
-        high_biased = place("high_biased", [P, HALF], F32, 13312)
-        first_gates = keep.tile([P, P], F32, name="first_gates")
+        first_biased = keep.tile([P, P], F32, name="first_biased")
+        high_biased = place("high_biased", [P, HALF], F32, 4096)
+        first_gates = place("first_gates", [P, P], F32, 5120)
         rest_gates = keep.tile([P, N - P], F32, name="rest_gates")
         nc.vector.tensor_tensor(first_biased[:], first_sums[:], first_rows[:], ADD)
+        quantize_q(1, 1, keep.tile([P, P], U32, name="q_codes11", align_bytes=64))
+        maps[1] = place("map1", [P, T], F32, 18432)
+        for lo in range(0, T, N):
+            nc.gpsimd.memset(maps[1][:, lo : lo + N], 0.0)
         nc.vector.tensor_tensor(high_biased[:], high_sums[:], high_rows[:], ADD)
         nc.scalar.activation(first_gates[:], first_biased[:], ACT.Sigmoid, bias=neg_th[:, 0:1])
-        second_biased = place("second_biased", [P, P], F32, 26368)
+        second_biased = place("second_biased", [P, P], F32, 5632)
         nc.scalar.activation(second_biased[:], second_sums[:], ACT.Identity, bias=low_cols[:, 1:2])
         nc.scalar.activation(rest_gates[:, P:], high_biased[:], ACT.Sigmoid, bias=neg_th[:, 0:1])
-        other_low = [bank("other_low0", [P, P], 4)]
         other_high = bank("other_high", [P, HALF], 3)
-        for g in reversed(range(PASSES)):
-            by_slot(other_low[0][:], 1, 0, g, first=PASSES - 1)
         for g in reversed(range(PASSES)):
             by_query(other_high[:], 1, HALF, N, g, first=PASSES - 1)
         second_turned = bank("second_turned", [P, P], 5)
@@ -232,17 +231,18 @@ def tile_attend_sigscat_topk_kernel(tc, qT, k_words, k_scales, kb, th, offs, out
         nc.scalar.activation(rest_gates[:, :P], second_turned[:], ACT.Sigmoid, bias=neg_th[:, 0:1])
         nc.vector.tensor_tensor(maps[0][:].indirect(part_list(0, P)), first_gates[:], zeros[:], ADD)
 
-        other_low.append(bank("other_low1", [P, P], 2))
-        for g in range(PASSES):
-            by_slot(other_low[1][:], 1, P, g)
-        other_high_biased = place("other_high_biased", [P, HALF], F32, 12288)
+        other_low = [bank("other_low0", [P, P], 4), bank("other_low1", [P, P], 2)]
+        for i in range(2):
+            for g in reversed(range(PASSES)):
+                by_slot(other_low[i][:], 1, i * P, g, first=PASSES - 1)
+        other_high_biased = keep.tile([P, HALF], F32, name="other_high_biased")
         nc.vector.tensor_tensor(other_high_biased[:], other_high[:], high_rows[:], ADD)
         nc.vector.tensor_copy(maps[0][:].indirect(part_list(P, N)), rest_gates[:])
         store(0)
 
-        other_low_biased = [place("other_low_biased0", [P, P], F32, 26880), keep.tile([P, P], F32, name="other_low_biased1")]
+        other_low_biased = [keep.tile([P, P], F32, name=f"other_low_biased{i}") for i in range(2)]
         nc.scalar.activation(other_low_biased[0][:], other_low[0][:], ACT.Identity, bias=low_cols[:, 0:1])
-        other_high_gates = place("other_high_gates", [P, HALF], F32, 25856)
+        other_high_gates = keep.tile([P, HALF], F32, name="other_high_gates")
         nc.scalar.activation(other_high_gates[:], other_high_biased[:], ACT.Sigmoid, bias=neg_th[:, 1:2])
         nc.scalar.activation(other_low_biased[1][:], other_low[1][:], ACT.Identity, bias=low_cols[:, 1:2])
         other_turned = bank("other_turned", [P, 2, P], 6)

@@ -22,11 +22,9 @@ PASSES = D // K_PASS
 Q_TILES = NQ // P
 HALF = N // 2
 QUAD = 32
-SCALE_ROWS = 16
 BANK_BYTES = 2048
 KB_ROW = P - 1
-KB_ON_VECTOR = 768
-MAP_ON_VECTOR = 384
+KB_ON_VECTOR = 1024
 FLOPS = 2 * NQ * N * D
 
 
@@ -46,14 +44,9 @@ def tile_attend_sigscat_topk_kernel(tc, qT, k_words, k_scales, kb, th, offs, out
 
         scale_pool = keep.tile([P, T // 4], I32, name="scale_pool")
 
-        def load_scales(g):
-            end = (g + 1) * P // PASSES
-            nc.sync.dma_start(scale_pool[end - SCALE_ROWS : end, :], k_scales.bitcast(I32)[g])
-
-        load_scales(0)
+        nc.sync.dma_start(scale_pool[P - QUAD :, :], k_scales.bitcast(I32).rearrange("g f w -> f g w"))
         offsets = lists.tile([P, N // 16], U16, name="offsets")
         nc.sync.dma_start(offsets[:], offs)
-        load_scales(1)
 
         def part_list(lo, hi):
             return offsets[:, lo // 16 : hi // 16]
@@ -85,8 +78,7 @@ def tile_attend_sigscat_topk_kernel(tc, qT, k_words, k_scales, kb, th, offs, out
         nc.gpsimd.memset(warm_in[:], 0.0)
         nc.scalar.activation(warm_out[:], warm_in[:], ACT.Sigmoid)
 
-        for g in range(PASSES):
-            zero_on_vector(scale_pool, slice(g * P // PASSES, (g + 1) * P // PASSES - SCALE_ROWS), 0, T // 4)
+        zero_on_vector(scale_pool, slice(0, P - QUAD), 0, T // 4)
         zero_on_vector(kb_pool, slice(0, KB_ROW), 0, KB_ON_VECTOR)
         nc.gpsimd.memset(kb_pool[:KB_ROW, KB_ON_VECTOR:], 0.0)
         ident = keep.tile([P, P], F32, name="ident")
@@ -97,25 +89,25 @@ def tile_attend_sigscat_topk_kernel(tc, qT, k_words, k_scales, kb, th, offs, out
         zeros = keep.tile([P, P], F32, name="zeros")
         nc.gpsimd.memset(zeros[:], 0.0)
 
-        listed_bytes = place("listed_bytes", [P, N], U8, 8192)
+        maps = {0: keep.tile([P, T], F32, name="map0")}
+        nc.gpsimd.memset(maps[0][:], 0.0)
+
+        listed_bytes = keep.tile([P, N], U8, name="listed_bytes")
         nc.vector.tensor_copy(listed_bytes[:], scale_pool[:].bitcast(U8).indirect(offsets[:]))
-        paired = keep.tile([P, PASSES * N // 4], I32, name="paired")
-        for g in range(PASSES):
-            end = (g + 1) * P // PASSES
-            nc.vector.tensor_copy(paired[P - QUAD :, g * N // 4 : (g + 1) * N // 4], listed_bytes[:].bitcast(I32)[end - QUAD : end, :])
-        for r in range(4):
-            nc.sync.dma_start(planes[r:P:QUAD, :], paired[P - SCALE_ROWS + r : P : 4, :])
+        for u in range(4):
+            rows = P - QUAD + 8 * u
+            nc.sync.dma_start(
+                planes[QUAD * u : QUAD * u + 4, :].rearrange("r (g w) -> r g w", g=PASSES),
+                listed_bytes[:].bitcast(I32)[rows : rows + 8, :],
+            )
         load_closing(1, 4096)
-        maps = {0: place("map0", [P, T], F32, 8192)}
-        zero_on_vector(maps[0], slice(0, P), 0, MAP_ON_VECTOR)
-        nc.gpsimd.memset(maps[0][:, MAP_ON_VECTOR:], 0.0)
         k_planes = [planes[:].bitcast(U8)[:, g * N : (g + 1) * N] for g in range(PASSES)]
 
-        kb_listed = place("kb_listed", [P, N], F32, 16896)
+        kb_listed = keep.tile([P, N], F32, name="kb_listed")
         for lo in range(0, N, HALF):
             nc.scalar.activation(kb_listed[:, lo : lo + HALF], kb_pool[:].indirect(part_list(lo, lo + HALF)), ACT.Copy)
         low_cols = keep.tile([P, 2], F32, name="low_cols")
-        high_cols = keep.tile([P, 2], F32, name="high_cols")
+        high_cols = place("high_cols", [P, 2, 320], F32, 17344)
         first_rows = keep.tile([P, P], F32, name="first_rows")
 
         def turn_bias(h, cols, b):
@@ -128,10 +120,10 @@ def tile_attend_sigscat_topk_kernel(tc, qT, k_words, k_scales, kb, th, offs, out
         spread = bank("first_spread", [P, P], 5)
         nc.tensor.transpose(spread[:], low_cols[:, 0:1].to_broadcast([P, P]), ident[:])
         nc.scalar.copy(first_rows[:], spread[:])
-        turn_bias(1, high_cols[:], 6)
+        turn_bias(1, high_cols[:, :, 0], 6)
         spread = bank("high_spread", [P, 2, P], 7)
         for i in range(2):
-            nc.tensor.transpose(spread[:, i, :], high_cols[:, i : i + 1].to_broadcast([P, P]), ident[:])
+            nc.tensor.transpose(spread[:, i, :], high_cols[:, i, 0:1].to_broadcast([P, P]), ident[:])
 
         q_codes, q_scales, k_parted, word_pairs, rounded = {}, {}, {}, {}, {}
 
@@ -162,17 +154,18 @@ def tile_attend_sigscat_topk_kernel(tc, qT, k_words, k_scales, kb, th, offs, out
         neg_th = keep.tile([P, Q_TILES], F32, name="neg_th")
         nc.scalar.activation(neg_th[:], th_turned[:, P - Q_TILES :], ACT.Copy, scale=-1.0)
         rounded[0, 0] = place("q_bf00", [P, P, PACK], BF16, 16384)
+        rounded[0, 1] = place("q_bf01", [P, P, PACK], BF16, 17408)
+        rounded[1, 0] = place("q_bf10", [P, P, PACK], BF16, 18432)
         round_q(nc.scalar.copy, 0, 0)
-        rounded[1, 0] = place("q_bf10", [P, P, PACK], BF16, 17408)
-        round_q(nc.scalar.copy, 1, 0)
-        rounded[0, 1] = place("q_bf01", [P, P, PACK], BF16, 28672)
-        round_q(nc.vector.tensor_copy, 0, 1)
+        round_q(nc.vector.tensor_copy, 0, 1, 0, P // 2)
+        round_q(nc.scalar.copy, 0, 1, P // 2, P)
         for g in range(PASSES):
             quantize_q(0, g, keep.tile([P, P], U32, name=f"q_codes0{g}", align_bytes=64))
-        quantize_q(1, 0, place("q_codes10", [P, P], U32, 28672))
-        high_rows = place("high_rows", [P, HALF], F32, 29184)
+        round_q(nc.scalar.copy, 1, 0)
+        high_rows = place("high_rows", [P, HALF], F32, 17408)
         nc.vector.tensor_copy(high_rows[:], spread[:].rearrange("p c s -> p (c s)"))
-        rounded[1, 1] = place("q_bf11", [P, P, PACK], BF16, 18432)
+        quantize_q(1, 0, keep.tile([P, P], U32, name="q_codes10", align_bytes=64))
+        rounded[1, 1] = place("q_bf11", [P, P, PACK], BF16, 19456)
         round_q(nc.scalar.copy, 1, 1)
 
         def store(t):
@@ -215,7 +208,7 @@ def tile_attend_sigscat_topk_kernel(tc, qT, k_words, k_scales, kb, th, offs, out
         rest_gates = keep.tile([P, N - P], F32, name="rest_gates")
         nc.vector.tensor_tensor(first_biased[:], first_sums[:], first_rows[:], ADD)
         quantize_q(1, 1, keep.tile([P, P], U32, name="q_codes11", align_bytes=64))
-        maps[1] = place("map1", [P, T], F32, 18432)
+        maps[1] = place("map1", [P, T], F32, 19456)
         for lo in range(0, T, N):
             nc.gpsimd.memset(maps[1][:, lo : lo + N], 0.0)
         nc.vector.tensor_tensor(high_biased[:], high_sums[:], high_rows[:], ADD)

@@ -25,6 +25,7 @@ QUAD = 32
 BANK_BYTES = 2048
 KB_ROW = P - 1
 KB_ON_VECTOR = 1024
+CLOSING_ON_VECTOR = 96
 FLOPS = 2 * NQ * N * D
 
 
@@ -86,7 +87,7 @@ def tile_attend_sigscat_topk_kernel(tc, qT, k_words, k_scales, kb, th, offs, out
         planes = keep.tile([P, PASSES * N // 4], I32, name="planes", align_bytes=64)
         nc.gpsimd.memset(planes[:], 0)
         nc.gpsimd.memset(th_rows[: P - Q_TILES, :], 0.0)
-        zeros = keep.tile([P, P], F32, name="zeros")
+        zeros = keep.tile([P, N - P], F32, name="zeros")
         nc.gpsimd.memset(zeros[:], 0.0)
 
         maps = {0: keep.tile([P, T], F32, name="map0")}
@@ -157,8 +158,8 @@ def tile_attend_sigscat_topk_kernel(tc, qT, k_words, k_scales, kb, th, offs, out
         rounded[0, 1] = place("q_bf01", [P, P, PACK], BF16, 17408)
         rounded[1, 0] = place("q_bf10", [P, P, PACK], BF16, 18432)
         round_q(nc.scalar.copy, 0, 0)
-        round_q(nc.vector.tensor_copy, 0, 1, 0, P // 2)
-        round_q(nc.scalar.copy, 0, 1, P // 2, P)
+        round_q(nc.vector.tensor_copy, 0, 1, 0, CLOSING_ON_VECTOR)
+        round_q(nc.scalar.copy, 0, 1, CLOSING_ON_VECTOR, P)
         for g in range(PASSES):
             quantize_q(0, g, keep.tile([P, P], U32, name=f"q_codes0{g}", align_bytes=64))
         round_q(nc.scalar.copy, 1, 0)
@@ -209,8 +210,7 @@ def tile_attend_sigscat_topk_kernel(tc, qT, k_words, k_scales, kb, th, offs, out
         nc.vector.tensor_tensor(first_biased[:], first_sums[:], first_rows[:], ADD)
         quantize_q(1, 1, keep.tile([P, P], U32, name="q_codes11", align_bytes=64))
         maps[1] = place("map1", [P, T], F32, 19456)
-        for lo in range(0, T, N):
-            nc.gpsimd.memset(maps[1][:, lo : lo + N], 0.0)
+        nc.gpsimd.memset(maps[1][:], 0.0)
         nc.vector.tensor_tensor(high_biased[:], high_sums[:], high_rows[:], ADD)
         nc.scalar.activation(first_gates[:], first_biased[:], ACT.Sigmoid, bias=neg_th[:, 0:1])
         second_biased = place("second_biased", [P, P], F32, 5632)
@@ -222,7 +222,7 @@ def tile_attend_sigscat_topk_kernel(tc, qT, k_words, k_scales, kb, th, offs, out
         second_turned = bank("second_turned", [P, P], 5)
         nc.tensor.transpose(second_turned[:], second_biased[:], ident[:])
         nc.scalar.activation(rest_gates[:, :P], second_turned[:], ACT.Sigmoid, bias=neg_th[:, 0:1])
-        nc.vector.tensor_tensor(maps[0][:].indirect(part_list(0, P)), first_gates[:], zeros[:], ADD)
+        nc.vector.tensor_tensor(maps[0][:].indirect(part_list(0, P)), first_gates[:], zeros[:, :P], ADD)
 
         other_low = [bank("other_low0", [P, P], 4), bank("other_low1", [P, P], 2)]
         for i in range(2):
@@ -230,7 +230,7 @@ def tile_attend_sigscat_topk_kernel(tc, qT, k_words, k_scales, kb, th, offs, out
                 by_slot(other_low[i][:], 1, i * P, g, first=PASSES - 1)
         other_high_biased = keep.tile([P, HALF], F32, name="other_high_biased")
         nc.vector.tensor_tensor(other_high_biased[:], other_high[:], high_rows[:], ADD)
-        nc.vector.tensor_copy(maps[0][:].indirect(part_list(P, N)), rest_gates[:])
+        nc.vector.tensor_tensor(maps[0][:].indirect(part_list(P, N)), rest_gates[:], zeros[:], ADD)
         store(0)
 
         other_low_biased = [keep.tile([P, P], F32, name=f"other_low_biased{i}") for i in range(2)]

@@ -107,7 +107,7 @@ def tile_attend_sigscat_topk_kernel(tc, qT, k_words, k_scales, kb, th, offs, out
         kb_listed = keep.tile([P, N], F32, name="kb_listed")
         for lo in range(0, N, HALF):
             nc.scalar.activation(kb_listed[:, lo : lo + HALF], kb_pool[:].indirect(part_list(lo, lo + HALF)), ACT.Copy)
-        low_cols = keep.tile([P, 2], F32, name="low_cols")
+        low_cols = place("low_cols", [P, 2], F32, 8192)
         high_cols = place("high_cols", [P, 2, 320], F32, 17344)
         first_rows = keep.tile([P, P], F32, name="first_rows")
 
@@ -217,8 +217,8 @@ def tile_attend_sigscat_topk_kernel(tc, qT, k_words, k_scales, kb, th, offs, out
         nc.scalar.activation(second_biased[:], second_sums[:], ACT.Identity, bias=low_cols[:, 1:2])
         nc.scalar.activation(rest_gates[:, P:], high_biased[:], ACT.Sigmoid, bias=neg_th[:, 0:1])
         other_high = bank("other_high", [P, HALF], 3)
-        for g in reversed(range(PASSES)):
-            by_query(other_high[:], 1, HALF, N, g, first=PASSES - 1)
+        for g in range(PASSES):
+            by_query(other_high[:], 1, HALF, N, g)
         second_turned = bank("second_turned", [P, P], 5)
         nc.tensor.transpose(second_turned[:], second_biased[:], ident[:])
         nc.scalar.activation(rest_gates[:, :P], second_turned[:], ACT.Sigmoid, bias=neg_th[:, 0:1])
@@ -233,14 +233,13 @@ def tile_attend_sigscat_topk_kernel(tc, qT, k_words, k_scales, kb, th, offs, out
         nc.vector.tensor_tensor(maps[0][:].indirect(part_list(P, N)), rest_gates[:], zeros[:], ADD)
         store(0)
 
-        other_low_biased = [keep.tile([P, P], F32, name=f"other_low_biased{i}") for i in range(2)]
-        nc.scalar.activation(other_low_biased[0][:], other_low[0][:], ACT.Identity, bias=low_cols[:, 0:1])
-        other_high_gates = keep.tile([P, HALF], F32, name="other_high_gates")
-        nc.scalar.activation(other_high_gates[:], other_high_biased[:], ACT.Sigmoid, bias=neg_th[:, 1:2])
-        nc.scalar.activation(other_low_biased[1][:], other_low[1][:], ACT.Identity, bias=low_cols[:, 1:2])
         other_turned = bank("other_turned", [P, 2, P], 6)
         for i in range(2):
-            nc.tensor.transpose(other_turned[:, i, :], other_low_biased[i][:], ident[:])
+            biased = keep.tile([P, P], F32, name=f"other_low_biased{i}")
+            nc.scalar.activation(biased[:], other_low[i][:], ACT.Identity, bias=low_cols[:, i : i + 1])
+            nc.tensor.transpose(other_turned[:, i, :], biased[:], ident[:])
+        other_high_gates = place("other_high_gates", [P, HALF], F32, 8192)
+        nc.scalar.activation(other_high_gates[:], other_high_biased[:], ACT.Sigmoid, bias=neg_th[:, 1:2])
         other_low_gates = keep.tile([P, HALF], F32, name="other_low_gates")
         nc.scalar.activation(other_low_gates[:], other_turned[:].rearrange("p c s -> p (c s)"), ACT.Sigmoid, bias=neg_th[:, 1:2])
         nc.scalar.activation(maps[1][:].indirect(part_list(HALF, N)), other_high_gates[:], ACT.Copy)

from contextlib import ExitStack

import concourse.mybir as mybir
from concourse.masks import make_identity

F32 = mybir.dt.float32
BF16 = mybir.dt.bfloat16
I32 = mybir.dt.int32
U32 = mybir.dt.uint32
U16 = mybir.dt.uint16
U8 = mybir.dt.uint8
FP8X4 = mybir.dt.float8_e4m3fn_x4
FP4X4 = mybir.dt.float4_e2m1fn_x4
ACT = mybir.ActivationFunctionType
ADD = mybir.AluOpType.add

P = 128
T, D, NQ, N = 2048, 1024, 256, 512
PACK = 4
K_PASS = P * PACK
PASSES = D // K_PASS
Q_TILES = NQ // P
HALF = N // 2
QUAD = 32
BANK_BYTES = 2048
KB_ROW = P - 1
KB_ON_VECTOR = 1024
CLOSING_ON_VECTOR = 96
FLOPS = 2 * NQ * N * D


def tile_attend_sigscat_topk_kernel(tc, qT, k_words, k_scales, kb, th, offs, out):
    nc = tc.nc
    with ExitStack() as ctx:
        lists = ctx.enter_context(tc.tile_pool(name="lists", bufs=1))
        keep = ctx.enter_context(tc.tile_pool(name="keep", bufs=1))
        placed = ctx.enter_context(tc.tile_pool(name="placed", bufs=1))
        psum = ctx.enter_context(tc.psum_pool(name="psum", bufs=1))

        def bank(name, shape, b):
            return psum.tile(shape, F32, name=name, offset=b * BANK_BYTES)

        def place(name, shape, dtype, at):
            return placed.tile(shape, dtype, name=name, offset=at, align_bytes=64)

        scale_pool = keep.tile([P, T // 4], I32, name="scale_pool")

        nc.sync.dma_start(scale_pool[P - QUAD :, :], k_scales.bitcast(I32).rearrange("g f w -> f g w"))
        offsets = lists.tile([P, N // 16], U16, name="offsets")
        nc.sync.dma_start(offsets[:], offs)

        def part_list(lo, hi):
            return offsets[:, lo // 16 : hi // 16]

        kb_pool = keep.tile([P, T], F32, name="kb_pool")
        nc.sync.dma_start(kb_pool[KB_ROW : KB_ROW + 1, :], kb[0:1, :])
        word_pool = keep.tile([P, T], I32, name="word_pool")
        nc.sync.dma_start(word_pool[:], k_words[0].rearrange("p t b -> p (t b)").bitcast(I32))
        th_rows = keep.tile([P, P], F32, name="th_rows")
        nc.sync.dma_start(th_rows[P - Q_TILES :, :], th[0].rearrange("(t p) o -> t (p o)", p=P))
        q_rows = qT[0].rearrange("(g p j) w -> g p j w", g=PASSES, j=PACK)
        first_pass = place("first_pass", [P, PACK, NQ], F32, 0)
        nc.sync.dma_start(first_pass[:], q_rows[0])
        q_raw = {(t, 0): first_pass[:, :, t * P : (t + 1) * P] for t in range(Q_TILES)}

        def load_closing(t, at):
            tile = place(f"q_raw{t}1", [P, PACK, P], F32, at)
            nc.sync.dma_start(tile[:], q_rows[1][:, :, t * P : (t + 1) * P])
            q_raw[t, 1] = tile[:]

        load_closing(0, 6144)

        def zero_on_vector(tile, rows, lo, hi):
            nc.vector.memset(tile[rows, lo : hi - 1], 0)
            nc.vector.memset(tile[rows, hi - 1 : hi], 0)

        warm_in = keep.tile([P, 1], F32, name="warm_in")
        warm_out = keep.tile([P, 1], F32, name="warm_out")
        nc.gpsimd.memset(warm_in[:], 0.0)
        nc.scalar.activation(warm_out[:], warm_in[:], ACT.Sigmoid)

        zero_on_vector(scale_pool, slice(0, P - QUAD), 0, T // 4)
        zero_on_vector(kb_pool, slice(0, KB_ROW), 0, KB_ON_VECTOR)
        nc.gpsimd.memset(kb_pool[:KB_ROW, KB_ON_VECTOR:], 0.0)
        ident = keep.tile([P, P], F32, name="ident")
        make_identity(nc, ident[:])
        planes = keep.tile([P, PASSES * N // 4], I32, name="planes", align_bytes=64)
        nc.gpsimd.memset(planes[:], 0)
        nc.gpsimd.memset(th_rows[: P - Q_TILES, :], 0.0)
        zeros = keep.tile([P, N - P], F32, name="zeros")
        nc.gpsimd.memset(zeros[:], 0.0)

        maps = {0: keep.tile([P, T], F32, name="map0")}
        nc.gpsimd.memset(maps[0][:], 0.0)

        listed_bytes = keep.tile([P, N], U8, name="listed_bytes")
        nc.vector.tensor_copy(listed_bytes[:], scale_pool[:].bitcast(U8).indirect(offsets[:]))
        for u in range(4):
            rows = P - QUAD + 8 * u
            nc.sync.dma_start(
                planes[QUAD * u : QUAD * u + 4, :].rearrange("r (g w) -> r g w", g=PASSES),
                listed_bytes[:].bitcast(I32)[rows : rows + 8, :],
            )
        load_closing(1, 4096)
        k_planes = [planes[:].bitcast(U8)[:, g * N : (g + 1) * N] for g in range(PASSES)]

        kb_listed = keep.tile([P, N], F32, name="kb_listed")
        for lo in range(0, N, HALF):
            nc.scalar.activation(kb_listed[:, lo : lo + HALF], kb_pool[:].indirect(part_list(lo, lo + HALF)), ACT.Copy)
        low_cols = place("low_cols", [P, 2], F32, 8192)
        high_cols = place("high_cols", [P, 2, 320], F32, 17344)
        first_rows = keep.tile([P, P], F32, name="first_rows")

        def turn_bias(h, cols, b):
            turned = bank(f"kb_turned{h}", [P, 2, P], b)
            for i in range(2):
                nc.tensor.transpose(turned[:, i, :], kb_listed[:, (2 * h + i) * P : (2 * h + i + 1) * P], ident[:])
            nc.scalar.copy(cols, turned[:, :, KB_ROW])

        turn_bias(0, low_cols[:], 4)
        spread = bank("first_spread", [P, P], 5)
        nc.tensor.transpose(spread[:], low_cols[:, 0:1].to_broadcast([P, P]), ident[:])
        nc.scalar.copy(first_rows[:], spread[:])
        turn_bias(1, high_cols[:, :, 0], 6)
        spread = bank("high_spread", [P, 2, P], 7)
        for i in range(2):
            nc.tensor.transpose(spread[:, i, :], high_cols[:, i, 0:1].to_broadcast([P, P]), ident[:])

        q_codes, q_scales, k_parted, word_pairs, rounded = {}, {}, {}, {}, {}

        def round_q(engine_copy, t, g, lo=0, hi=P):
            engine_copy(
                rounded[t, g][:, lo:hi].rearrange("p (c i) j -> p c j i", i=4),
                q_raw[t, g][:, :, lo:hi].rearrange("p j (c i) -> p c j i", i=4),
            )

        def quantize_q(t, g, codes):
            scales = keep.tile([P, P], U8, name=f"q_scales{t}{g}", align_bytes=64)
            nc.vector.quantize_mx(out=codes[:].bitcast(FP8X4), scales=scales[:], in_=rounded[t, g][:].rearrange("p w j -> p (w j)"))
            q_codes[t, g], q_scales[t, g] = codes[:].bitcast(FP8X4), scales[:]

        for h in range(2):
            word_pairs[h] = keep.tile([P, HALF], U32, name=f"word_pairs{h}")
            nc.vector.tensor_copy(word_pairs[h][:], word_pool[:].bitcast(U32).indirect(part_list(h * HALF, (h + 1) * HALF)))
        for h in range(2):
            k_parted[h] = keep.tile([P, PASSES, HALF], U16, name=f"k_codes{h}", align_bytes=64)
            nc.vector.tensor_copy(k_parted[h][:], word_pairs[h][:].bitcast(U16).rearrange("p (n g) -> p g n", g=PASSES))

        def k_codes(lo, hi, g):
            h = lo // HALF
            return k_parted[h][:, g, lo - h * HALF : hi - h * HALF].bitcast(FP4X4)

        th_turned = bank("th_turned", [P, P], 4)
        nc.tensor.transpose(th_turned[:], th_rows[:], ident[:])
        neg_th = keep.tile([P, Q_TILES], F32, name="neg_th")
        nc.scalar.activation(neg_th[:], th_turned[:, P - Q_TILES :], ACT.Copy, scale=-1.0)
        rounded[0, 0] = place("q_bf00", [P, P, PACK], BF16, 16384)
        rounded[0, 1] = place("q_bf01", [P, P, PACK], BF16, 17408)
        rounded[1, 0] = place("q_bf10", [P, P, PACK], BF16, 18432)
        round_q(nc.scalar.copy, 0, 0)
        round_q(nc.vector.tensor_copy, 0, 1, 0, CLOSING_ON_VECTOR)
        round_q(nc.scalar.copy, 0, 1, CLOSING_ON_VECTOR, P)
        for g in range(PASSES):
            quantize_q(0, g, keep.tile([P, P], U32, name=f"q_codes0{g}", align_bytes=64))
        round_q(nc.scalar.copy, 1, 0)
        high_rows = place("high_rows", [P, HALF], F32, 17408)
        nc.vector.tensor_copy(high_rows[:], spread[:].rearrange("p c s -> p (c s)"))
        quantize_q(1, 0, keep.tile([P, P], U32, name="q_codes10", align_bytes=64))
        rounded[1, 1] = place("q_bf11", [P, P, PACK], BF16, 19456)
        round_q(nc.scalar.copy, 1, 1)

        def store(t):
            for lo in range(0, T, T // 2):
                nc.sync.dma_start(out[0, t * P : (t + 1) * P, lo : lo + T // 2], maps[t][:, lo : lo + T // 2])

        def by_query(sums, t, lo, hi, g, first=0):
            nc.tensor.matmul_mx(
                out=sums,
                lhsT=q_codes[t, g],
                lhsT_scale=q_scales[t, g],
                rhs=k_codes(lo, hi, g),
                rhs_scale=k_planes[g][:, lo:hi],
                start=(g == first),
                stop=(g != first),
            )

        def by_slot(sums, t, lo, g, first=0):
            nc.tensor.matmul_mx(
                out=sums,
                lhsT=k_codes(lo, lo + P, g),
                lhsT_scale=k_planes[g][:, lo : lo + P],
                rhs=q_codes[t, g],
                rhs_scale=q_scales[t, g],
                start=(g == first),
                stop=(g != first),
            )

        first_sums = bank("first_sums", [P, P], 0)
        high_sums = bank("high_sums", [P, HALF], 1)
        second_sums = bank("second_sums", [P, P], 2)
        for g in range(PASSES):
            by_query(first_sums[:], 0, 0, P, g)
            by_query(high_sums[:], 0, HALF, N, g)
        for g in reversed(range(PASSES)):
            by_slot(second_sums[:], 0, P, g, first=PASSES - 1)
        first_biased = keep.tile([P, P], F32, name="first_biased")
        high_biased = place("high_biased", [P, HALF], F32, 4096)
        first_gates = place("first_gates", [P, P], F32, 5120)
        rest_gates = keep.tile([P, N - P], F32, name="rest_gates")
        nc.vector.tensor_tensor(first_biased[:], first_sums[:], first_rows[:], ADD)
        quantize_q(1, 1, keep.tile([P, P], U32, name="q_codes11", align_bytes=64))
        maps[1] = place("map1", [P, T], F32, 19456)
        nc.gpsimd.memset(maps[1][:], 0.0)
        nc.vector.tensor_tensor(high_biased[:], high_sums[:], high_rows[:], ADD)
        nc.scalar.activation(first_gates[:], first_biased[:], ACT.Sigmoid, bias=neg_th[:, 0:1])
        second_biased = place("second_biased", [P, P], F32, 5632)
        nc.scalar.activation(second_biased[:], second_sums[:], ACT.Identity, bias=low_cols[:, 1:2])
        nc.scalar.activation(rest_gates[:, P:], high_biased[:], ACT.Sigmoid, bias=neg_th[:, 0:1])
        other_high = bank("other_high", [P, HALF], 3)
        for g in range(PASSES):
            by_query(other_high[:], 1, HALF, N, g)
        second_turned = bank("second_turned", [P, P], 5)
        nc.tensor.transpose(second_turned[:], second_biased[:], ident[:])
        nc.scalar.activation(rest_gates[:, :P], second_turned[:], ACT.Sigmoid, bias=neg_th[:, 0:1])
        nc.vector.tensor_tensor(maps[0][:].indirect(part_list(0, P)), first_gates[:], zeros[:, :P], ADD)

        other_low = [bank("other_low0", [P, P], 4), bank("other_low1", [P, P], 2)]
        for i in range(2):
            for g in reversed(range(PASSES)):
                by_slot(other_low[i][:], 1, i * P, g, first=PASSES - 1)
        other_high_biased = keep.tile([P, HALF], F32, name="other_high_biased")
        nc.vector.tensor_tensor(other_high_biased[:], other_high[:], high_rows[:], ADD)
        nc.vector.tensor_tensor(maps[0][:].indirect(part_list(P, N)), rest_gates[:], zeros[:], ADD)
        store(0)

        other_turned = bank("other_turned", [P, 2, P], 6)
        for i in range(2):
            biased = keep.tile([P, P], F32, name=f"other_low_biased{i}")
            nc.scalar.activation(biased[:], other_low[i][:], ACT.Identity, bias=low_cols[:, i : i + 1])
            nc.tensor.transpose(other_turned[:, i, :], biased[:], ident[:])
        other_high_gates = place("other_high_gates", [P, HALF], F32, 8192)
        nc.scalar.activation(other_high_gates[:], other_high_biased[:], ACT.Sigmoid, bias=neg_th[:, 1:2])
        other_low_gates = keep.tile([P, HALF], F32, name="other_low_gates")
        nc.scalar.activation(other_low_gates[:], other_turned[:].rearrange("p c s -> p (c s)"), ACT.Sigmoid, bias=neg_th[:, 1:2])
        nc.scalar.activation(maps[1][:].indirect(part_list(HALF, N)), other_high_gates[:], ACT.Copy)
        nc.vector.tensor_copy(maps[1][:].indirect(part_list(0, HALF)), other_low_gates[:])
        store(1)
